import numpy as np
import ml_dtypes


def mxq(x, axis, fmt="e4m3"):
    dtype, down = {"e4m3": (ml_dtypes.float8_e4m3fn, 7), "e5m2": (ml_dtypes.float8_e5m2, 14)}[fmt]
    v = np.moveaxis(np.asarray(x, np.float32).astype(ml_dtypes.bfloat16).astype(np.float64), axis, -1)
    blocks = v.reshape(v.shape[:-1] + (-1, 32))
    amax = np.abs(blocks).max(-1, keepdims=True)
    byte = np.maximum(np.where(amax > 0, np.frexp(amax)[1] - 1 + 127, 0) - down, 1)
    scale = np.exp2(byte - 127.0)
    codes = (blocks / scale).astype(np.float32).astype(dtype).astype(np.float64)
    return np.moveaxis((codes * scale).reshape(v.shape), -1, axis)


WIDE = False


def mx_kscale(k):
    if not WIDE:
        return np.ones(k)
    levels = np.array([10, -10, 5, -5, 0])
    if k % 512:
        return np.exp2(np.random.permutation(np.resize(levels, k // 32))).repeat(32)
    a = np.empty((k // 512, 16))
    for p in range(k // 512):
        a[p, :8] = np.random.permutation(np.resize(levels, 8))
        for g in range(8):
            far = levels[np.abs(levels - a[p, g]) >= 10]
            a[p, g + 8] = far[np.random.randint(len(far))]
    return np.exp2(a.ravel()).repeat(32)


BF16 = ml_dtypes.bfloat16


def bf(x):
    return np.asarray(x, np.float32).astype(BF16)


def f64(x):
    return np.asarray(x).astype(np.float64)


E2M1 = np.array([0.0, 0.5, 1.0, 1.5, 2.0, 3.0, 4.0, 6.0, -0.0, -0.5, -1.0, -1.5, -2.0, -3.0, -4.0, -6.0])


def pack_weight(w, fmt):
    k, n = w.shape
    w = f64(bf(w)).reshape(k // 32, 32, n)
    amax = np.abs(w).max(1)
    if fmt == "e4m3":
        byte = np.frexp(amax)[1] - 1 + 127 - 7
    else:
        mant, ex = np.frexp(amax / 6.0)
        byte = np.where(mant > 0.5, ex, ex - 1) + 127
    byte = np.clip(np.where(amax > 0, byte, 1), 1, 254)
    scaled = (w * np.exp2(127.0 - byte)[:, None, :]).reshape(k, n).astype(np.float32)
    by_word = np.ascontiguousarray(scaled.reshape(k // 512, 128, 4, n).transpose(0, 1, 3, 2))
    if fmt == "e4m3":
        words = by_word.astype(ml_dtypes.float8_e4m3fn).view(np.uint8)
    else:
        c = by_word.astype(ml_dtypes.float4_e2m1fn).view(np.uint8) & 0xF
        words = c[..., 0::2] | (c[..., 1::2] << 4)
    return np.ascontiguousarray(words), np.ascontiguousarray(byte.astype(np.uint8).reshape(k // 512, 16, n))


def unpack_weight(words, scales, fmt):
    g, p, n, _ = words.shape
    if fmt == "e4m3":
        vals = np.ascontiguousarray(words).view(ml_dtypes.float8_e4m3fn).astype(np.float64)
    else:
        nib = np.empty((g, p, n, 4), np.uint8)
        nib[..., 0::2] = words & 0xF
        nib[..., 1::2] = words >> 4
        vals = E2M1[nib]
    vals = vals * np.repeat(np.exp2(scales.astype(np.float64) - 127.0), 8, axis=1)[..., None]
    return vals.transpose(0, 1, 3, 2).reshape(g * 512, n)
def pack4(w):
    words, scales = pack_weight(w, "e2m1")
    return words.reshape(words.shape[0], 128, -1), scales


def unpack4(words, scales):
    return unpack_weight(words.reshape(words.shape[0], 128, -1, 2), scales, "e2m1")


R, T, A, F, P = 1536, 2048, 1024, 1536, 512


def setup_inputs():
    s, f = mx_kscale(T), mx_kscale(F)
    t = mx_kscale(A)
    h = np.random.standard_normal((F, A)) * f[:, None] / t
    x = np.random.standard_normal((F, P)) / (np.sqrt(F) * A ** 0.25) / f[:, None]
    h_words, h_scales = pack4(h)
    x_words, x_scales = pack4(x)
    return {"d": bf(np.random.standard_normal((R, T)) / A ** 0.25 * s),
            "b": bf(np.random.standard_normal((A, T)) / np.sqrt(T) / s * t[:, None]),
            "gap": bf(np.random.uniform(0.5, 2.0, T)),
            "h_words": h_words, "h_scales": h_scales,
            "x_words": x_words, "x_scales": x_scales,
            "coul": bf(np.random.uniform(0.5, 2.0, A)),
            "n0": bf(np.random.standard_normal((R, P)))}


def reference(d, b, gap, h_words, h_scales, x_words, x_scales, coul, n0):
    scaled = f64(b) / f64(gap)
    chi = mxq(f64(d), 1, "e4m3") @ mxq(scaled, 1, "e4m3").T
    trial = unpack4(h_words, h_scales).T @ unpack4(x_words, x_scales)
    pot = trial * f64(coul)[:, None]
    induced = mxq(chi, 1, "e4m3") @ mxq(pot, 0, "e4m3")
    return f64(n0) - induced

@@ -1,0 +1,355 @@
+from contextlib import ExitStack
+
+import concourse.mybir as mybir
+from concourse.masks import make_identity
+
+R, T, A, F, P = 1536, 2048, 1024, 1536, 512
+FLOPS = 2 * (R * T * A + F * A * P + R * A * P)
+
+F32 = mybir.dt.float32
+BF16 = mybir.dt.bfloat16
+U32 = mybir.dt.uint32
+I32 = mybir.dt.int32
+U8 = mybir.dt.uint8
+FP8X4 = mybir.dt.float8_e4m3fn_x4
+FP4X4 = mybir.dt.float4_e2m1fn_x4
+ALU = mybir.AluOpType
+
+NJ = T // 512
+NF = F // 512
+NG = A // 512
+NB = A // 128
+NP = R // 256
+
+
+def tile_rpa_density_step_s12_kernel(tc, d, b, gap, h_words, h_scales, x_words, x_scales, coul, n0, out):
+    nc = tc.nc
+    with ExitStack() as ctx:
+        keep = ctx.enter_context(tc.tile_pool(name="keep", bufs=1))
+        braw = ctx.enter_context(tc.tile_pool(name="braw", bufs=5))
+        draw = ctx.enter_context(tc.tile_pool(name="draw", bufs=5))
+        work = ctx.enter_context(tc.tile_pool(name="work", bufs=3))
+        work2 = ctx.enter_context(tc.tile_pool(name="work2", bufs=2))
+        work4 = ctx.enter_context(tc.tile_pool(name="work4", bufs=4))
+        trp = ctx.enter_context(tc.psum_pool(name="trp", bufs=4))
+        mmp = ctx.enter_context(tc.psum_pool(name="mmp", bufs=4))
+
+        ident = keep.tile([128, 128], F32, name="ident")
+        consts = keep.tile([128, 512], BF16, name="consts", align_bytes=64)
+        ginv = keep.tile([128, NJ, 2, 2], F32, name="ginv")
+        coulp = keep.tile([128, NG, 2, 2], F32, name="coulp")
+        x_w = keep.tile([128, NF, 2 * P], U8, name="x_w", align_bytes=64)
+        x_s = keep.tile([128, NF, P], U8, name="x_s", align_bytes=64)
+        h_w = keep.tile([128, NF, 2 * A], U8, name="h_w", align_bytes=64)
+        h_s = keep.tile([128, NF, A], U8, name="h_s", align_bytes=64)
+        trial = [keep.tile([128, NG, 4, 128], F32, name=f"trial{m}") for m in range(4)]
+        bcodes = [keep.tile([128, NJ * 128], U32, name=f"bcodes{i}", align_bytes=64) for i in range(NB)]
+        bscale = [keep.tile([128, NJ * 128], U8, name=f"bscale{i}", align_bytes=64) for i in range(NB)]
+        pcodes = [keep.tile([128, P], U32, name=f"pcodes{g}", align_bytes=64) for g in range(NG)]
+        pscale = [keep.tile([128, P], U8, name=f"pscale{g}", align_bytes=64) for g in range(NG)]
+        ccodes = [[keep.tile([128, 256], U32, name=f"ccodes{q}_{g}", align_bytes=64) for g in range(NG)] for q in range(NP)]
+        cscale = [[keep.tile([128, 256], U8, name=f"cscale{q}_{g}", align_bytes=64) for g in range(NG)] for q in range(NP)]
+        n0_sb = [keep.tile([128, 4, P], BF16, name=f"n0_{c}") for c in range(3)]
+
+        b_rows = b.rearrange("(g p t) k -> g t p k", p=128, t=4)
+        b_sb, d_sb, d_perm, bT, dT, dcodes, dscale, pot, chi = {}, {}, {}, {}, {}, {}, {}, {}, {}
+        tr_b, tr_d, tr_p, ps_c, ps_o, ps_t = {}, {}, {}, {}, {}, {}
+
+        def load_b(i):
+            b_sb[i] = braw.tile([128, T], BF16, name="b_sb")
+            nc.sync.dma_start(out=b_sb[i][:], in_=b_rows[i // 4, i % 4])
+
+        def load_d(r):
+            d_sb[r] = draw.tile([128, T], BF16, name="d_sb")
+            nc.sync.dma_start(out=d_sb[r][:], in_=d[r * 128 : (r + 1) * 128, :])
+
+        def load_n0(c):
+            nc.sync.dma_start(out=n0_sb[c][:], in_=n0[c * 512 : (c + 1) * 512, :].rearrange("(c p) n -> p c n", p=128))
+
+        def prep_b(i):
+            for h in range(2):
+                tr = trp.tile([128, 4, 128], F32, name="tr")
+                tr_b[i, h] = tr
+                words = b_sb[i][:].bitcast(F32)
+                for s in range(4):
+                    j, u = 2 * h + s // 2, s % 2
+                    nc.tensor.transpose(tr[:, s, :], words[:, 256 * j + u : 256 * (j + 1) : 2], ident[:])
+
+        def evict_b(i):
+            bT[i] = work.tile([128, NJ, 128, 2, 2], BF16, name="bT", align_bytes=64)
+            for j in range(NJ):
+                src = tr_b[i, j // 2][:, 2 * (j % 2) : 2 * (j % 2) + 2, :].bitcast(BF16).rearrange("p u (a e) -> p a u e", e=2)
+                nc.vector.tensor_tensor(
+                    out=bT[i][:, j],
+                    in0=src,
+                    in1=ginv[:, j].unsqueeze(1).to_broadcast([128, 128, 2, 2]),
+                    op=ALU.mult,
+                )
+
+        def quant_b(i):
+            nc.vector.quantize_mx(out=bcodes[i][:].bitcast(FP8X4), scales=bscale[i][:], in_=bT[i][:].rearrange("p j a u e -> p (j a u e)"))
+
+        def mul_t(k):
+            half, m = k // 4, k % 4
+            ps = mmp.tile([128, 512], F32, name="mm")
+            ps_t[k] = ps
+            for j in range(NF):
+                nc.tensor.matmul_mx(
+                    out=ps[:],
+                    lhsT=x_w[:, j, 256 * m : 256 * (m + 1)].bitcast(FP4X4),
+                    lhsT_scale=x_s[:, j, 128 * m : 128 * (m + 1)],
+                    rhs=h_w[:, j, 1024 * half : 1024 * (half + 1)].bitcast(FP4X4),
+                    rhs_scale=h_s[:, j, 512 * half : 512 * (half + 1)],
+                    start=(j == 0),
+                    stop=(j == NF - 1),
+                )
+
+        def evict_t(k):
+            half, m = k // 4, k % 4
+            nc.scalar.copy(out=trial[m][:, half], in_=ps_t[k][:].rearrange("p (a t) -> p t a", t=4))
+
+        def prep_p(k):
+            g, m = k // 4, k % 4
+            tr = trp.tile([128, 4, 128], F32, name="tr")
+            tr_p[k] = tr
+            for t in range(4):
+                nc.tensor.transpose(tr[:, t, :], trial[m][:, g, t, :], ident[:])
+
+        def evict_p(k):
+            g, m = k // 4, k % 4
+            if m == 0:
+                pot[g] = work2.tile([128, P, 4], BF16, name="pot", align_bytes=64)
+            nc.vector.tensor_tensor(
+                out=pot[g][:, 128 * m : 128 * (m + 1), :],
+                in0=tr_p[k][:].rearrange("p t n -> p n t"),
+                in1=coulp[:, g].rearrange("p u e -> p (u e)").unsqueeze(1).to_broadcast([128, 128, 4]),
+                op=ALU.mult,
+            )
+
+        def quant_p(g):
+            nc.vector.quantize_mx(out=pcodes[g][:].bitcast(FP8X4), scales=pscale[g][:], in_=pot[g][:].rearrange("p n t -> p (n t)"))
+
+        def perm_d(r, eng):
+            d_perm[r] = work.tile([128, 2, T // 4], F32, name="d_perm")
+            src = d_sb[r][:].bitcast(F32).rearrange("p (w u) -> p u w", u=2)
+            if eng == "S":
+                nc.scalar.copy(out=d_perm[r][:], in_=src)
+            else:
+                nc.vector.tensor_copy(out=d_perm[r][:], in_=src)
+
+        def prep_d(q):
+            for r in (2 * q, 2 * q + 1):
+                for h in range(2):
+                    tr = trp.tile([128, 4, 128], F32, name="tr")
+                    tr_d[r, h] = tr
+                    for s in range(4):
+                        j, u = 2 * h + s // 2, s % 2
+                        nc.tensor.transpose(tr[:, s, :], d_perm[r][:, u, 128 * j : 128 * (j + 1)], ident[:])
+
+        def evict_d(q, engs):
+            dT[q] = work2.tile([128, NJ, 256, 2], F32, name="dT", align_bytes=64)
+            for r in (2 * q, 2 * q + 1):
+                for h in range(2):
+                    dst = dT[q][:, 2 * h : 2 * h + 2, 128 * (r % 2) : 128 * (r % 2) + 128, :]
+                    src = tr_d[r, h][:].rearrange("p (j u) a -> p j a u", u=2)
+                    if engs[2 * (r % 2) + h] == "S":
+                        nc.scalar.copy(out=dst, in_=src)
+                    else:
+                        nc.vector.tensor_copy(out=dst, in_=src)
+
+        def quant_d(q):
+            dcodes[q] = work4.tile([128, NJ, 256], U32, name="dcodes", align_bytes=64)
+            dscale[q] = work4.tile([128, NJ, 256], U8, name="dscale", align_bytes=64)
+            for h in range(2):
+                nc.vector.quantize_mx(
+                    out=dcodes[q][:, 2 * h : 2 * h + 2].rearrange("p j a -> p (j a)").bitcast(FP8X4),
+                    scales=dscale[q][:, 2 * h : 2 * h + 2].rearrange("p j a -> p (j a)"),
+                    in_=dT[q][:, 2 * h : 2 * h + 2].rearrange("p j a u -> p (j a u)").bitcast(BF16),
+                )
+
+        def mul_c(q, g):
+            for tp in range(2):
+                ps = mmp.tile([128, 2, 256], F32, name="mm")
+                ps_c[q, g, tp] = ps
+                for e in range(2):
+                    i = 4 * g + 2 * tp + e
+                    for j in range(NJ):
+                        nc.tensor.matmul_mx(
+                            out=ps[:, e, :],
+                            lhsT=bcodes[i][:, 128 * j : 128 * (j + 1)].bitcast(FP8X4),
+                            lhsT_scale=bscale[i][:, 128 * j : 128 * (j + 1)],
+                            rhs=dcodes[q][:, j, :].bitcast(FP8X4),
+                            rhs_scale=dscale[q][:, j, :],
+                            start=(j == 0),
+                            stop=(j == NJ - 1),
+                        )
+
+        def evict_c(q, g, engs):
+            chi[q, g] = work4.tile([128, 256, 4], BF16, name="chi", align_bytes=64)
+            for tp in range(2):
+                dst = chi[q, g][:, :, 2 * tp : 2 * tp + 2]
+                src = ps_c[q, g, tp][:].rearrange("p e a -> p a e")
+                if engs[tp] == "S":
+                    nc.scalar.copy(out=dst, in_=src)
+                else:
+                    nc.vector.tensor_copy(out=dst, in_=src)
+
+        def quant_c(q, g):
+            nc.vector.quantize_mx(out=ccodes[q][g][:].bitcast(FP8X4), scales=cscale[q][g][:], in_=chi[q, g][:].rearrange("p a t -> p (a t)"))
+
+        def mul_o(q):
+            for r in (2 * q, 2 * q + 1):
+                ps = mmp.tile([128, 512], F32, name="mm")
+                ps_o[r] = ps
+                cols = slice(128 * (r % 2), 128 * (r % 2) + 128)
+                for g in range(NG):
+                    nc.tensor.matmul_mx(
+                        out=ps[:],
+                        lhsT=ccodes[q][g][:, cols].bitcast(FP8X4),
+                        lhsT_scale=cscale[q][g][:, cols],
+                        rhs=pcodes[g][:].bitcast(FP8X4),
+                        rhs_scale=pscale[g][:],
+                        start=(g == 0),
+                        stop=(g == NG - 1),
+                    )
+
+        def evict_o(q):
+            for r in (2 * q, 2 * q + 1):
+                res = work4.tile([128, P], F32, name="res")
+                nc.vector.tensor_tensor(out=res[:], in0=n0_sb[r // 4][:, r % 4, :], in1=ps_o[r][:], op=ALU.subtract)
+                nc.sync.dma_start(out=out[r * 128 : (r + 1) * 128, :], in_=res[:])
+
+        with tc.manual_schedule():
+            nc.vector.memset(consts[:], 0.0)
+            nc.scalar.dma_start(out=consts[0:4, :], in_=gap.rearrange("(j k) -> j k", k=512))
+            nc.scalar.dma_start(out=consts[4:6, :], in_=coul.rearrange("(j k) -> j k", k=512))
+            load_b(0)
+            load_b(1)
+            make_identity(nc, ident[:])
+            nc.vector.memset(x_s[:].rearrange("p g n -> p (g n)").bitcast(I32), 0)
+            nc.vector.memset(h_s[:].rearrange("p g n -> p (g n)").bitcast(I32), 0)
+            for q in range(4):
+                nc.scalar.dma_start(out=x_s[32 * q : 32 * q + 4].bitcast(I32), in_=x_scales.bitcast(I32)[:, 4 * q : 4 * q + 4, :].rearrange("g q n -> q g n"))
+                nc.scalar.dma_start(out=h_s[32 * q : 32 * q + 4].bitcast(I32), in_=h_scales.bitcast(I32)[:, 4 * q : 4 * q + 4, :].rearrange("g q n -> q g n"))
+            nc.sync.dma_start(out=x_w[:].bitcast(I32), in_=x_words.bitcast(I32).rearrange("g p n -> p g n"))
+            nc.sync.dma_start(out=h_w[:].bitcast(I32), in_=h_words.bitcast(I32).rearrange("g p n -> p g n"))
+            for i in (2, 3):
+                load_b(i)
+            for r in (0, 1):
+                load_d(r)
+            for i in (4, 5):
+                load_b(i)
+            for r in (2, 3):
+                load_d(r)
+            for i in (6, 7):
+                load_b(i)
+            for r in range(4, 12):
+                load_d(r)
+                if r % 4 == 3 or r == 5:
+                    load_n0({5: 0, 7: 1, 11: 2}[r])
+
+            prep_b(0)
+            trc = trp.tile([128, 4, 128], F32, name="tr")
+            for u in range(2):
+                nc.tensor.transpose(trc[:, u, :], consts[:].bitcast(F32)[:, u : 256 : 2], ident[:])
+            cview = trc[:, 0:2, :].bitcast(BF16)
+            nc.vector.reciprocal(out=ginv[:].rearrange("p j u e -> p u j e"), in_=cview[:, :, 0:8].rearrange("p u (j e) -> p u j e", e=2))
+            nc.vector.tensor_copy(out=coulp[:].rearrange("p j u e -> p u j e"), in_=cview[:, :, 8:12].rearrange("p u (j e) -> p u j e", e=2))
+            prep_b(1)
+            evict_b(0)
+            evict_b(1)
+            quant_b(0)
+            for k in range(4):
+                mul_t(k)
+                evict_t(k)
+            prep_b(2)
+            evict_b(2)
+            quant_b(1)
+            for k in range(4, 8):
+                mul_t(k)
+                evict_t(k)
+            perm_d(0, "S")
+            perm_d(1, "S")
+            prep_b(3)
+            evict_b(3)
+            quant_b(2)
+            prep_d(0)
+            evict_d(0, "SSSS")
+            quant_b(3)
+            prep_b(4)
+            perm_d(2, "S")
+            quant_d(0)
+            evict_b(4)
+            mul_c(0, 0)
+            perm_d(3, "S")
+            prep_b(5)
+            evict_b(5)
+            quant_b(4)
+            evict_c(0, 0, "SS")
+            prep_d(1)
+            evict_d(1, "SSSS")
+            quant_b(5)
+            quant_c(0, 0)
+            quant_d(1)
+            mul_c(1, 0)
+            prep_b(6)
+            evict_b(6)
+            perm_d(4, "S")
+            evict_c(1, 0, "SS")
+            perm_d(5, "S")
+            prep_b(7)
+            evict_b(7)
+            quant_b(6)
+            quant_b(7)
+            quant_c(1, 0)
+            prep_d(2)
+            evict_d(2, "SSSS")
+            quant_d(2)
+            mul_c(0, 1)
+            evict_c(0, 1, "SS")
+            for k in range(4):
+                prep_p(k)
+                evict_p(k)
+            mul_c(1, 1)
+            evict_c(1, 1, "SS")
+            quant_p(0)
+            quant_c(0, 1)
+            for k in range(4, 8):
+                prep_p(k)
+                evict_p(k)
+            perm_d(6, "V")
+            perm_d(7, "V")
+            mul_c(2, 0)
+            quant_p(1)
+            quant_c(1, 1)
+            evict_c(2, 0, "SS")
+            prep_d(3)
+            evict_d(3, "SSSS")
+            mul_o(0)
+            mul_c(2, 1)
+            evict_o(0)
+            quant_c(2, 0)
+            quant_d(3)
+            evict_c(2, 1, "SS")
+            mul_o(1)
+            for q in range(3, NP):
+                if q + 1 < NP:
+                    perm_d(2 * q + 2, "V")
+                    perm_d(2 * q + 3, "V")
+                mul_c(q, 0)
+                quant_c(q - 1, 1)
+                evict_o(q - 2)
+                evict_c(q, 0, "SV")
+                if q + 1 < NP:
+                    prep_d(q + 1)
+                    evict_d(q + 1, "SSSS")
+                mul_c(q, 1)
+                quant_c(q, 0)
+                if q + 1 < NP:
+                    quant_d(q + 1)
+                mul_o(q - 1)
+                evict_c(q, 1, "SV")
+            evict_o(NP - 2)
+            quant_c(NP - 1, 1)
+            mul_o(NP - 1)
+            evict_o(NP - 1)

@@ -10,346 +10,432 @@ F32 = mybir.dt.float32
 BF16 = mybir.dt.bfloat16
 U32 = mybir.dt.uint32
 I32 = mybir.dt.int32
+U16 = mybir.dt.uint16
 U8 = mybir.dt.uint8
 FP8X4 = mybir.dt.float8_e4m3fn_x4
 FP4X4 = mybir.dt.float4_e2m1fn_x4
 ALU = mybir.AluOpType
+ACT = mybir.ActivationFunctionType
 
 NJ = T // 512
 NF = F // 512
 NG = A // 512
 NB = A // 128
-NP = R // 256
+NS = NB // 2
+NQ = R // 256
+NM = P // 128
 
 
 def tile_rpa_density_step_s12_kernel(tc, d, b, gap, h_words, h_scales, x_words, x_scales, coul, n0, out):
     nc = tc.nc
     with ExitStack() as ctx:
         keep = ctx.enter_context(tc.tile_pool(name="keep", bufs=1))
-        braw = ctx.enter_context(tc.tile_pool(name="braw", bufs=5))
-        draw = ctx.enter_context(tc.tile_pool(name="draw", bufs=5))
-        work = ctx.enter_context(tc.tile_pool(name="work", bufs=3))
-        work2 = ctx.enter_context(tc.tile_pool(name="work2", bufs=2))
+        rows = ctx.enter_context(tc.tile_pool(name="rows", bufs=6))
+        work1 = ctx.enter_context(tc.tile_pool(name="work1", bufs=1))
+        work3 = ctx.enter_context(tc.tile_pool(name="work3", bufs=3))
         work4 = ctx.enter_context(tc.tile_pool(name="work4", bufs=4))
-        trp = ctx.enter_context(tc.psum_pool(name="trp", bufs=4))
-        mmp = ctx.enter_context(tc.psum_pool(name="mmp", bufs=4))
+        chis = ctx.enter_context(tc.tile_pool(name="chis", bufs=6))
+        psum = ctx.enter_context(tc.psum_pool(name="psum", bufs=1))
 
         ident = keep.tile([128, 128], F32, name="ident")
-        consts = keep.tile([128, 512], BF16, name="consts", align_bytes=64)
-        ginv = keep.tile([128, NJ, 2, 2], F32, name="ginv")
-        coulp = keep.tile([128, NG, 2, 2], F32, name="coulp")
+        gap_sb = keep.tile([128, NJ, 4], BF16, name="gap_sb")
+        ginv = keep.tile([128, NJ, 4], F32, name="ginv")
+        coul_in = keep.tile([128, NG * 128], BF16, name="coul_in")
+        coul_rows = keep.tile([128, NG * 128], F32, name="coul_rows")
+        coul_col = keep.tile([128, NG, 4], F32, name="coul_col")
         x_w = keep.tile([128, NF, 2 * P], U8, name="x_w", align_bytes=64)
         x_s = keep.tile([128, NF, P], U8, name="x_s", align_bytes=64)
-        h_w = keep.tile([128, NF, 2 * A], U8, name="h_w", align_bytes=64)
-        h_s = keep.tile([128, NF, A], U8, name="h_s", align_bytes=64)
-        trial = [keep.tile([128, NG, 4, 128], F32, name=f"trial{m}") for m in range(4)]
+        h_in = [keep.tile([128, NF, 256], I32, name=f"h_in{g}") for g in range(NG)]
+        hs_in = keep.tile([128, NF, A // 4], I32, name="hs_in")
+        h_w = [keep.tile([128, 4, NF, 256], U8, name=f"h_w{g}", align_bytes=64) for g in range(NG)]
+        h_s = [keep.tile([128, 4, NF, 128], U8, name=f"h_s{g}", align_bytes=64) for g in range(NG)]
         bcodes = [keep.tile([128, NJ * 128], U32, name=f"bcodes{i}", align_bytes=64) for i in range(NB)]
         bscale = [keep.tile([128, NJ * 128], U8, name=f"bscale{i}", align_bytes=64) for i in range(NB)]
+        dcodes = [[keep.tile([128, 2, 256], U32, name=f"dcodes{q}_{h}", align_bytes=64) for h in range(2)] for q in range(NQ)]
+        dscale = [[keep.tile([128, 2, 256], U8, name=f"dscale{q}_{h}", align_bytes=64) for h in range(2)] for q in range(NQ)]
+        pot_s = [keep.tile([128, 4, P], BF16, name=f"pot_s{g}") for g in range(NG)]
         pcodes = [keep.tile([128, P], U32, name=f"pcodes{g}", align_bytes=64) for g in range(NG)]
         pscale = [keep.tile([128, P], U8, name=f"pscale{g}", align_bytes=64) for g in range(NG)]
-        ccodes = [[keep.tile([128, 256], U32, name=f"ccodes{q}_{g}", align_bytes=64) for g in range(NG)] for q in range(NP)]
-        cscale = [[keep.tile([128, 256], U8, name=f"cscale{q}_{g}", align_bytes=64) for g in range(NG)] for q in range(NP)]
-        n0_sb = [keep.tile([128, 4, P], BF16, name=f"n0_{c}") for c in range(3)]
+        ccodes = [[keep.tile([128, 256], U32, name=f"ccodes{q}_{g}", align_bytes=64) for g in range(NG)] for q in range(NQ)]
+        cscale = [[keep.tile([128, 256], U8, name=f"cscale{q}_{g}", align_bytes=64) for g in range(NG)] for q in range(NQ)]
 
-        b_rows = b.rearrange("(g p t) k -> g t p k", p=128, t=4)
-        b_sb, d_sb, d_perm, bT, dT, dcodes, dscale, pot, chi = {}, {}, {}, {}, {}, {}, {}, {}, {}
-        tr_b, tr_d, tr_p, ps_c, ps_o, ps_t = {}, {}, {}, {}, {}, {}
+        b_rows = b.rearrange("(g m t e) k -> g t e m k", m=64, t=4, e=2)
+        b_sb, d_sb, n0_sb, d_perm, b_t, d_t, pot, chi = {}, {}, {}, {}, {}, {}, {}, {}
+        tr_b, tr_d, tr_p, ps_c, ps_o, ps_t, res, spread, b_perm = {}, {}, {}, {}, {}, {}, {}, {}, {}
+        turn = {"b": 0, "rest": 0}
+        ring = {"b": [0, 1, 2, 3], "rest": [4, 5, 6, 7]}
+
+        def bank(n, shape):
+            return psum.tile(shape, F32, name=f"bank{n}")
+
+        def copy(eng, dst, src):
+            if eng == "S":
+                nc.scalar.copy(out=dst, in_=src)
+            else:
+                nc.vector.tensor_copy(out=dst, in_=src)
 
         def load_b(i):
-            b_sb[i] = braw.tile([128, T], BF16, name="b_sb")
-            nc.sync.dma_start(out=b_sb[i][:], in_=b_rows[i // 4, i % 4])
+            b_sb[i] = rows.tile([128, T], BF16, name="b_sb")
+            for e in range(2):
+                nc.sync.dma_start(out=b_sb[i][e:128:2, :], in_=b_rows[i // 4, i % 4, e])
 
         def load_d(r):
-            d_sb[r] = draw.tile([128, T], BF16, name="d_sb")
+            d_sb[r] = rows.tile([128, T], BF16, name="d_sb")
             nc.sync.dma_start(out=d_sb[r][:], in_=d[r * 128 : (r + 1) * 128, :])
 
         def load_n0(c):
+            n0_sb[c] = rows.tile([128, 4, P], BF16, name="b_sb")
             nc.sync.dma_start(out=n0_sb[c][:], in_=n0[c * 512 : (c + 1) * 512, :].rearrange("(c p) n -> p c n", p=128))
 
-        def prep_b(i):
-            for h in range(2):
-                tr = trp.tile([128, 4, 128], F32, name="tr")
-                tr_b[i, h] = tr
-                words = b_sb[i][:].bitcast(F32)
-                for s in range(4):
-                    j, u = 2 * h + s // 2, s % 2
-                    nc.tensor.transpose(tr[:, s, :], words[:, 256 * j + u : 256 * (j + 1) : 2], ident[:])
+        def load_h(g):
+            nc.sync.dma_start(out=h_in[g][:], in_=h_words.bitcast(I32)[:, :, 256 * g : 256 * (g + 1)].rearrange("j p n -> p j n"))
 
-        def evict_b(i):
-            bT[i] = work.tile([128, NJ, 128, 2, 2], BF16, name="bT", align_bytes=64)
-            for j in range(NJ):
-                src = tr_b[i, j // 2][:, 2 * (j % 2) : 2 * (j % 2) + 2, :].bitcast(BF16).rearrange("p u (a e) -> p a u e", e=2)
-                nc.vector.tensor_tensor(
-                    out=bT[i][:, j],
-                    in0=src,
-                    in1=ginv[:, j].unsqueeze(1).to_broadcast([128, 128, 2, 2]),
-                    op=ALU.mult,
-                )
+        def perm_b(i, h, eng):
+            b_perm[i, h] = work4.tile([128, 2, T // 8], F32, name="b_perm")
+            copy(eng, b_perm[i, h][:], b_sb[i][:].bitcast(F32)[:, 512 * h : 512 * (h + 1)].rearrange("p (w u) -> p u w", u=2))
+
+        def turn_b(banks, i):
+            for h in range(2):
+                tr_b[i, h] = bank(banks[h], [128, 2, 2, 128])
+                for jj in range(2):
+                    for u in range(2):
+                        nc.tensor.transpose(tr_b[i, h][:, u, jj, :], b_perm[i, h][:, u, 128 * jj : 128 * (jj + 1)], ident[:])
+
+        def scale_b(i, h):
+            if h == 0:
+                b_t[i] = work3.tile([128, NJ, 128, 2, 2], BF16, name="b_t", align_bytes=64)
+            nc.vector.tensor_tensor(
+                out=b_t[i][:, 2 * h : 2 * h + 2],
+                in0=tr_b[i, h][:].bitcast(BF16).rearrange("p u j (a e) -> p j a u e", e=2),
+                in1=ginv[:, 2 * h : 2 * h + 2].rearrange("p j (u e) -> p j u e", e=2).unsqueeze(2).to_broadcast([128, 2, 128, 2, 2]),
+                op=ALU.mult,
+            )
 
         def quant_b(i):
-            nc.vector.quantize_mx(out=bcodes[i][:].bitcast(FP8X4), scales=bscale[i][:], in_=bT[i][:].rearrange("p j a u e -> p (j a u e)"))
+            nc.vector.quantize_mx(out=bcodes[i][:].bitcast(FP8X4), scales=bscale[i][:], in_=b_t[i][:].rearrange("p j a u e -> p (j a u e)"))
 
-        def mul_t(k):
-            half, m = k // 4, k % 4
-            ps = mmp.tile([128, 512], F32, name="mm")
-            ps_t[k] = ps
+        def sort_h(g):
+            nc.vector.tensor_copy(
+                out=h_w[g][:].bitcast(I32).rearrange("p t j (c i) -> p j c t i", i=4),
+                in_=h_in[g][:].rearrange("p j (c i t) -> p j c t i", t=4, i=4),
+            )
+
+        def sort_hs(g):
+            nc.vector.tensor_copy(
+                out=h_s[g][:].bitcast(U16).rearrange("p t j m -> p t j m"),
+                in_=hs_in[:, :, 128 * g : 128 * (g + 1)].bitcast(U16).rearrange("p j (m t) -> p t j m", t=4),
+            )
+
+        def mul_t(banks, g, t):
+            ps_t[g, t] = bank(banks[0], [128, 512])
             for j in range(NF):
                 nc.tensor.matmul_mx(
-                    out=ps[:],
-                    lhsT=x_w[:, j, 256 * m : 256 * (m + 1)].bitcast(FP4X4),
-                    lhsT_scale=x_s[:, j, 128 * m : 128 * (m + 1)],
-                    rhs=h_w[:, j, 1024 * half : 1024 * (half + 1)].bitcast(FP4X4),
-                    rhs_scale=h_s[:, j, 512 * half : 512 * (half + 1)],
+                    out=ps_t[g, t][:],
+                    lhsT=h_w[g][:, t, j, :].bitcast(FP4X4),
+                    lhsT_scale=h_s[g][:, t, j, :],
+                    rhs=x_w[:, j, :].bitcast(FP4X4),
+                    rhs_scale=x_s[:, j, :],
                     start=(j == 0),
                     stop=(j == NF - 1),
                 )
 
-        def evict_t(k):
-            half, m = k // 4, k % 4
-            nc.scalar.copy(out=trial[m][:, half], in_=ps_t[k][:].rearrange("p (a t) -> p t a", t=4))
+        def scale_t(g, t):
+            nc.scalar.activation(out=pot_s[g][:, t, :], in_=ps_t[g, t][:], func=ACT.Copy, scale=coul_col[:, g, t : t + 1])
 
-        def prep_p(k):
-            g, m = k // 4, k % 4
-            tr = trp.tile([128, 4, 128], F32, name="tr")
-            tr_p[k] = tr
-            for t in range(4):
-                nc.tensor.transpose(tr[:, t, :], trial[m][:, g, t, :], ident[:])
-
-        def evict_p(k):
-            g, m = k // 4, k % 4
-            if m == 0:
-                pot[g] = work2.tile([128, P, 4], BF16, name="pot", align_bytes=64)
-            nc.vector.tensor_tensor(
-                out=pot[g][:, 128 * m : 128 * (m + 1), :],
-                in0=tr_p[k][:].rearrange("p t n -> p n t"),
-                in1=coulp[:, g].rearrange("p u e -> p (u e)").unsqueeze(1).to_broadcast([128, 128, 4]),
-                op=ALU.mult,
-            )
+        def weave_p(g):
+            pot[g] = work1.tile([128, P, 4], BF16, name="pot", align_bytes=64)
+            nc.vector.tensor_copy(out=pot[g][:].rearrange("p (c i) t -> p c t i", i=4), in_=pot_s[g][:].rearrange("p t (c i) -> p c t i", i=4))
 
         def quant_p(g):
             nc.vector.quantize_mx(out=pcodes[g][:].bitcast(FP8X4), scales=pscale[g][:], in_=pot[g][:].rearrange("p n t -> p (n t)"))
 
-        def perm_d(r, eng):
-            d_perm[r] = work.tile([128, 2, T // 4], F32, name="d_perm")
-            src = d_sb[r][:].bitcast(F32).rearrange("p (w u) -> p u w", u=2)
-            if eng == "S":
-                nc.scalar.copy(out=d_perm[r][:], in_=src)
-            else:
-                nc.vector.tensor_copy(out=d_perm[r][:], in_=src)
+        def perm_d(r, h, eng):
+            d_perm[r, h] = chis.tile([128, 2, T // 8], F32, name="d_perm", bufs=8)
+            copy(eng, d_perm[r, h][:], d_sb[r][:].bitcast(F32)[:, 512 * h : 512 * (h + 1)].rearrange("p (w u) -> p u w", u=2))
 
-        def prep_d(q):
-            for r in (2 * q, 2 * q + 1):
-                for h in range(2):
-                    tr = trp.tile([128, 4, 128], F32, name="tr")
-                    tr_d[r, h] = tr
-                    for s in range(4):
-                        j, u = 2 * h + s // 2, s % 2
-                        nc.tensor.transpose(tr[:, s, :], d_perm[r][:, u, 128 * j : 128 * (j + 1)], ident[:])
-
-        def evict_d(q, engs):
-            dT[q] = work2.tile([128, NJ, 256, 2], F32, name="dT", align_bytes=64)
-            for r in (2 * q, 2 * q + 1):
-                for h in range(2):
-                    dst = dT[q][:, 2 * h : 2 * h + 2, 128 * (r % 2) : 128 * (r % 2) + 128, :]
-                    src = tr_d[r, h][:].rearrange("p (j u) a -> p j a u", u=2)
-                    if engs[2 * (r % 2) + h] == "S":
-                        nc.scalar.copy(out=dst, in_=src)
-                    else:
-                        nc.vector.tensor_copy(out=dst, in_=src)
-
-        def quant_d(q):
-            dcodes[q] = work4.tile([128, NJ, 256], U32, name="dcodes", align_bytes=64)
-            dscale[q] = work4.tile([128, NJ, 256], U8, name="dscale", align_bytes=64)
+        def turn_d(banks, r):
             for h in range(2):
-                nc.vector.quantize_mx(
-                    out=dcodes[q][:, 2 * h : 2 * h + 2].rearrange("p j a -> p (j a)").bitcast(FP8X4),
-                    scales=dscale[q][:, 2 * h : 2 * h + 2].rearrange("p j a -> p (j a)"),
-                    in_=dT[q][:, 2 * h : 2 * h + 2].rearrange("p j a u -> p (j a u)").bitcast(BF16),
-                )
+                tr_d[r, h] = bank(banks[h], [128, 2, 2, 128])
+                for jj in range(2):
+                    for u in range(2):
+                        nc.tensor.transpose(tr_d[r, h][:, jj, u, :], d_perm[r, h][:, u, 128 * jj : 128 * (jj + 1)], ident[:])
 
-        def mul_c(q, g):
-            for tp in range(2):
-                ps = mmp.tile([128, 2, 256], F32, name="mm")
-                ps_c[q, g, tp] = ps
-                for e in range(2):
-                    i = 4 * g + 2 * tp + e
-                    for j in range(NJ):
-                        nc.tensor.matmul_mx(
-                            out=ps[:, e, :],
-                            lhsT=bcodes[i][:, 128 * j : 128 * (j + 1)].bitcast(FP8X4),
-                            lhsT_scale=bscale[i][:, 128 * j : 128 * (j + 1)],
-                            rhs=dcodes[q][:, j, :].bitcast(FP8X4),
-                            rhs_scale=dscale[q][:, j, :],
-                            start=(j == 0),
-                            stop=(j == NJ - 1),
-                        )
+        def evict_d(r, h, eng):
+            q = r // 2
+            if r % 2 == 0:
+                d_t[q, h] = work4.tile([128, 2, 256, 2], F32, name="d_t", align_bytes=64)
+            copy(eng, d_t[q, h][:, :, 128 * (r % 2) : 128 * (r % 2) + 128, :], tr_d[r, h][:].rearrange("p j u a -> p j a u"))
 
-        def evict_c(q, g, engs):
-            chi[q, g] = work4.tile([128, 256, 4], BF16, name="chi", align_bytes=64)
-            for tp in range(2):
-                dst = chi[q, g][:, :, 2 * tp : 2 * tp + 2]
-                src = ps_c[q, g, tp][:].rearrange("p e a -> p a e")
-                if engs[tp] == "S":
-                    nc.scalar.copy(out=dst, in_=src)
-                else:
-                    nc.vector.tensor_copy(out=dst, in_=src)
+        def quant_d(q, h):
+            nc.vector.quantize_mx(
+                out=dcodes[q][h][:].rearrange("p j a -> p (j a)").bitcast(FP8X4),
+                scales=dscale[q][h][:].rearrange("p j a -> p (j a)"),
+                in_=d_t[q, h][:].rearrange("p j a u -> p (j a u)").bitcast(BF16),
+            )
+
+        def mul_c(banks, q, s):
+            ps_c[q, s] = bank(banks[0], [128, 2, 256])
+            for e in range(2):
+                i = 2 * s + e
+                for j in range(NJ):
+                    nc.tensor.matmul_mx(
+                        out=ps_c[q, s][:, e, :],
+                        lhsT=bcodes[i][:, 128 * j : 128 * (j + 1)].bitcast(FP8X4),
+                        lhsT_scale=bscale[i][:, 128 * j : 128 * (j + 1)],
+                        rhs=dcodes[q][j // 2][:, j % 2, :].bitcast(FP8X4),
+                        rhs_scale=dscale[q][j // 2][:, j % 2, :],
+                        start=(j == 0),
+                        stop=(j == NJ - 1),
+                    )
+
+        def evict_c(q, s, eng):
+            g, tp = s // 2, s % 2
+            if tp == 0:
+                chi[q, g] = chis.tile([128, 256, 4], BF16, name="chi", align_bytes=64)
+            copy(eng, chi[q, g][:, :, 2 * tp : 2 * tp + 2], ps_c[q, s][:].rearrange("p e a -> p a e"))
 
         def quant_c(q, g):
             nc.vector.quantize_mx(out=ccodes[q][g][:].bitcast(FP8X4), scales=cscale[q][g][:], in_=chi[q, g][:].rearrange("p a t -> p (a t)"))
 
-        def mul_o(q):
-            for r in (2 * q, 2 * q + 1):
-                ps = mmp.tile([128, 512], F32, name="mm")
-                ps_o[r] = ps
-                cols = slice(128 * (r % 2), 128 * (r % 2) + 128)
-                for g in range(NG):
-                    nc.tensor.matmul_mx(
-                        out=ps[:],
-                        lhsT=ccodes[q][g][:, cols].bitcast(FP8X4),
-                        lhsT_scale=cscale[q][g][:, cols],
-                        rhs=pcodes[g][:].bitcast(FP8X4),
-                        rhs_scale=pscale[g][:],
-                        start=(g == 0),
-                        stop=(g == NG - 1),
-                    )
+        def mul_o(banks, r):
+            q = r // 2
+            ps_o[r] = bank(banks[0], [128, 512])
+            cols = slice(128 * (r % 2), 128 * (r % 2) + 128)
+            for g in range(NG):
+                nc.tensor.matmul_mx(
+                    out=ps_o[r][:],
+                    lhsT=ccodes[q][g][:, cols].bitcast(FP8X4),
+                    lhsT_scale=cscale[q][g][:, cols],
+                    rhs=pcodes[g][:].bitcast(FP8X4),
+                    rhs_scale=pscale[g][:],
+                    start=(g == 0),
+                    stop=(g == NG - 1),
+                )
 
-        def evict_o(q):
-            for r in (2 * q, 2 * q + 1):
-                res = work4.tile([128, P], F32, name="res")
-                nc.vector.tensor_tensor(out=res[:], in0=n0_sb[r // 4][:, r % 4, :], in1=ps_o[r][:], op=ALU.subtract)
-                nc.sync.dma_start(out=out[r * 128 : (r + 1) * 128, :], in_=res[:])
+        def evict_o(r):
+            res[r] = chis.tile([128, P], F32, name="res")
+            nc.vector.tensor_tensor(out=res[r][:], in0=n0_sb[r // 4][:, r % 4, :], in1=ps_o[r][:], op=ALU.subtract)
+
+        def store(r):
+            nc.sync.dma_start(out=out[r * 128 : (r + 1) * 128, :], in_=res[r][:])
+
+        def widen_coul():
+            nc.scalar.copy(out=coul_rows[0:4, :], in_=coul_in[0:4, :])
+
+        def turn_coul(banks):
+            spread[0] = bank(banks[0], [128, NG, 128])
+            for g in range(NG):
+                nc.tensor.transpose(spread[0][:, g, :], coul_rows[:, 128 * g : 128 * (g + 1)], ident[:])
+
+        def evict_coul():
+            nc.scalar.copy(out=coul_col[:], in_=spread[0][:, :, 0:4])
+
+        def invert_gap():
+            nc.vector.reciprocal(out=ginv[:], in_=gap_sb[:])
 
         with tc.manual_schedule():
-            nc.vector.memset(consts[:], 0.0)
-            nc.scalar.dma_start(out=consts[0:4, :], in_=gap.rearrange("(j k) -> j k", k=512))
-            nc.scalar.dma_start(out=consts[4:6, :], in_=coul.rearrange("(j k) -> j k", k=512))
+            queue = {"SP": [], "PE": [], "S": [], "V": []}
+            holder = {}
+
+            def step(eng, key, needs, fn, *args):
+                queue[eng].append((key, list(needs), fn, args))
+
+            def pe(kind, key, needs, frees, fn, *args):
+                banks = []
+                for reader in frees:
+                    n = ring[kind][turn[kind] % len(ring[kind])]
+                    turn[kind] = turn[kind] + 1
+                    if n in holder:
+                        needs = needs + [holder[n]]
+                    holder[n] = reader
+                    banks.append(n)
+                step("PE", key, needs, fn, banks, *args)
+
+            def emit():
+                done = set()
+                at = {eng: 0 for eng in queue}
+                while any(at[eng] < len(queue[eng]) for eng in queue):
+                    before = len(done)
+                    for eng in queue:
+                        while at[eng] < len(queue[eng]) and all(n in done for n in queue[eng][at[eng]][1]):
+                            key, needs, fn, args = queue[eng][at[eng]]
+                            fn(*args)
+                            done.add(key)
+                            at[eng] = at[eng] + 1
+                    assert len(done) > before, [(e, queue[e][at[e]][0], [n for n in queue[e][at[e]][1] if n not in done]) for e in queue if at[e] < len(queue[e])]
+
+            def p_tb(i): pe("b", ("tb", i), [("pb", i, 0), ("pb", i, 1)], [("mb", i, 0), ("mb", i, 1)], turn_b, i)
+            def p_td(r): pe("rest", ("td", r), [("pd", r, 0), ("pd", r, 1)], [("ed", r, 0), ("ed", r, 1)], turn_d, r)
+            def p_t(g, m): pe("rest", ("t", g, m), [("sh", g), ("shs", g), "lx"], [("st", g, m)], mul_t, g, m)
+            def p_c(q, s): pe("rest", ("c", q, s), [("qb", 2 * s), ("qb", 2 * s + 1), ("qd", q, 0), ("qd", q, 1)], [("ec", q, s)], mul_c, q, s)
+            def p_o(r): pe("rest", ("o", r), [("qc", r // 2, 0), ("qc", r // 2, 1), ("qp", 0), ("qp", 1)], [("eo", r)], mul_o, r)
+            def s_pd(r, eng):
+                for h in range(2):
+                    step(eng, ("pd", r, h), [("ld", r)] + ([("td", r - 4)] if r >= 4 else []), perm_d, r, h, eng)
+            def s_ed(r, h, eng): step(eng, ("ed", r, h), [("td", r)] + ([("qd", r // 2 - 2, h)] if r >= 4 else []), evict_d, r, h, eng)
+            def s_ec(q, s, eng): step(eng, ("ec", q, s), [("c", q, s)], evict_c, q, s, eng)
+            def v_wp(g): step("V", ("wp", g), [("st", g, t) for t in range(4)] + ([("qp", 0)] if g else []), weave_p, g)
+            def v_mb(i, h): step("V", ("mb", i, h), [("tb", i), "ginv"] + ([("qb", i - 3)] if i >= 3 else []), scale_b, i, h)
+            def v_qb(i): step("V", ("qb", i), [("mb", i, 0), ("mb", i, 1)], quant_b, i)
+            def s_st(g, m): step("S", ("st", g, m), [("t", g, m), "coul_col"], scale_t, g, m)
+            def v_qd(q, h): step("V", ("qd", q, h), [("ed", 2 * q, h), ("ed", 2 * q + 1, h)], quant_d, q, h)
+            def v_qc(q, g): step("V", ("qc", q, g), [("ec", q, 2 * g), ("ec", q, 2 * g + 1)], quant_c, q, g)
+            def v_qp(g): step("V", ("qp", g), [("wp", g)], quant_p, g)
+            def v_eo(r): step("V", ("eo", r), [("o", r), ("ln", r // 4)] + ([("so", r - 6)] if r >= 6 else []), evict_o, r)
+            def d_lb(i): step("SP", ("lb", i), [("pb", i - 6, 1)] if i >= 6 else [], load_b, i)
+            def d_ld(r): step("SP", ("ld", r), [("pd", r - 6, 1)] if r >= 6 else [], load_d, r)
+            def s_pb(i, eng):
+                for h in range(2):
+                    step(eng, ("pb", i, h), [("lb", i)] + ([("tb", i - 2)] if i >= 2 else []), perm_b, i, h, eng)
+            def p_unit(q, s):
+                p_c(q, s)
+            def s_e(r):
+                s_ed(r, 0, "S")
+                s_ed(r, 1, "S")
+            def v_m(i):
+                for j in range(2):
+                    v_mb(i, j)
+            def v_sh(g):
+                step("V", ("shs", g), [], sort_hs, g)
+                step("V", ("sh", g), [("lh", g)], sort_h, g)
+            def load_x():
+                nc.sync.dma_start(out=x_w[:].bitcast(I32), in_=x_words.bitcast(I32).rearrange("j p n -> p j n"))
+
+            nc.scalar.dma_start(out=gap_sb[:], in_=gap.rearrange("(j p t) -> p j t", p=128, t=4))
             load_b(0)
             load_b(1)
+            nc.vector.memset(hs_in[:], 0)
+            nc.vector.memset(x_s[:].rearrange("p j n -> p (j n)").bitcast(I32), 0)
+            nc.vector.memset(coul_rows[:], 0.0)
+            nc.gpsimd.dma_start(out=coul_in[0:4, :].rearrange("t (m e) -> t m e", e=2), in_=coul.rearrange("(m t e) -> t m e", t=4, e=2))
             make_identity(nc, ident[:])
-            nc.vector.memset(x_s[:].rearrange("p g n -> p (g n)").bitcast(I32), 0)
-            nc.vector.memset(h_s[:].rearrange("p g n -> p (g n)").bitcast(I32), 0)
-            for q in range(4):
-                nc.scalar.dma_start(out=x_s[32 * q : 32 * q + 4].bitcast(I32), in_=x_scales.bitcast(I32)[:, 4 * q : 4 * q + 4, :].rearrange("g q n -> q g n"))
-                nc.scalar.dma_start(out=h_s[32 * q : 32 * q + 4].bitcast(I32), in_=h_scales.bitcast(I32)[:, 4 * q : 4 * q + 4, :].rearrange("g q n -> q g n"))
-            nc.sync.dma_start(out=x_w[:].bitcast(I32), in_=x_words.bitcast(I32).rearrange("g p n -> p g n"))
-            nc.sync.dma_start(out=h_w[:].bitcast(I32), in_=h_words.bitcast(I32).rearrange("g p n -> p g n"))
-            for i in (2, 3):
-                load_b(i)
-            for r in (0, 1):
-                load_d(r)
-            for i in (4, 5):
-                load_b(i)
-            for r in (2, 3):
-                load_d(r)
-            for i in (6, 7):
-                load_b(i)
-            for r in range(4, 12):
-                load_d(r)
-                if r % 4 == 3 or r == 5:
-                    load_n0({5: 0, 7: 1, 11: 2}[r])
+            for c in range(4):
+                nc.sync.dma_start(out=hs_in[32 * c : 32 * c + 4], in_=h_scales.bitcast(I32)[:, 4 * c : 4 * c + 4, :].rearrange("j r n -> r j n"))
+            load_h(0)
+            load_x()
+            for c in range(4):
+                nc.sync.dma_start(out=x_s[32 * c : 32 * c + 4].bitcast(I32), in_=x_scales.bitcast(I32)[:, 4 * c : 4 * c + 4, :].rearrange("j r n -> r j n"))
+            for key in (("lb", 0), ("lb", 1), ("lh", 0), "lx"):
+                step("SP", key, [], len, [])
+            d_lb(2)
+            d_ld(0)
+            step("SP", ("lh", 1), [], load_h, 1)
+            for i in range(3, 8):
+                d_lb(i)
+                d_ld(i - 2)
+            for r in range(6, 2 * NQ):
+                d_ld(r)
+            for c in range(3):
+                step("SP", ("ln", c), [("pb", 2 + c, 1)], load_n0, c)
+            for r in range(12):
+                step("SP", ("so", r), [("eo", r)], store, r)
 
-            prep_b(0)
-            trc = trp.tile([128, 4, 128], F32, name="tr")
-            for u in range(2):
-                nc.tensor.transpose(trc[:, u, :], consts[:].bitcast(F32)[:, u : 256 : 2], ident[:])
-            cview = trc[:, 0:2, :].bitcast(BF16)
-            nc.vector.reciprocal(out=ginv[:].rearrange("p j u e -> p u j e"), in_=cview[:, :, 0:8].rearrange("p u (j e) -> p u j e", e=2))
-            nc.vector.tensor_copy(out=coulp[:].rearrange("p j u e -> p u j e"), in_=cview[:, :, 8:12].rearrange("p u (j e) -> p u j e", e=2))
-            prep_b(1)
-            evict_b(0)
-            evict_b(1)
-            quant_b(0)
-            for k in range(4):
-                mul_t(k)
-                evict_t(k)
-            prep_b(2)
-            evict_b(2)
-            quant_b(1)
-            for k in range(4, 8):
-                mul_t(k)
-                evict_t(k)
-            perm_d(0, "S")
-            perm_d(1, "S")
-            prep_b(3)
-            evict_b(3)
-            quant_b(2)
-            prep_d(0)
-            evict_d(0, "SSSS")
-            quant_b(3)
-            prep_b(4)
-            perm_d(2, "S")
-            quant_d(0)
-            evict_b(4)
-            mul_c(0, 0)
-            perm_d(3, "S")
-            prep_b(5)
-            evict_b(5)
-            quant_b(4)
-            evict_c(0, 0, "SS")
-            prep_d(1)
-            evict_d(1, "SSSS")
-            quant_b(5)
-            quant_c(0, 0)
-            quant_d(1)
-            mul_c(1, 0)
-            prep_b(6)
-            evict_b(6)
-            perm_d(4, "S")
-            evict_c(1, 0, "SS")
-            perm_d(5, "S")
-            prep_b(7)
-            evict_b(7)
-            quant_b(6)
-            quant_b(7)
-            quant_c(1, 0)
-            prep_d(2)
-            evict_d(2, "SSSS")
-            quant_d(2)
-            mul_c(0, 1)
-            evict_c(0, 1, "SS")
-            for k in range(4):
-                prep_p(k)
-                evict_p(k)
-            mul_c(1, 1)
-            evict_c(1, 1, "SS")
-            quant_p(0)
-            quant_c(0, 1)
-            for k in range(4, 8):
-                prep_p(k)
-                evict_p(k)
-            perm_d(6, "V")
-            perm_d(7, "V")
-            mul_c(2, 0)
-            quant_p(1)
-            quant_c(1, 1)
-            evict_c(2, 0, "SS")
-            prep_d(3)
-            evict_d(3, "SSSS")
-            mul_o(0)
-            mul_c(2, 1)
-            evict_o(0)
-            quant_c(2, 0)
-            quant_d(3)
-            evict_c(2, 1, "SS")
-            mul_o(1)
-            for q in range(3, NP):
-                if q + 1 < NP:
-                    perm_d(2 * q + 2, "V")
-                    perm_d(2 * q + 3, "V")
-                mul_c(q, 0)
-                quant_c(q - 1, 1)
-                evict_o(q - 2)
-                evict_c(q, 0, "SV")
-                if q + 1 < NP:
-                    prep_d(q + 1)
-                    evict_d(q + 1, "SSSS")
-                mul_c(q, 1)
-                quant_c(q, 0)
-                if q + 1 < NP:
-                    quant_d(q + 1)
-                mul_o(q - 1)
-                evict_c(q, 1, "SV")
-            evict_o(NP - 2)
-            quant_c(NP - 1, 1)
-            mul_o(NP - 1)
-            evict_o(NP - 1)
+            mx = [("t", g, t) for g in range(NG) for t in range(4)]
+            for s in range(NS):
+                mx = mx + [("c", q, s) for q in range(s)] + [("c", s, t) for t in range(s + 1)]
+            mx = mx + [("c", q, t) for q in range(NS, NQ) for t in range(NS)]
+            runs = [3, 3, 2, 1, 1, 2, 2, 3, 4, 3]
+
+            def product(kind, u, v):
+                if kind == "t":
+                    p_t(u, v)
+                    s_st(u, v)
+                else:
+                    p_c(u, v)
+                    s_ec(u, v, "S")
+
+            p_tb(0)
+            p_tb(1)
+            pe("rest", "spread", ["coul_rows"], ["coul_col"], turn_coul)
+            s_pb(1, "S")
+            step("S", "coul_rows", [], widen_coul)
+            step("S", "coul_col", ["spread"], evict_coul)
+            s_pb(2, "S")
+            s_pd(0, "S")
+            at = 0
+            for n, count in enumerate(runs):
+                tiles = [] if n == 0 else [n - 1] if n < 7 else [2 * n - 8, 2 * n - 7]
+                if 1 <= n < 7:
+                    p_tb(n + 1)
+                if n == 7:
+                    ring["rest"] = [0, 1] + [4 + (turn["rest"] + k) % 4 for k in range(4)] + [2, 3]
+                    turn["rest"] = 0
+                for r in tiles:
+                    p_td(r)
+                for r in tiles:
+                    s_e(r)
+                if n == 1:
+                    s_pd(1, "S")
+                for kind, u, v in mx[at : at + count]:
+                    product(kind, u, v)
+                if 1 <= n < 6:
+                    s_pd(n + 1, "S")
+                at = at + count
+            for n, (kind, u, v) in enumerate(mx[at:]):
+                product(kind, u, v)
+                p_o(n)
+            for r in range(8, 12):
+                p_o(r)
+
+            s_pb(0, "V")
+            step("V", "ginv", [], invert_gap)
+            v_m(0)
+            v_sh(0)
+            v_mb(1, 0)
+            v_qb(0)
+            v_mb(1, 1)
+            v_sh(1)
+            v_qb(1)
+            s_pb(3, "V")
+            for i in range(2, 8):
+                v_mb(i, 0)
+                if i % 2 == 1 and i > 3:
+                    v_qd(i // 2 - 1, 0)
+                    v_qd(i // 2 - 1, 1)
+                v_mb(i, 1)
+                if i == 3:
+                    v_qd(0, 0)
+                    v_qd(0, 1)
+                    v_qb(3)
+                if i + 2 < 8:
+                    s_pb(i + 2, "V")
+                else:
+                    s_pd(i + 1, "V")
+                if i != 3:
+                    v_qb(i)
+            s_pd(9, "V")
+            v_qd(3, 0)
+            v_qd(3, 1)
+            v_qc(0, 0)
+            v_qc(1, 0)
+            s_pd(10, "V")
+            s_pd(11, "V")
+            v_qc(2, 0)
+            v_wp(0)
+            v_qc(0, 1)
+            v_qp(0)
+            v_qd(4, 0)
+            v_qd(4, 1)
+            v_wp(1)
+            v_qc(1, 1)
+            v_qp(1)
+            v_qc(2, 1)
+            v_qc(3, 0)
+            v_qd(5, 0)
+            v_qd(5, 1)
+            v_qc(3, 1)
+            v_eo(0)
+            v_eo(1)
+            v_qc(4, 0)
+            v_eo(2)
+            v_eo(3)
+            v_qc(4, 1)
+            v_eo(4)
+            v_eo(5)
+            v_qc(5, 0)
+            v_eo(6)
+            v_eo(7)
+            v_qc(5, 1)
+            for r in range(8, 12):
+                v_eo(r)
+            emit()

@@ -38,7 +38,8 @@ def tile_rpa_density_step_s12_kernel(tc, d, b, gap, h_words, h_scales, x_words, 
         psum = ctx.enter_context(tc.psum_pool(name="psum", bufs=1))
 
         ident = keep.tile([128, 128], F32, name="ident")
-        gap_sb = keep.tile([128, NJ, 4], BF16, name="gap_sb")
+        gap_in = keep.tile([128, 512], BF16, name="gap_in")
+        gap_rows = keep.tile([128, 2, 128], F32, name="gap_rows")
         ginv = keep.tile([128, NJ, 4], F32, name="ginv")
         coul_in = keep.tile([128, NG * 128], BF16, name="coul_in")
         coul_rows = keep.tile([128, NG * 128], F32, name="coul_rows")
@@ -92,7 +93,7 @@ def tile_rpa_density_step_s12_kernel(tc, d, b, gap, h_words, h_scales, x_words, 
 
         def perm_b(i, h, eng):
             b_perm[i, h] = work4.tile([128, 2, T // 8], F32, name="b_perm")
-            copy(eng, b_perm[i, h][:], b_sb[i][:].bitcast(F32)[:, 512 * h : 512 * (h + 1)].rearrange("p (w u) -> p u w", u=2))
+            copy(eng, b_perm[i, h][:].rearrange("p u (q r) -> p u q r", r=8), b_sb[i][:].bitcast(F32)[:, 512 * h : 512 * (h + 1)].rearrange("p (q u r) -> p u q r", u=2, r=8))
 
         def turn_b(banks, i):
             for h in range(2):
@@ -122,8 +123,8 @@ def tile_rpa_density_step_s12_kernel(tc, d, b, gap, h_words, h_scales, x_words, 
 
         def sort_hs(g):
             nc.vector.tensor_copy(
-                out=h_s[g][:].bitcast(U16).rearrange("p t j m -> p t j m"),
-                in_=hs_in[:, :, 128 * g : 128 * (g + 1)].bitcast(U16).rearrange("p j (m t) -> p t j m", t=4),
+                out=h_s[g][:].bitcast(U16).rearrange("p t j (c i) -> p j c t i", i=8),
+                in_=hs_in[:, :, 128 * g : 128 * (g + 1)].bitcast(U16).rearrange("p j (c i t) -> p j c t i", t=4, i=8),
             )
 
         def mul_t(banks, g, t):
@@ -151,7 +152,7 @@ def tile_rpa_density_step_s12_kernel(tc, d, b, gap, h_words, h_scales, x_words, 
 
         def perm_d(r, h, eng):
             d_perm[r, h] = chis.tile([128, 2, T // 8], F32, name="d_perm", bufs=8)
-            copy(eng, d_perm[r, h][:], d_sb[r][:].bitcast(F32)[:, 512 * h : 512 * (h + 1)].rearrange("p (w u) -> p u w", u=2))
+            copy(eng, d_perm[r, h][:].rearrange("p u (q r) -> p u q r", r=8), d_sb[r][:].bitcast(F32)[:, 512 * h : 512 * (h + 1)].rearrange("p (q u r) -> p u q r", u=2, r=8))
 
         def turn_d(banks, r):
             for h in range(2):
@@ -231,7 +232,15 @@ def tile_rpa_density_step_s12_kernel(tc, d, b, gap, h_words, h_scales, x_words, 
             nc.scalar.copy(out=coul_col[:], in_=spread[0][:, :, 0:4])
 
         def invert_gap():
-            nc.vector.reciprocal(out=ginv[:], in_=gap_sb[:])
+            nc.vector.reciprocal(out=ginv[:].rearrange("p j (u e) -> p u j e", e=2), in_=spread[1][:, :, 0:NJ].bitcast(BF16).rearrange("p u (j e) -> p u j e", e=2))
+
+        def sort_gap():
+            nc.vector.tensor_copy(out=gap_rows[0:NJ].rearrange("p u (q r) -> p u q r", r=8), in_=gap_in[0:NJ, :].bitcast(F32).rearrange("p (q u r) -> p u q r", u=2, r=8))
+
+        def turn_gap(banks):
+            spread[1] = bank(banks[0], [128, 2, 128])
+            for u in range(2):
+                nc.tensor.transpose(spread[1][:, u, :], gap_rows[:, u, :], ident[:])
 
         with tc.manual_schedule():
             queue = {"SP": [], "PE": [], "S": [], "V": []}
@@ -301,14 +310,15 @@ def tile_rpa_density_step_s12_kernel(tc, d, b, gap, h_words, h_scales, x_words, 
             def load_x():
                 nc.sync.dma_start(out=x_w[:].bitcast(I32), in_=x_words.bitcast(I32).rearrange("j p n -> p j n"))
 
-            nc.scalar.dma_start(out=gap_sb[:], in_=gap.rearrange("(j p t) -> p j t", p=128, t=4))
+            nc.scalar.dma_start(out=gap_in[0:NJ, :], in_=gap.rearrange("(j k) -> j k", k=512))
             load_b(0)
             load_b(1)
             nc.vector.memset(hs_in[:], 0)
             nc.vector.memset(x_s[:].rearrange("p j n -> p (j n)").bitcast(I32), 0)
+            nc.vector.memset(gap_rows[:], 0.0)
             nc.vector.memset(coul_rows[:], 0.0)
-            nc.gpsimd.dma_start(out=coul_in[0:4, :].rearrange("t (m e) -> t m e", e=2), in_=coul.rearrange("(m t e) -> t m e", t=4, e=2))
             make_identity(nc, ident[:])
+            nc.gpsimd.dma_start(out=coul_in[0:4, :].rearrange("t (m e) -> t m e", e=2), in_=coul.rearrange("(m t e) -> t m e", t=4, e=2))
             for c in range(4):
                 nc.sync.dma_start(out=hs_in[32 * c : 32 * c + 4], in_=h_scales.bitcast(I32)[:, 4 * c : 4 * c + 4, :].rearrange("j r n -> r j n"))
             load_h(0)
@@ -344,6 +354,7 @@ def tile_rpa_density_step_s12_kernel(tc, d, b, gap, h_words, h_scales, x_words, 
                     p_c(u, v)
                     s_ec(u, v, "S")
 
+            pe("rest", "tgap", ["gap_rows"], ["ginv"], turn_gap)
             p_tb(0)
             p_tb(1)
             pe("rest", "spread", ["coul_rows"], ["coul_col"], turn_coul)
@@ -377,8 +388,9 @@ def tile_rpa_density_step_s12_kernel(tc, d, b, gap, h_words, h_scales, x_words, 
             for r in range(8, 12):
                 p_o(r)
 
+            step("V", "gap_rows", [], sort_gap)
             s_pb(0, "V")
-            step("V", "ginv", [], invert_gap)
+            step("V", "ginv", ["tgap"], invert_gap)
             v_m(0)
             v_sh(0)
             v_mb(1, 0)

@@ -38,11 +38,9 @@ def tile_rpa_density_step_s12_kernel(tc, d, b, gap, h_words, h_scales, x_words, 
         psum = ctx.enter_context(tc.psum_pool(name="psum", bufs=1))
 
         ident = keep.tile([128, 128], F32, name="ident")
-        gap_in = keep.tile([128, 512], BF16, name="gap_in")
-        gap_rows = keep.tile([128, 2, 128], F32, name="gap_rows")
+        gap_in = keep.tile([128, NJ, 4], BF16, name="gap_in")
         ginv = keep.tile([128, NJ, 4], F32, name="ginv")
-        coul_in = keep.tile([128, NG * 128], BF16, name="coul_in")
-        coul_rows = keep.tile([128, NG * 128], F32, name="coul_rows")
+        coul_in = keep.tile([128, NG, 4], BF16, name="coul_in")
         coul_col = keep.tile([128, NG, 4], F32, name="coul_col")
         x_w = keep.tile([128, NF, 2 * P], U8, name="x_w", align_bytes=64)
         x_s = keep.tile([128, NF, P], U8, name="x_s", align_bytes=64)
@@ -60,7 +58,7 @@ def tile_rpa_density_step_s12_kernel(tc, d, b, gap, h_words, h_scales, x_words, 
         ccodes = [[keep.tile([128, 256], U32, name=f"ccodes{q}_{g}", align_bytes=64) for g in range(NG)] for q in range(NQ)]
         cscale = [[keep.tile([128, 256], U8, name=f"cscale{q}_{g}", align_bytes=64) for g in range(NG)] for q in range(NQ)]
 
-        b_rows = b.rearrange("(g m t e) k -> g t e m k", m=64, t=4, e=2)
+        b_rows = b.rearrange("(g p t) k -> g t p k", p=128, t=4)
         b_sb, d_sb, n0_sb, d_perm, b_t, d_t, pot, chi = {}, {}, {}, {}, {}, {}, {}, {}
         tr_b, tr_d, tr_p, ps_c, ps_o, ps_t, res, spread, b_perm = {}, {}, {}, {}, {}, {}, {}, {}, {}
         turn = {"b": 0, "rest": 0}
@@ -77,8 +75,7 @@ def tile_rpa_density_step_s12_kernel(tc, d, b, gap, h_words, h_scales, x_words, 
 
         def load_b(i):
             b_sb[i] = rows.tile([128, T], BF16, name="b_sb")
-            for e in range(2):
-                nc.sync.dma_start(out=b_sb[i][e:128:2, :], in_=b_rows[i // 4, i % 4, e])
+            nc.sync.dma_start(out=b_sb[i][:], in_=b_rows[i // 4, i % 4])
 
         def load_d(r):
             d_sb[r] = rows.tile([128, T], BF16, name="d_sb")
@@ -93,14 +90,18 @@ def tile_rpa_density_step_s12_kernel(tc, d, b, gap, h_words, h_scales, x_words, 
 
         def perm_b(i, h, eng):
             b_perm[i, h] = work4.tile([128, 2, T // 8], F32, name="b_perm")
-            copy(eng, b_perm[i, h][:].rearrange("p u (q r) -> p u q r", r=8), b_sb[i][:].bitcast(F32)[:, 512 * h : 512 * (h + 1)].rearrange("p (q u r) -> p u q r", u=2, r=8))
+            copy(eng, b_perm[i, h][:].rearrange("p u (c i) -> p c u i", i=4), b_sb[i][:].bitcast(F32)[:, 512 * h : 512 * (h + 1)].rearrange("p (c i u) -> p c u i", u=2, i=4))
 
         def turn_b(banks, i):
             for h in range(2):
                 tr_b[i, h] = bank(banks[h], [128, 2, 2, 128])
                 for jj in range(2):
                     for u in range(2):
-                        nc.tensor.transpose(tr_b[i, h][:, u, jj, :], b_perm[i, h][:, u, 128 * jj : 128 * (jj + 1)], ident[:])
+                        if (i, h) in b_perm:
+                            words = b_perm[i, h][:, u, 128 * jj : 128 * (jj + 1)]
+                        else:
+                            words = b_sb[i][:].bitcast(F32)[:, 512 * h + 256 * jj + u : 512 * h + 256 * (jj + 1) : 2]
+                        nc.tensor.transpose(tr_b[i, h][:, u, jj, :], words, ident[:])
 
         def scale_b(i, h):
             if h == 0:
@@ -117,14 +118,14 @@ def tile_rpa_density_step_s12_kernel(tc, d, b, gap, h_words, h_scales, x_words, 
 
         def sort_h(g):
             nc.vector.tensor_copy(
-                out=h_w[g][:].bitcast(I32).rearrange("p t j (c i) -> p j c t i", i=4),
-                in_=h_in[g][:].rearrange("p j (c i t) -> p j c t i", t=4, i=4),
+                out=h_w[g][:].bitcast(U16).rearrange("p t j (c i) -> p j c t i", i=8),
+                in_=h_in[g][:].bitcast(U16).rearrange("p j (c i t) -> p j c t i", t=4, i=8),
             )
 
         def sort_hs(g):
             nc.vector.tensor_copy(
-                out=h_s[g][:].bitcast(U16).rearrange("p t j (c i) -> p j c t i", i=8),
-                in_=hs_in[:, :, 128 * g : 128 * (g + 1)].bitcast(U16).rearrange("p j (c i t) -> p j c t i", t=4, i=8),
+                out=h_s[g][:].rearrange("p t j (c i) -> p j c t i", i=16),
+                in_=hs_in[:, :, 128 * g : 128 * (g + 1)].bitcast(U8).rearrange("p j (c i t) -> p j c t i", t=4, i=16),
             )
 
         def mul_t(banks, g, t):
@@ -152,7 +153,7 @@ def tile_rpa_density_step_s12_kernel(tc, d, b, gap, h_words, h_scales, x_words, 
 
         def perm_d(r, h, eng):
             d_perm[r, h] = chis.tile([128, 2, T // 8], F32, name="d_perm", bufs=8)
-            copy(eng, d_perm[r, h][:].rearrange("p u (q r) -> p u q r", r=8), d_sb[r][:].bitcast(F32)[:, 512 * h : 512 * (h + 1)].rearrange("p (q u r) -> p u q r", u=2, r=8))
+            copy(eng, d_perm[r, h][:].rearrange("p u (c i) -> p c u i", i=4), d_sb[r][:].bitcast(F32)[:, 512 * h : 512 * (h + 1)].rearrange("p (c i u) -> p c u i", u=2, i=4))
 
         def turn_d(banks, r):
             for h in range(2):
@@ -221,28 +222,13 @@ def tile_rpa_density_step_s12_kernel(tc, d, b, gap, h_words, h_scales, x_words, 
             nc.sync.dma_start(out=out[r * 128 : (r + 1) * 128, :], in_=res[r][:])
 
         def widen_coul():
-            nc.scalar.copy(out=coul_rows[0:4, :], in_=coul_in[0:4, :])
-
-        def turn_coul(banks):
-            spread[0] = bank(banks[0], [128, NG, 128])
-            for g in range(NG):
-                nc.tensor.transpose(spread[0][:, g, :], coul_rows[:, 128 * g : 128 * (g + 1)], ident[:])
-
-        def evict_coul():
-            nc.scalar.copy(out=coul_col[:], in_=spread[0][:, :, 0:4])
+            nc.scalar.copy(out=coul_col[:], in_=coul_in[:])
 
         def invert_gap():
-            nc.vector.reciprocal(out=ginv[:].rearrange("p j (u e) -> p u j e", e=2), in_=spread[1][:, :, 0:NJ].bitcast(BF16).rearrange("p u (j e) -> p u j e", e=2))
-
-        def sort_gap():
-            nc.vector.tensor_copy(out=gap_rows[0:NJ].rearrange("p u (q r) -> p u q r", r=8), in_=gap_in[0:NJ, :].bitcast(F32).rearrange("p (q u r) -> p u q r", u=2, r=8))
-
-        def turn_gap(banks):
-            spread[1] = bank(banks[0], [128, 2, 128])
-            for u in range(2):
-                nc.tensor.transpose(spread[1][:, u, :], gap_rows[:, u, :], ident[:])
+            nc.vector.reciprocal(out=ginv[:], in_=gap_in[:])
 
         with tc.manual_schedule():
+            SORTED = (2, 4, 6)
             queue = {"SP": [], "PE": [], "S": [], "V": []}
             holder = {}
 
@@ -273,7 +259,7 @@ def tile_rpa_density_step_s12_kernel(tc, d, b, gap, h_words, h_scales, x_words, 
                             at[eng] = at[eng] + 1
                     assert len(done) > before, [(e, queue[e][at[e]][0], [n for n in queue[e][at[e]][1] if n not in done]) for e in queue if at[e] < len(queue[e])]
 
-            def p_tb(i): pe("b", ("tb", i), [("pb", i, 0), ("pb", i, 1)], [("mb", i, 0), ("mb", i, 1)], turn_b, i)
+            def p_tb(i): pe("b", ("tb", i), [("pb", i, 0), ("pb", i, 1)] if i in SORTED else [("lb", i)], [("mb", i, 0), ("mb", i, 1)], turn_b, i)
             def p_td(r): pe("rest", ("td", r), [("pd", r, 0), ("pd", r, 1)], [("ed", r, 0), ("ed", r, 1)], turn_d, r)
             def p_t(g, m): pe("rest", ("t", g, m), [("sh", g), ("shs", g), "lx"], [("st", g, m)], mul_t, g, m)
             def p_c(q, s): pe("rest", ("c", q, s), [("qb", 2 * s), ("qb", 2 * s + 1), ("qd", q, 0), ("qd", q, 1)], [("ec", q, s)], mul_c, q, s)
@@ -291,7 +277,7 @@ def tile_rpa_density_step_s12_kernel(tc, d, b, gap, h_words, h_scales, x_words, 
             def v_qc(q, g): step("V", ("qc", q, g), [("ec", q, 2 * g), ("ec", q, 2 * g + 1)], quant_c, q, g)
             def v_qp(g): step("V", ("qp", g), [("wp", g)], quant_p, g)
             def v_eo(r): step("V", ("eo", r), [("o", r), ("ln", r // 4)] + ([("so", r - 6)] if r >= 6 else []), evict_o, r)
-            def d_lb(i): step("SP", ("lb", i), [("pb", i - 6, 1)] if i >= 6 else [], load_b, i)
+            def d_lb(i): step("SP", ("lb", i), [("tb", i - 6)] if i >= 6 else [], load_b, i)
             def d_ld(r): step("SP", ("ld", r), [("pd", r - 6, 1)] if r >= 6 else [], load_d, r)
             def s_pb(i, eng):
                 for h in range(2):
@@ -305,26 +291,24 @@ def tile_rpa_density_step_s12_kernel(tc, d, b, gap, h_words, h_scales, x_words, 
                 for j in range(2):
                     v_mb(i, j)
             def v_sh(g):
-                step("V", ("shs", g), [], sort_hs, g)
                 step("V", ("sh", g), [("lh", g)], sort_h, g)
+                step("V", ("shs", g), [], sort_hs, g)
             def load_x():
                 nc.sync.dma_start(out=x_w[:].bitcast(I32), in_=x_words.bitcast(I32).rearrange("j p n -> p j n"))
 
-            nc.scalar.dma_start(out=gap_in[0:NJ, :], in_=gap.rearrange("(j k) -> j k", k=512))
+            nc.scalar.dma_start(out=gap_in[:], in_=gap.rearrange("(j p t) -> p j t", p=128, t=4))
             load_b(0)
             load_b(1)
+            load_h(0)
             nc.vector.memset(hs_in[:], 0)
             nc.vector.memset(x_s[:].rearrange("p j n -> p (j n)").bitcast(I32), 0)
-            nc.vector.memset(gap_rows[:], 0.0)
-            nc.vector.memset(coul_rows[:], 0.0)
             make_identity(nc, ident[:])
-            nc.gpsimd.dma_start(out=coul_in[0:4, :].rearrange("t (m e) -> t m e", e=2), in_=coul.rearrange("(m t e) -> t m e", t=4, e=2))
+            nc.gpsimd.dma_start(out=coul_in[:], in_=coul.rearrange("(g p t) -> p g t", p=128, t=4))
             for c in range(4):
-                nc.sync.dma_start(out=hs_in[32 * c : 32 * c + 4], in_=h_scales.bitcast(I32)[:, 4 * c : 4 * c + 4, :].rearrange("j r n -> r j n"))
-            load_h(0)
+                nc.sync.dma_start(out=hs_in[c:128:32], in_=h_scales.bitcast(I32)[:, c:16:4, :].rearrange("j r n -> r j n"))
             load_x()
             for c in range(4):
-                nc.sync.dma_start(out=x_s[32 * c : 32 * c + 4].bitcast(I32), in_=x_scales.bitcast(I32)[:, 4 * c : 4 * c + 4, :].rearrange("j r n -> r j n"))
+                nc.sync.dma_start(out=x_s[c:128:32].bitcast(I32), in_=x_scales.bitcast(I32)[:, c:16:4, :].rearrange("j r n -> r j n"))
             for key in (("lb", 0), ("lb", 1), ("lh", 0), "lx"):
                 step("SP", key, [], len, [])
             d_lb(2)
@@ -336,7 +320,7 @@ def tile_rpa_density_step_s12_kernel(tc, d, b, gap, h_words, h_scales, x_words, 
             for r in range(6, 2 * NQ):
                 d_ld(r)
             for c in range(3):
-                step("SP", ("ln", c), [("pb", 2 + c, 1)], load_n0, c)
+                step("SP", ("ln", c), [("tb", 2 + c)], load_n0, c)
             for r in range(12):
                 step("SP", ("so", r), [("eo", r)], store, r)
 
@@ -354,14 +338,10 @@ def tile_rpa_density_step_s12_kernel(tc, d, b, gap, h_words, h_scales, x_words, 
                     p_c(u, v)
                     s_ec(u, v, "S")
 
-            pe("rest", "tgap", ["gap_rows"], ["ginv"], turn_gap)
             p_tb(0)
             p_tb(1)
-            pe("rest", "spread", ["coul_rows"], ["coul_col"], turn_coul)
-            s_pb(1, "S")
-            step("S", "coul_rows", [], widen_coul)
-            step("S", "coul_col", ["spread"], evict_coul)
             s_pb(2, "S")
+            step("S", "coul_col", [], widen_coul)
             s_pd(0, "S")
             at = 0
             for n, count in enumerate(runs):
@@ -388,17 +368,15 @@ def tile_rpa_density_step_s12_kernel(tc, d, b, gap, h_words, h_scales, x_words, 
             for r in range(8, 12):
                 p_o(r)
 
-            step("V", "gap_rows", [], sort_gap)
-            s_pb(0, "V")
-            step("V", "ginv", ["tgap"], invert_gap)
-            v_m(0)
+            step("V", "ginv", [], invert_gap)
+            v_mb(0, 0)
             v_sh(0)
+            v_mb(0, 1)
             v_mb(1, 0)
             v_qb(0)
             v_mb(1, 1)
             v_sh(1)
             v_qb(1)
-            s_pb(3, "V")
             for i in range(2, 8):
                 v_mb(i, 0)
                 if i % 2 == 1 and i > 3:
@@ -409,10 +387,10 @@ def tile_rpa_density_step_s12_kernel(tc, d, b, gap, h_words, h_scales, x_words, 
                     v_qd(0, 0)
                     v_qd(0, 1)
                     v_qb(3)
-                if i + 2 < 8:
-                    s_pb(i + 2, "V")
-                else:
+                if i + 2 >= 8:
                     s_pd(i + 1, "V")
+                elif i + 2 in SORTED:
+                    s_pb(i + 2, "V")
                 if i != 3:
                     v_qb(i)
             s_pd(9, "V")

@@ -23,7 +23,7 @@ NG = A // 512
 NB = A // 128
 NS = NB // 2
 NQ = R // 256
-NM = P // 128
+FIRST_BLOCK = 8
 
 
 def tile_rpa_density_step_s12_kernel(tc, d, b, gap, h_words, h_scales, x_words, x_scales, coul, n0, out):
@@ -33,6 +33,7 @@ def tile_rpa_density_step_s12_kernel(tc, d, b, gap, h_words, h_scales, x_words, 
         rows = ctx.enter_context(tc.tile_pool(name="rows", bufs=6))
         work1 = ctx.enter_context(tc.tile_pool(name="work1", bufs=1))
         work3 = ctx.enter_context(tc.tile_pool(name="work3", bufs=3))
+        work2 = ctx.enter_context(tc.tile_pool(name="work2", bufs=2))
         work4 = ctx.enter_context(tc.tile_pool(name="work4", bufs=4))
         chis = ctx.enter_context(tc.tile_pool(name="chis", bufs=6))
         psum = ctx.enter_context(tc.psum_pool(name="psum", bufs=1))
@@ -60,7 +61,7 @@ def tile_rpa_density_step_s12_kernel(tc, d, b, gap, h_words, h_scales, x_words, 
 
         b_rows = b.rearrange("(g p t) k -> g t p k", p=128, t=4)
         b_sb, d_sb, n0_sb, d_perm, b_t, d_t, pot, chi = {}, {}, {}, {}, {}, {}, {}, {}
-        tr_b, tr_d, tr_p, ps_c, ps_o, ps_t, res, spread, b_perm = {}, {}, {}, {}, {}, {}, {}, {}, {}
+        tr_b, tr_d, tr_p, ps_c, ps_o, ps_t, res, d_flip, b_perm = {}, {}, {}, {}, {}, {}, {}, {}, {}
         turn = {"b": 0, "rest": 0}
         ring = {"b": [0, 1, 2, 3], "rest": [4, 5, 6, 7]}
 
@@ -152,7 +153,7 @@ def tile_rpa_density_step_s12_kernel(tc, d, b, gap, h_words, h_scales, x_words, 
             nc.vector.quantize_mx(out=pcodes[g][:].bitcast(FP8X4), scales=pscale[g][:], in_=pot[g][:].rearrange("p n t -> p (n t)"))
 
         def perm_d(r, h, eng):
-            d_perm[r, h] = chis.tile([128, 2, T // 8], F32, name="d_perm", bufs=8)
+            d_perm[r, h] = chis.tile([128, 2, T // 8], F32, name="d_perm", bufs=6)
             copy(eng, d_perm[r, h][:].rearrange("p u (c i) -> p c u i", i=4), d_sb[r][:].bitcast(F32)[:, 512 * h : 512 * (h + 1)].rearrange("p (c i u) -> p c u i", u=2, i=4))
 
         def turn_d(banks, r):
@@ -167,6 +168,34 @@ def tile_rpa_density_step_s12_kernel(tc, d, b, gap, h_words, h_scales, x_words, 
             if r % 2 == 0:
                 d_t[q, h] = work4.tile([128, 2, 256, 2], F32, name="d_t", align_bytes=64)
             copy(eng, d_t[q, h][:, :, 128 * (r % 2) : 128 * (r % 2) + 128, :], tr_d[r, h][:].rearrange("p j u a -> p j a u"))
+
+        def load_blocks(r):
+            d_sb[r] = rows.tile([128, 4, NJ, 128], BF16, name="d_sb")
+            src = d[256 * (r // 2) : 256 * (r // 2 + 1), :].rearrange("(i c) (j s k) -> s i c j k", c=8, s=4, k=128)
+            for s in (0, 2, 1, 3):
+                nc.sync.dma_start(out=d_sb[r][32 * s : 32 * (s + 1)], in_=src[s, :, 4 * (r % 2) : 4 * (r % 2) + 4])
+
+        def perm_blocks(r, eng):
+            d_perm[r] = work3.tile([128, 16, 2, 32], F32, name="b_t", align_bytes=64)
+            copy(
+                eng,
+                d_perm[r][:].rearrange("p n u (a i) -> p n a u i", i=4),
+                d_sb[r][:].rearrange("p c j k -> p (c j k)").bitcast(F32).rearrange("p (n a i u) -> p n a u i", n=16, i=4, u=2),
+            )
+
+        def turn_blocks(r):
+            d_flip[r] = work2.tile([128, 4, NJ, 2, 32], F32, name="d_flip", align_bytes=64)
+            nc.vector.transpose(out=d_flip[r][:].rearrange("p c j u i -> p (c j u i)"), in_=d_perm[r][:].rearrange("p n u w -> p (n u w)"))
+
+        def weave_blocks(r, h, eng):
+            q = r // 2
+            if r % 2 == 0:
+                d_t[q, h] = work4.tile([128, 2, 256, 2], F32, name="d_t", align_bytes=64)
+            copy(
+                eng,
+                d_t[q, h][:, :, 128 * (r % 2) : 128 * (r % 2) + 128, :].rearrange("p j (c i) u -> p j c i u", i=32),
+                d_flip[r][:, :, 2 * h : 2 * h + 2].rearrange("p c j u i -> p j c i u"),
+            )
 
         def quant_d(q, h):
             nc.vector.quantize_mx(
@@ -194,7 +223,8 @@ def tile_rpa_density_step_s12_kernel(tc, d, b, gap, h_words, h_scales, x_words, 
             g, tp = s // 2, s % 2
             if tp == 0:
                 chi[q, g] = chis.tile([128, 256, 4], BF16, name="chi", align_bytes=64)
-            copy(eng, chi[q, g][:, :, 2 * tp : 2 * tp + 2], ps_c[q, s][:].rearrange("p e a -> p a e"))
+            order = "p e (c i) -> p i c e" if 2 * q >= FIRST_BLOCK else "p e (i c) -> p i c e"
+            copy(eng, chi[q, g][:, :, 2 * tp : 2 * tp + 2].rearrange("p (i c) e -> p i c e", c=8), ps_c[q, s][:].rearrange(order, c=8))
 
         def quant_c(q, g):
             nc.vector.quantize_mx(out=ccodes[q][g][:].bitcast(FP8X4), scales=cscale[q][g][:], in_=chi[q, g][:].rearrange("p a t -> p (a t)"))
@@ -266,7 +296,7 @@ def tile_rpa_density_step_s12_kernel(tc, d, b, gap, h_words, h_scales, x_words, 
             def p_o(r): pe("rest", ("o", r), [("qc", r // 2, 0), ("qc", r // 2, 1), ("qp", 0), ("qp", 1)], [("eo", r)], mul_o, r)
             def s_pd(r, eng):
                 for h in range(2):
-                    step(eng, ("pd", r, h), [("ld", r)] + ([("td", r - 4)] if r >= 4 else []), perm_d, r, h, eng)
+                    step(eng, ("pd", r, h), [("ld", r)] + ([("td", r - 3)] if r >= 3 else []), perm_d, r, h, eng)
             def s_ed(r, h, eng): step(eng, ("ed", r, h), [("td", r)] + ([("qd", r // 2 - 2, h)] if r >= 4 else []), evict_d, r, h, eng)
             def s_ec(q, s, eng): step(eng, ("ec", q, s), [("c", q, s)], evict_c, q, s, eng)
             def v_wp(g): step("V", ("wp", g), [("st", g, t) for t in range(4)] + ([("qp", 0)] if g else []), weave_p, g)
@@ -287,6 +317,15 @@ def tile_rpa_density_step_s12_kernel(tc, d, b, gap, h_words, h_scales, x_words, 
             def s_e(r):
                 s_ed(r, 0, "S")
                 s_ed(r, 1, "S")
+            def d_lk(r):
+                step("SP", ("ld", r), [("pd", r - 6, 1)], load_blocks, r)
+            def s_pk(r, eng):
+                step(eng, ("pk", r), [("ld", r), ("qb", r - 3) if r < 11 else ("tk", 8)], perm_blocks, r, eng)
+            def v_tk(r):
+                step("V", ("tk", r), [("pk", r)] + ([("ed", r - 2, 1)] if r >= 10 else []), turn_blocks, r)
+            def s_wk(r, eng):
+                for h in range(2):
+                    step(eng, ("ed", r, h), [("tk", r), ("qd", r // 2 - 2, h)], weave_blocks, r, h, eng)
             def v_m(i):
                 for j in range(2):
                     v_mb(i, j)
@@ -317,8 +356,10 @@ def tile_rpa_density_step_s12_kernel(tc, d, b, gap, h_words, h_scales, x_words, 
             for i in range(3, 8):
                 d_lb(i)
                 d_ld(i - 2)
-            for r in range(6, 2 * NQ):
+            for r in range(6, FIRST_BLOCK):
                 d_ld(r)
+            for r in range(FIRST_BLOCK, 2 * NQ):
+                d_lk(r)
             for c in range(3):
                 step("SP", ("ln", c), [("tb", 2 + c)], load_n0, c)
             for r in range(12):
@@ -328,7 +369,7 @@ def tile_rpa_density_step_s12_kernel(tc, d, b, gap, h_words, h_scales, x_words, 
             for s in range(NS):
                 mx = mx + [("c", q, s) for q in range(s)] + [("c", s, t) for t in range(s + 1)]
             mx = mx + [("c", q, t) for q in range(NS, NQ) for t in range(NS)]
-            runs = [3, 3, 2, 1, 1, 2, 2, 3, 4, 3]
+            runs = [3, 3, 2, 1, 1, 2, 2, 3]
 
             def product(kind, u, v):
                 if kind == "t":
@@ -362,11 +403,13 @@ def tile_rpa_density_step_s12_kernel(tc, d, b, gap, h_words, h_scales, x_words, 
                 if 1 <= n < 6:
                     s_pd(n + 1, "S")
                 at = at + count
+            side = {1: [(s_wk, 8)], 2: [(s_wk, 9)], 4: [(s_pk, 10)], 5: [(s_pk, 11)], 7: [(s_wk, 10)], 8: [(s_wk, 11)]}
             for n, (kind, u, v) in enumerate(mx[at:]):
+                for fn, r in side.get(n, []):
+                    fn(r, "S")
                 product(kind, u, v)
-                p_o(n)
-            for r in range(8, 12):
-                p_o(r)
+                for r in {7: [0], 8: [1], 9: [2], 10: [3, 4, 5], 11: [6], 14: [7, 8, 9, 10, 11]}.get(n, []):
+                    p_o(r)
 
             step("V", "ginv", [], invert_gap)
             v_mb(0, 0)
@@ -387,43 +430,46 @@ def tile_rpa_density_step_s12_kernel(tc, d, b, gap, h_words, h_scales, x_words, 
                     v_qd(0, 0)
                     v_qd(0, 1)
                     v_qb(3)
-                if i + 2 >= 8:
+                if i == 6:
                     s_pd(i + 1, "V")
                 elif i + 2 in SORTED:
                     s_pb(i + 2, "V")
                 if i != 3:
                     v_qb(i)
-            s_pd(9, "V")
+            s_pk(8, "V")
             v_qd(3, 0)
             v_qd(3, 1)
+            v_tk(8)
+            s_pk(9, "V")
             v_qc(0, 0)
-            v_qc(1, 0)
-            s_pd(10, "V")
-            s_pd(11, "V")
-            v_qc(2, 0)
+            v_tk(9)
             v_wp(0)
-            v_qc(0, 1)
+            v_qc(1, 0)
             v_qp(0)
+            v_qc(2, 0)
+            v_wp(1)
             v_qd(4, 0)
             v_qd(4, 1)
-            v_wp(1)
-            v_qc(1, 1)
             v_qp(1)
+            v_qc(0, 1)
+            v_tk(10)
+            v_qc(1, 1)
+            v_tk(11)
             v_qc(2, 1)
+            v_eo(0)
             v_qc(3, 0)
+            v_qc(3, 1)
+            v_eo(1)
             v_qd(5, 0)
             v_qd(5, 1)
-            v_qc(3, 1)
-            v_eo(0)
-            v_eo(1)
-            v_qc(4, 0)
             v_eo(2)
             v_eo(3)
-            v_qc(4, 1)
+            v_qc(4, 0)
             v_eo(4)
             v_eo(5)
-            v_qc(5, 0)
+            v_qc(4, 1)
             v_eo(6)
+            v_qc(5, 0)
             v_eo(7)
             v_qc(5, 1)
             for r in range(8, 12):

@@ -39,7 +39,8 @@ def tile_rpa_density_step_s12_kernel(tc, d, b, gap, h_words, h_scales, x_words, 
         psum = ctx.enter_context(tc.psum_pool(name="psum", bufs=1))
 
         ident = keep.tile([128, 128], F32, name="ident")
-        gap_in = keep.tile([128, NJ, 4], BF16, name="gap_in")
+        gap_in = keep.tile([128, 512], BF16, name="gap_in")
+        gap_rows = keep.tile([128, 2, 128], F32, name="gap_rows")
         ginv = keep.tile([128, NJ, 4], F32, name="ginv")
         coul_in = keep.tile([128, NG, 4], BF16, name="coul_in")
         coul_col = keep.tile([128, NG, 4], F32, name="coul_col")
@@ -93,9 +94,9 @@ def tile_rpa_density_step_s12_kernel(tc, d, b, gap, h_words, h_scales, x_words, 
             b_perm[i, h] = work4.tile([128, 2, T // 8], F32, name="b_perm")
             copy(eng, b_perm[i, h][:].rearrange("p u (c i) -> p c u i", i=4), b_sb[i][:].bitcast(F32)[:, 512 * h : 512 * (h + 1)].rearrange("p (c i u) -> p c u i", u=2, i=4))
 
-        def turn_b(banks, i):
-            for h in range(2):
-                tr_b[i, h] = bank(banks[h], [128, 2, 2, 128])
+        def turn_b(banks, i, h):
+            if True:
+                tr_b[i, h] = bank(banks[0], [128, 2, 2, 128])
                 for jj in range(2):
                     for u in range(2):
                         if (i, h) in b_perm:
@@ -255,7 +256,15 @@ def tile_rpa_density_step_s12_kernel(tc, d, b, gap, h_words, h_scales, x_words, 
             nc.scalar.copy(out=coul_col[:], in_=coul_in[:])
 
         def invert_gap():
-            nc.vector.reciprocal(out=ginv[:], in_=gap_in[:])
+            nc.vector.reciprocal(out=ginv[:].rearrange("p j (u e) -> p u j e", e=2), in_=tr_b["gap"][:, :, 0:NJ].bitcast(BF16).rearrange("p u (j e) -> p u j e", e=2))
+
+        def sort_gap():
+            nc.vector.tensor_copy(out=gap_rows[0:NJ], in_=gap_in[0:NJ, :].bitcast(F32).rearrange("p (w u) -> p u w", u=2))
+
+        def turn_gap(banks):
+            tr_b["gap"] = bank(banks[0], [128, 2, 128])
+            for u in range(2):
+                nc.tensor.transpose(tr_b["gap"][:, u, :], gap_rows[:, u, :], ident[:])
 
         with tc.manual_schedule():
             SORTED = (2, 4, 6)
@@ -289,7 +298,10 @@ def tile_rpa_density_step_s12_kernel(tc, d, b, gap, h_words, h_scales, x_words, 
                             at[eng] = at[eng] + 1
                     assert len(done) > before, [(e, queue[e][at[e]][0], [n for n in queue[e][at[e]][1] if n not in done]) for e in queue if at[e] < len(queue[e])]
 
-            def p_tb(i): pe("b", ("tb", i), [("pb", i, 0), ("pb", i, 1)] if i in SORTED else [("lb", i)], [("mb", i, 0), ("mb", i, 1)], turn_b, i)
+            def p_tbh(i, h): pe("b", ("tb", i) if h else ("tbh", i), [("pb", i, h)] if i in SORTED else [("lb", i)], [("mb", i, h)], turn_b, i, h)
+            def p_tb(i):
+                p_tbh(i, 0)
+                p_tbh(i, 1)
             def p_td(r): pe("rest", ("td", r), [("pd", r, 0), ("pd", r, 1)], [("ed", r, 0), ("ed", r, 1)], turn_d, r)
             def p_t(g, m): pe("rest", ("t", g, m), [("sh", g), ("shs", g), "lx"], [("st", g, m)], mul_t, g, m)
             def p_c(q, s): pe("rest", ("c", q, s), [("qb", 2 * s), ("qb", 2 * s + 1), ("qd", q, 0), ("qd", q, 1)], [("ec", q, s)], mul_c, q, s)
@@ -300,7 +312,7 @@ def tile_rpa_density_step_s12_kernel(tc, d, b, gap, h_words, h_scales, x_words, 
             def s_ed(r, h, eng): step(eng, ("ed", r, h), [("td", r)] + ([("qd", r // 2 - 2, h)] if r >= 4 else []), evict_d, r, h, eng)
             def s_ec(q, s, eng): step(eng, ("ec", q, s), [("c", q, s)], evict_c, q, s, eng)
             def v_wp(g): step("V", ("wp", g), [("st", g, t) for t in range(4)] + ([("qp", 0)] if g else []), weave_p, g)
-            def v_mb(i, h): step("V", ("mb", i, h), [("tb", i), "ginv"] + ([("qb", i - 3)] if i >= 3 else []), scale_b, i, h)
+            def v_mb(i, h): step("V", ("mb", i, h), [("tb", i) if h else ("tbh", i), "ginv"] + ([("qb", i - 3)] if i >= 3 else []), scale_b, i, h)
             def v_qb(i): step("V", ("qb", i), [("mb", i, 0), ("mb", i, 1)], quant_b, i)
             def s_st(g, m): step("S", ("st", g, m), [("t", g, m), "coul_col"], scale_t, g, m)
             def v_qd(q, h): step("V", ("qd", q, h), [("ed", 2 * q, h), ("ed", 2 * q + 1, h)], quant_d, q, h)
@@ -335,12 +347,13 @@ def tile_rpa_density_step_s12_kernel(tc, d, b, gap, h_words, h_scales, x_words, 
             def load_x():
                 nc.sync.dma_start(out=x_w[:].bitcast(I32), in_=x_words.bitcast(I32).rearrange("j p n -> p j n"))
 
-            nc.scalar.dma_start(out=gap_in[:], in_=gap.rearrange("(j p t) -> p j t", p=128, t=4))
+            nc.scalar.dma_start(out=gap_in[0:NJ, :], in_=gap.rearrange("(j k) -> j k", k=512))
             load_b(0)
-            load_b(1)
             load_h(0)
+            load_b(1)
             nc.vector.memset(hs_in[:], 0)
             nc.vector.memset(x_s[:].rearrange("p j n -> p (j n)").bitcast(I32), 0)
+            nc.vector.memset(gap_rows[:], 0.0)
             make_identity(nc, ident[:])
             nc.gpsimd.dma_start(out=coul_in[:], in_=coul.rearrange("(g p t) -> p g t", p=128, t=4))
             for c in range(4):
@@ -379,7 +392,9 @@ def tile_rpa_density_step_s12_kernel(tc, d, b, gap, h_words, h_scales, x_words, 
                     p_c(u, v)
                     s_ec(u, v, "S")
 
-            p_tb(0)
+            p_tbh(0, 0)
+            pe("rest", "tgap", ["gap_rows"], ["ginv"], turn_gap)
+            p_tbh(0, 1)
             p_tb(1)
             s_pb(2, "S")
             step("S", "coul_col", [], widen_coul)
@@ -411,9 +426,11 @@ def tile_rpa_density_step_s12_kernel(tc, d, b, gap, h_words, h_scales, x_words, 
                 for r in {7: [0], 8: [1], 9: [2], 10: [3, 4, 5], 11: [6], 14: [7, 8, 9, 10, 11]}.get(n, []):
                     p_o(r)
 
-            step("V", "ginv", [], invert_gap)
+            step("V", "gap_rows", [], sort_gap)
+            step("V", ("sh", 0), [("lh", 0)], sort_h, 0)
+            step("V", "ginv", ["tgap"], invert_gap)
             v_mb(0, 0)
-            v_sh(0)
+            step("V", ("shs", 0), [], sort_hs, 0)
             v_mb(0, 1)
             v_mb(1, 0)
             v_qb(0)

@@ -22,8 +22,10 @@ NF = F // 512
 NG = A // 512
 NB = A // 128
 NS = NB // 2
-NQ = R // 256
+ND = R // 128
+NQ = ND // 2
 FIRST_BLOCK = 8
+SORTED = (2, 4, 6)
 
 
 def tile_rpa_density_step_s12_kernel(tc, d, b, gap, h_words, h_scales, x_words, x_scales, coul, n0, out):
@@ -35,7 +37,7 @@ def tile_rpa_density_step_s12_kernel(tc, d, b, gap, h_words, h_scales, x_words, 
         work3 = ctx.enter_context(tc.tile_pool(name="work3", bufs=3))
         work2 = ctx.enter_context(tc.tile_pool(name="work2", bufs=2))
         work4 = ctx.enter_context(tc.tile_pool(name="work4", bufs=4))
-        chis = ctx.enter_context(tc.tile_pool(name="chis", bufs=6))
+        work6 = ctx.enter_context(tc.tile_pool(name="work6", bufs=6))
         psum = ctx.enter_context(tc.psum_pool(name="psum", bufs=1))
 
         ident = keep.tile([128, 128], F32, name="ident")
@@ -62,9 +64,7 @@ def tile_rpa_density_step_s12_kernel(tc, d, b, gap, h_words, h_scales, x_words, 
 
         b_rows = b.rearrange("(g p t) k -> g t p k", p=128, t=4)
         b_sb, d_sb, n0_sb, d_perm, b_t, d_t, pot, chi = {}, {}, {}, {}, {}, {}, {}, {}
-        tr_b, tr_d, tr_p, ps_c, ps_o, ps_t, res, d_flip, b_perm = {}, {}, {}, {}, {}, {}, {}, {}, {}
-        turn = {"b": 0, "rest": 0}
-        ring = {"b": [0, 1, 2, 3], "rest": [4, 5, 6, 7]}
+        tr_gap, tr_b, tr_d, ps_c, ps_o, ps_t, res, d_flip, b_perm, blocks = {}, {}, {}, {}, {}, {}, {}, {}, {}, {}
 
         def bank(n, shape):
             return psum.tile(shape, F32, name=f"bank{n}")
@@ -74,6 +74,10 @@ def tile_rpa_density_step_s12_kernel(tc, d, b, gap, h_words, h_scales, x_words, 
                 nc.scalar.copy(out=dst, in_=src)
             else:
                 nc.vector.tensor_copy(out=dst, in_=src)
+
+        def sort_pairs(eng, dst, tile, h):
+            pairs = tile[:].bitcast(F32)[:, 512 * h : 512 * (h + 1)]
+            copy(eng, dst[:].rearrange("p u (c i) -> p c u i", i=4), pairs.rearrange("p (c i u) -> p c u i", u=2, i=4))
 
         def load_b(i):
             b_sb[i] = rows.tile([128, T], BF16, name="b_sb")
@@ -90,20 +94,26 @@ def tile_rpa_density_step_s12_kernel(tc, d, b, gap, h_words, h_scales, x_words, 
         def load_h(g):
             nc.sync.dma_start(out=h_in[g][:], in_=h_words.bitcast(I32)[:, :, 256 * g : 256 * (g + 1)].rearrange("j p n -> p j n"))
 
+        def load_x():
+            nc.sync.dma_start(out=x_w[:].bitcast(I32), in_=x_words.bitcast(I32).rearrange("j p n -> p j n"))
+
+        def load_scales(plane, scales):
+            for r in range(4):
+                nc.sync.dma_start(out=plane[r:128:32], in_=scales.bitcast(I32)[:, r:16:4, :].rearrange("j Q n -> Q j n"))
+
         def perm_b(i, h, eng):
             b_perm[i, h] = work4.tile([128, 2, T // 8], F32, name="b_perm")
-            copy(eng, b_perm[i, h][:].rearrange("p u (c i) -> p c u i", i=4), b_sb[i][:].bitcast(F32)[:, 512 * h : 512 * (h + 1)].rearrange("p (c i u) -> p c u i", u=2, i=4))
+            sort_pairs(eng, b_perm[i, h], b_sb[i], h)
 
         def turn_b(banks, i, h):
-            if True:
-                tr_b[i, h] = bank(banks[0], [128, 2, 2, 128])
-                for jj in range(2):
-                    for u in range(2):
-                        if (i, h) in b_perm:
-                            words = b_perm[i, h][:, u, 128 * jj : 128 * (jj + 1)]
-                        else:
-                            words = b_sb[i][:].bitcast(F32)[:, 512 * h + 256 * jj + u : 512 * h + 256 * (jj + 1) : 2]
-                        nc.tensor.transpose(tr_b[i, h][:, u, jj, :], words, ident[:])
+            tr_b[i, h] = bank(banks[0], [128, 2, 2, 128])
+            for jj in range(2):
+                for u in range(2):
+                    if i in SORTED:
+                        pairs = b_perm[i, h][:, u, 128 * jj : 128 * (jj + 1)]
+                    else:
+                        pairs = b_sb[i][:].bitcast(F32)[:, 512 * h + 256 * jj + u : 512 * h + 256 * (jj + 1) : 2]
+                    nc.tensor.transpose(tr_b[i, h][:, u, jj, :], pairs, ident[:])
 
         def scale_b(i, h):
             if h == 0:
@@ -154,8 +164,8 @@ def tile_rpa_density_step_s12_kernel(tc, d, b, gap, h_words, h_scales, x_words, 
             nc.vector.quantize_mx(out=pcodes[g][:].bitcast(FP8X4), scales=pscale[g][:], in_=pot[g][:].rearrange("p n t -> p (n t)"))
 
         def perm_d(r, h, eng):
-            d_perm[r, h] = chis.tile([128, 2, T // 8], F32, name="d_perm", bufs=6)
-            copy(eng, d_perm[r, h][:].rearrange("p u (c i) -> p c u i", i=4), d_sb[r][:].bitcast(F32)[:, 512 * h : 512 * (h + 1)].rearrange("p (c i u) -> p c u i", u=2, i=4))
+            d_perm[r, h] = work6.tile([128, 2, T // 8], F32, name="d_perm")
+            sort_pairs(eng, d_perm[r, h], d_sb[r], h)
 
         def turn_d(banks, r):
             for h in range(2):
@@ -164,11 +174,11 @@ def tile_rpa_density_step_s12_kernel(tc, d, b, gap, h_words, h_scales, x_words, 
                     for u in range(2):
                         nc.tensor.transpose(tr_d[r, h][:, jj, u, :], d_perm[r, h][:, u, 128 * jj : 128 * (jj + 1)], ident[:])
 
-        def evict_d(r, h, eng):
+        def evict_d(r, h):
             q = r // 2
             if r % 2 == 0:
                 d_t[q, h] = work4.tile([128, 2, 256, 2], F32, name="d_t", align_bytes=64)
-            copy(eng, d_t[q, h][:, :, 128 * (r % 2) : 128 * (r % 2) + 128, :], tr_d[r, h][:].rearrange("p j u a -> p j a u"))
+            nc.scalar.copy(out=d_t[q, h][:, :, 128 * (r % 2) : 128 * (r % 2) + 128, :], in_=tr_d[r, h][:].rearrange("p j u a -> p j a u"))
 
         def load_blocks(r):
             d_sb[r] = rows.tile([128, 4, NJ, 128], BF16, name="d_sb")
@@ -177,25 +187,24 @@ def tile_rpa_density_step_s12_kernel(tc, d, b, gap, h_words, h_scales, x_words, 
                 nc.sync.dma_start(out=d_sb[r][32 * s : 32 * (s + 1)], in_=src[s, :, 4 * (r % 2) : 4 * (r % 2) + 4])
 
         def perm_blocks(r, eng):
-            d_perm[r] = work3.tile([128, 16, 2, 32], F32, name="b_t", align_bytes=64)
+            blocks[r] = work3.tile([128, 16, 2, 32], F32, name="b_t", align_bytes=64)
             copy(
                 eng,
-                d_perm[r][:].rearrange("p n u (a i) -> p n a u i", i=4),
+                blocks[r][:].rearrange("p n u (a i) -> p n a u i", i=4),
                 d_sb[r][:].rearrange("p c j k -> p (c j k)").bitcast(F32).rearrange("p (n a i u) -> p n a u i", n=16, i=4, u=2),
             )
 
         def turn_blocks(r):
             d_flip[r] = work2.tile([128, 4, NJ, 2, 32], F32, name="d_flip", align_bytes=64)
-            nc.vector.transpose(out=d_flip[r][:].rearrange("p c j u i -> p (c j u i)"), in_=d_perm[r][:].rearrange("p n u w -> p (n u w)"))
+            nc.vector.transpose(out=d_flip[r][:].rearrange("p c j u i -> p (c j u i)"), in_=blocks[r][:].rearrange("p n u w -> p (n u w)"))
 
-        def weave_blocks(r, h, eng):
+        def weave_blocks(r, h):
             q = r // 2
             if r % 2 == 0:
                 d_t[q, h] = work4.tile([128, 2, 256, 2], F32, name="d_t", align_bytes=64)
-            copy(
-                eng,
-                d_t[q, h][:, :, 128 * (r % 2) : 128 * (r % 2) + 128, :].rearrange("p j (c i) u -> p j c i u", i=32),
-                d_flip[r][:, :, 2 * h : 2 * h + 2].rearrange("p c j u i -> p j c i u"),
+            nc.scalar.copy(
+                out=d_t[q, h][:, :, 128 * (r % 2) : 128 * (r % 2) + 128, :].rearrange("p j (c i) u -> p j c i u", i=32),
+                in_=d_flip[r][:, :, 2 * h : 2 * h + 2].rearrange("p c j u i -> p j c i u"),
             )
 
         def quant_d(q, h):
@@ -220,12 +229,12 @@ def tile_rpa_density_step_s12_kernel(tc, d, b, gap, h_words, h_scales, x_words, 
                         stop=(j == NJ - 1),
                     )
 
-        def evict_c(q, s, eng):
+        def evict_c(q, s):
             g, tp = s // 2, s % 2
             if tp == 0:
-                chi[q, g] = chis.tile([128, 256, 4], BF16, name="chi", align_bytes=64)
+                chi[q, g] = work6.tile([128, 256, 4], BF16, name="chi", align_bytes=64)
             order = "p e (c i) -> p i c e" if 2 * q >= FIRST_BLOCK else "p e (i c) -> p i c e"
-            copy(eng, chi[q, g][:, :, 2 * tp : 2 * tp + 2].rearrange("p (i c) e -> p i c e", c=8), ps_c[q, s][:].rearrange(order, c=8))
+            nc.scalar.copy(out=chi[q, g][:, :, 2 * tp : 2 * tp + 2].rearrange("p (i c) e -> p i c e", c=8), in_=ps_c[q, s][:].rearrange(order, c=8))
 
         def quant_c(q, g):
             nc.vector.quantize_mx(out=ccodes[q][g][:].bitcast(FP8X4), scales=cscale[q][g][:], in_=chi[q, g][:].rearrange("p a t -> p (a t)"))
@@ -246,7 +255,7 @@ def tile_rpa_density_step_s12_kernel(tc, d, b, gap, h_words, h_scales, x_words, 
                 )
 
         def evict_o(r):
-            res[r] = chis.tile([128, P], F32, name="res")
+            res[r] = work6.tile([128, P], F32, name="res")
             nc.vector.tensor_tensor(out=res[r][:], in0=n0_sb[r // 4][:, r % 4, :], in1=ps_o[r][:], op=ALU.subtract)
 
         def store(r):
@@ -255,98 +264,247 @@ def tile_rpa_density_step_s12_kernel(tc, d, b, gap, h_words, h_scales, x_words, 
         def widen_coul():
             nc.scalar.copy(out=coul_col[:], in_=coul_in[:])
 
-        def invert_gap():
-            nc.vector.reciprocal(out=ginv[:].rearrange("p j (u e) -> p u j e", e=2), in_=tr_b["gap"][:, :, 0:NJ].bitcast(BF16).rearrange("p u (j e) -> p u j e", e=2))
-
         def sort_gap():
             nc.vector.tensor_copy(out=gap_rows[0:NJ], in_=gap_in[0:NJ, :].bitcast(F32).rearrange("p (w u) -> p u w", u=2))
 
         def turn_gap(banks):
-            tr_b["gap"] = bank(banks[0], [128, 2, 128])
+            tr_gap[0] = bank(banks[0], [128, 2, 128])
             for u in range(2):
-                nc.tensor.transpose(tr_b["gap"][:, u, :], gap_rows[:, u, :], ident[:])
+                nc.tensor.transpose(tr_gap[0][:, u, :], gap_rows[:, u, :], ident[:])
+
+        def invert_gap():
+            gaps = tr_gap[0][:, :, 0:NJ].bitcast(BF16).rearrange("p u (j e) -> p u j e", e=2)
+            nc.vector.reciprocal(out=ginv[:].rearrange("p j (u e) -> p u j e", e=2), in_=gaps)
+
+        queue = {"sync": [], "tensor": [], "scalar": [], "vector": []}
+        engine = {"S": "scalar", "V": "vector"}
+        ring = {"b": [0, 1, 2, 3], "rest": [4, 5, 6, 7]}
+        turn = {"b": 0, "rest": 0}
+        holder = {}
+
+        def step(where, key, needs, fn, *args):
+            queue[where].append((key, needs, fn, args))
+
+        def tensor_step(kind, key, needs, readers, fn, *args):
+            banks = []
+            for reader in readers:
+                n = ring[kind][turn[kind] % len(ring[kind])]
+                turn[kind] = turn[kind] + 1
+                if n in holder:
+                    needs = needs + [holder[n]]
+                holder[n] = reader
+                banks.append(n)
+            step("tensor", key, needs, fn, banks, *args)
+
+        def emit(done):
+            at = {where: 0 for where in queue}
+            while any(at[where] < len(queue[where]) for where in queue):
+                before = len(done)
+                for where in queue:
+                    while at[where] < len(queue[where]) and all(n in done for n in queue[where][at[where]][1]):
+                        key, needs, fn, args = queue[where][at[where]]
+                        fn(*args)
+                        done.add(key)
+                        at[where] = at[where] + 1
+                assert len(done) > before
+
+        def reuse(name, n, *rest):
+            return [(name, n) + rest] if n >= 0 else []
+
+        def plan_load_b(i):
+            step("sync", ("load_b", i), reuse("turn_b", i - 6, 1), load_b, i)
+
+        def plan_load_d(r):
+            step("sync", ("load_d", r), reuse("perm_d", r - 6, 1), load_d if r < FIRST_BLOCK else load_blocks, r)
+
+        def plan_perm_b(i, eng):
+            for h in range(2):
+                step(engine[eng], ("perm_b", i, h), [("load_b", i), ("turn_b", i - 2, 1)], perm_b, i, h, eng)
+
+        def plan_turn_b(i, h):
+            tensor_step("b", ("turn_b", i, h), [("perm_b", i, h) if i in SORTED else ("load_b", i)], [("scale_b", i, h)], turn_b, i, h)
+
+        def plan_scale_b(i, h):
+            step("vector", ("scale_b", i, h), [("turn_b", i, h), "ginv"] + reuse("quant_b", i - 3), scale_b, i, h)
+
+        def plan_quant_b(i):
+            step("vector", ("quant_b", i), [("scale_b", i, 0), ("scale_b", i, 1)], quant_b, i)
+
+        def plan_perm_d(r, eng):
+            for h in range(2):
+                step(engine[eng], ("perm_d", r, h), [("load_d", r)] + reuse("turn_d", r - 3), perm_d, r, h, eng)
+
+        def plan_turn_d(r):
+            tensor_step("rest", ("turn_d", r), [("perm_d", r, 0), ("perm_d", r, 1)], [("d_t", r, 0), ("d_t", r, 1)], turn_d, r)
+
+        def plan_evict_d(r):
+            for h in range(2):
+                step("scalar", ("d_t", r, h), [("turn_d", r)] + reuse("quant_d", r // 2 - 2, h), evict_d, r, h)
+
+        def plan_perm_blocks(r, eng):
+            freed = ("quant_b", r - 3) if r - 3 < NB else ("turn_blocks", r - 3)
+            step(engine[eng], ("perm_blocks", r), [("load_d", r), freed], perm_blocks, r, eng)
+
+        def plan_turn_blocks(r):
+            freed = [("d_t", r - 2, 1)] if r - 2 >= FIRST_BLOCK else []
+            step("vector", ("turn_blocks", r), [("perm_blocks", r)] + freed, turn_blocks, r)
+
+        def plan_weave_blocks(r):
+            for h in range(2):
+                step("scalar", ("d_t", r, h), [("turn_blocks", r), ("quant_d", r // 2 - 2, h)], weave_blocks, r, h)
+
+        def plan_quant_d(q):
+            for h in range(2):
+                step("vector", ("quant_d", q, h), [("d_t", 2 * q, h), ("d_t", 2 * q + 1, h)], quant_d, q, h)
+
+        def plan_trial(g, t):
+            tensor_step("rest", ("mul_t", g, t), [("sort_h", g), ("sort_hs", g)], [("scale_t", g, t)], mul_t, g, t)
+            step("scalar", ("scale_t", g, t), [("mul_t", g, t), "coul_col"], scale_t, g, t)
+
+        def plan_weave_p(g):
+            step("vector", ("weave_p", g), [("scale_t", g, t) for t in range(4)] + reuse("quant_p", g - 1), weave_p, g)
+
+        def plan_quant_p(g):
+            step("vector", ("quant_p", g), [("weave_p", g)], quant_p, g)
+
+        def plan_response(q, s):
+            needs = [("quant_b", 2 * s), ("quant_b", 2 * s + 1), ("quant_d", q, 0), ("quant_d", q, 1)]
+            tensor_step("rest", ("mul_c", q, s), needs, [("evict_c", q, s)], mul_c, q, s)
+            step("scalar", ("evict_c", q, s), [("mul_c", q, s)], evict_c, q, s)
+
+        def plan_quant_c(q, g):
+            step("vector", ("quant_c", q, g), [("evict_c", q, 2 * g), ("evict_c", q, 2 * g + 1)], quant_c, q, g)
+
+        def plan_induced(r):
+            needs = [("quant_c", r // 2, 0), ("quant_c", r // 2, 1), ("quant_p", 0), ("quant_p", 1)]
+            tensor_step("rest", ("mul_o", r), needs, [("evict_o", r)], mul_o, r)
+
+        def plan_evict_o(r):
+            step("vector", ("evict_o", r), [("mul_o", r), ("load_n0", r // 4)] + reuse("store", r - 6), evict_o, r)
+
+        plan_load_b(2)
+        plan_load_d(0)
+        step("sync", ("load_h", 1), [], load_h, 1)
+        for i in range(3, NB):
+            plan_load_b(i)
+            plan_load_d(i - 2)
+        for r in range(NB - 2, ND):
+            plan_load_d(r)
+        for c in range(ND // 4):
+            step("sync", ("load_n0", c), [("turn_b", 2 + c, 1)], load_n0, c)
+        for r in range(ND):
+            step("sync", ("store", r), [("evict_o", r)], store, r)
+
+        trials = [(plan_trial, g, t) for g in range(NG) for t in range(4)]
+        waves = [[(plan_response, q, s) for q in range(s)] + [(plan_response, s, t) for t in range(s + 1)] for s in range(NS)]
+        rounds = [trials[:3], trials[3:6], trials[6:], waves[0]]
+        for wave in waves[1:-1]:
+            rounds = rounds + [wave[: len(wave) // 2], wave[len(wave) // 2 :]]
+        last = len(rounds) - 1
+
+        plan_turn_b(0, 0)
+        tensor_step("rest", "turn_gap", ["gap_rows"], ["ginv"], turn_gap)
+        plan_turn_b(0, 1)
+        plan_turn_b(1, 0)
+        plan_turn_b(1, 1)
+        plan_perm_b(2, "S")
+        step("scalar", "coul_col", [], widen_coul)
+        plan_perm_d(0, "S")
+        for n, products in enumerate(rounds):
+            tiles = [n - 1] if n > 0 else []
+            if 0 < n < last:
+                plan_turn_b(n + 1, 0)
+                plan_turn_b(n + 1, 1)
+            if n == last:
+                tiles = [n - 1, n]
+                ring["rest"] = [0, 1] + [4 + (turn["rest"] + k) % 4 for k in range(4)] + [2, 3]
+                turn["rest"] = 0
+            for r in tiles:
+                plan_turn_d(r)
+            for r in tiles:
+                plan_evict_d(r)
+            if n == 1:
+                plan_perm_d(1, "S")
+            for plan, u, v in products:
+                plan(u, v)
+            if 0 < n < last - 1:
+                plan_perm_d(n + 1, "S")
+
+        units = waves[-1] + [(plan_response, q, s) for q in range(NS, NQ) for s in range(NS)]
+        before = {(1, 3): [(plan_weave_blocks, 8)], (2, 3): [(plan_weave_blocks, 9)], (3, 2): [(plan_perm_blocks, 10, "S")]}
+        before[4, 0] = [(plan_weave_blocks, 10)]
+        before[4, 2] = [(plan_weave_blocks, 11)]
+        after = {(4, 0): [0], (4, 1): [1], (4, 2): [2], (4, 3): [3, 4, 5, 6], (5, 3): [7, 8, 9, 10, 11]}
+        for plan, q, s in units:
+            for job in before.get((q, s), []):
+                job[0](*job[1:])
+            plan(q, s)
+            for r in after.get((q, s), []):
+                plan_induced(r)
+
+        step("vector", "gap_rows", [], sort_gap)
+        step("vector", ("sort_h", 0), [], sort_h, 0)
+        step("vector", "ginv", ["turn_gap"], invert_gap)
+        plan_scale_b(0, 0)
+        step("vector", ("sort_hs", 0), [], sort_hs, 0)
+        plan_scale_b(0, 1)
+        plan_scale_b(1, 0)
+        plan_quant_b(0)
+        plan_scale_b(1, 1)
+        step("vector", ("sort_h", 1), [("load_h", 1)], sort_h, 1)
+        step("vector", ("sort_hs", 1), [], sort_hs, 1)
+        plan_quant_b(1)
+        for i in range(2, NB):
+            plan_scale_b(i, 0)
+            if i in (5, 7):
+                plan_quant_d(i // 2 - 1)
+            plan_scale_b(i, 1)
+            if i == 3:
+                plan_quant_d(0)
+            if i + 2 in SORTED:
+                plan_perm_b(i + 2, "V")
+            if i == NB - 2:
+                plan_perm_d(last, "V")
+            plan_quant_b(i)
+
+        plan_perm_blocks(8, "V")
+        plan_quant_d(3)
+        plan_turn_blocks(8)
+        plan_perm_blocks(9, "V")
+        plan_quant_c(0, 0)
+        plan_turn_blocks(9)
+        plan_weave_p(0)
+        plan_quant_c(1, 0)
+        plan_quant_p(0)
+        plan_quant_c(2, 0)
+        plan_weave_p(1)
+        plan_quant_d(4)
+        plan_quant_p(1)
+        plan_quant_c(0, 1)
+        plan_quant_c(1, 1)
+        plan_turn_blocks(10)
+        plan_quant_c(2, 1)
+        plan_quant_c(3, 0)
+        plan_perm_blocks(11, "V")
+        plan_evict_o(0)
+        plan_turn_blocks(11)
+        plan_quant_c(3, 1)
+        plan_evict_o(1)
+        plan_evict_o(2)
+        plan_quant_d(5)
+        plan_evict_o(3)
+        plan_quant_c(4, 0)
+        plan_evict_o(4)
+        plan_evict_o(5)
+        plan_quant_c(4, 1)
+        plan_evict_o(6)
+        plan_quant_c(5, 0)
+        plan_evict_o(7)
+        plan_quant_c(5, 1)
+        for r in range(8, ND):
+            plan_evict_o(r)
 
         with tc.manual_schedule():
-            SORTED = (2, 4, 6)
-            queue = {"SP": [], "PE": [], "S": [], "V": []}
-            holder = {}
-
-            def step(eng, key, needs, fn, *args):
-                queue[eng].append((key, list(needs), fn, args))
-
-            def pe(kind, key, needs, frees, fn, *args):
-                banks = []
-                for reader in frees:
-                    n = ring[kind][turn[kind] % len(ring[kind])]
-                    turn[kind] = turn[kind] + 1
-                    if n in holder:
-                        needs = needs + [holder[n]]
-                    holder[n] = reader
-                    banks.append(n)
-                step("PE", key, needs, fn, banks, *args)
-
-            def emit():
-                done = set()
-                at = {eng: 0 for eng in queue}
-                while any(at[eng] < len(queue[eng]) for eng in queue):
-                    before = len(done)
-                    for eng in queue:
-                        while at[eng] < len(queue[eng]) and all(n in done for n in queue[eng][at[eng]][1]):
-                            key, needs, fn, args = queue[eng][at[eng]]
-                            fn(*args)
-                            done.add(key)
-                            at[eng] = at[eng] + 1
-                    assert len(done) > before, [(e, queue[e][at[e]][0], [n for n in queue[e][at[e]][1] if n not in done]) for e in queue if at[e] < len(queue[e])]
-
-            def p_tbh(i, h): pe("b", ("tb", i) if h else ("tbh", i), [("pb", i, h)] if i in SORTED else [("lb", i)], [("mb", i, h)], turn_b, i, h)
-            def p_tb(i):
-                p_tbh(i, 0)
-                p_tbh(i, 1)
-            def p_td(r): pe("rest", ("td", r), [("pd", r, 0), ("pd", r, 1)], [("ed", r, 0), ("ed", r, 1)], turn_d, r)
-            def p_t(g, m): pe("rest", ("t", g, m), [("sh", g), ("shs", g), "lx"], [("st", g, m)], mul_t, g, m)
-            def p_c(q, s): pe("rest", ("c", q, s), [("qb", 2 * s), ("qb", 2 * s + 1), ("qd", q, 0), ("qd", q, 1)], [("ec", q, s)], mul_c, q, s)
-            def p_o(r): pe("rest", ("o", r), [("qc", r // 2, 0), ("qc", r // 2, 1), ("qp", 0), ("qp", 1)], [("eo", r)], mul_o, r)
-            def s_pd(r, eng):
-                for h in range(2):
-                    step(eng, ("pd", r, h), [("ld", r)] + ([("td", r - 3)] if r >= 3 else []), perm_d, r, h, eng)
-            def s_ed(r, h, eng): step(eng, ("ed", r, h), [("td", r)] + ([("qd", r // 2 - 2, h)] if r >= 4 else []), evict_d, r, h, eng)
-            def s_ec(q, s, eng): step(eng, ("ec", q, s), [("c", q, s)], evict_c, q, s, eng)
-            def v_wp(g): step("V", ("wp", g), [("st", g, t) for t in range(4)] + ([("qp", 0)] if g else []), weave_p, g)
-            def v_mb(i, h): step("V", ("mb", i, h), [("tb", i) if h else ("tbh", i), "ginv"] + ([("qb", i - 3)] if i >= 3 else []), scale_b, i, h)
-            def v_qb(i): step("V", ("qb", i), [("mb", i, 0), ("mb", i, 1)], quant_b, i)
-            def s_st(g, m): step("S", ("st", g, m), [("t", g, m), "coul_col"], scale_t, g, m)
-            def v_qd(q, h): step("V", ("qd", q, h), [("ed", 2 * q, h), ("ed", 2 * q + 1, h)], quant_d, q, h)
-            def v_qc(q, g): step("V", ("qc", q, g), [("ec", q, 2 * g), ("ec", q, 2 * g + 1)], quant_c, q, g)
-            def v_qp(g): step("V", ("qp", g), [("wp", g)], quant_p, g)
-            def v_eo(r): step("V", ("eo", r), [("o", r), ("ln", r // 4)] + ([("so", r - 6)] if r >= 6 else []), evict_o, r)
-            def d_lb(i): step("SP", ("lb", i), [("tb", i - 6)] if i >= 6 else [], load_b, i)
-            def d_ld(r): step("SP", ("ld", r), [("pd", r - 6, 1)] if r >= 6 else [], load_d, r)
-            def s_pb(i, eng):
-                for h in range(2):
-                    step(eng, ("pb", i, h), [("lb", i)] + ([("tb", i - 2)] if i >= 2 else []), perm_b, i, h, eng)
-            def p_unit(q, s):
-                p_c(q, s)
-            def s_e(r):
-                s_ed(r, 0, "S")
-                s_ed(r, 1, "S")
-            def d_lk(r):
-                step("SP", ("ld", r), [("pd", r - 6, 1)], load_blocks, r)
-            def s_pk(r, eng):
-                step(eng, ("pk", r), [("ld", r), ("qb", r - 3) if r < 11 else ("tk", 8)], perm_blocks, r, eng)
-            def v_tk(r):
-                step("V", ("tk", r), [("pk", r)] + ([("ed", r - 2, 1)] if r >= 10 else []), turn_blocks, r)
-            def s_wk(r, eng):
-                for h in range(2):
-                    step(eng, ("ed", r, h), [("tk", r), ("qd", r // 2 - 2, h)], weave_blocks, r, h, eng)
-            def v_m(i):
-                for j in range(2):
-                    v_mb(i, j)
-            def v_sh(g):
-                step("V", ("sh", g), [("lh", g)], sort_h, g)
-                step("V", ("shs", g), [], sort_hs, g)
-            def load_x():
-                nc.sync.dma_start(out=x_w[:].bitcast(I32), in_=x_words.bitcast(I32).rearrange("j p n -> p j n"))
-
             nc.scalar.dma_start(out=gap_in[0:NJ, :], in_=gap.rearrange("(j k) -> j k", k=512))
             load_b(0)
             load_h(0)
@@ -356,139 +514,7 @@ def tile_rpa_density_step_s12_kernel(tc, d, b, gap, h_words, h_scales, x_words, 
             nc.vector.memset(gap_rows[:], 0.0)
             make_identity(nc, ident[:])
             nc.gpsimd.dma_start(out=coul_in[:], in_=coul.rearrange("(g p t) -> p g t", p=128, t=4))
-            for c in range(4):
-                nc.sync.dma_start(out=hs_in[c:128:32], in_=h_scales.bitcast(I32)[:, c:16:4, :].rearrange("j r n -> r j n"))
+            load_scales(hs_in, h_scales)
             load_x()
-            for c in range(4):
-                nc.sync.dma_start(out=x_s[c:128:32].bitcast(I32), in_=x_scales.bitcast(I32)[:, c:16:4, :].rearrange("j r n -> r j n"))
-            for key in (("lb", 0), ("lb", 1), ("lh", 0), "lx"):
-                step("SP", key, [], len, [])
-            d_lb(2)
-            d_ld(0)
-            step("SP", ("lh", 1), [], load_h, 1)
-            for i in range(3, 8):
-                d_lb(i)
-                d_ld(i - 2)
-            for r in range(6, FIRST_BLOCK):
-                d_ld(r)
-            for r in range(FIRST_BLOCK, 2 * NQ):
-                d_lk(r)
-            for c in range(3):
-                step("SP", ("ln", c), [("tb", 2 + c)], load_n0, c)
-            for r in range(12):
-                step("SP", ("so", r), [("eo", r)], store, r)
-
-            mx = [("t", g, t) for g in range(NG) for t in range(4)]
-            for s in range(NS):
-                mx = mx + [("c", q, s) for q in range(s)] + [("c", s, t) for t in range(s + 1)]
-            mx = mx + [("c", q, t) for q in range(NS, NQ) for t in range(NS)]
-            runs = [3, 3, 2, 1, 1, 2, 2, 3]
-
-            def product(kind, u, v):
-                if kind == "t":
-                    p_t(u, v)
-                    s_st(u, v)
-                else:
-                    p_c(u, v)
-                    s_ec(u, v, "S")
-
-            p_tbh(0, 0)
-            pe("rest", "tgap", ["gap_rows"], ["ginv"], turn_gap)
-            p_tbh(0, 1)
-            p_tb(1)
-            s_pb(2, "S")
-            step("S", "coul_col", [], widen_coul)
-            s_pd(0, "S")
-            at = 0
-            for n, count in enumerate(runs):
-                tiles = [] if n == 0 else [n - 1] if n < 7 else [2 * n - 8, 2 * n - 7]
-                if 1 <= n < 7:
-                    p_tb(n + 1)
-                if n == 7:
-                    ring["rest"] = [0, 1] + [4 + (turn["rest"] + k) % 4 for k in range(4)] + [2, 3]
-                    turn["rest"] = 0
-                for r in tiles:
-                    p_td(r)
-                for r in tiles:
-                    s_e(r)
-                if n == 1:
-                    s_pd(1, "S")
-                for kind, u, v in mx[at : at + count]:
-                    product(kind, u, v)
-                if 1 <= n < 6:
-                    s_pd(n + 1, "S")
-                at = at + count
-            side = {1: [(s_wk, 8)], 2: [(s_wk, 9)], 4: [(s_pk, 10)], 5: [(s_pk, 11)], 7: [(s_wk, 10)], 8: [(s_wk, 11)]}
-            for n, (kind, u, v) in enumerate(mx[at:]):
-                for fn, r in side.get(n, []):
-                    fn(r, "S")
-                product(kind, u, v)
-                for r in {7: [0], 8: [1], 9: [2], 10: [3, 4, 5], 11: [6], 14: [7, 8, 9, 10, 11]}.get(n, []):
-                    p_o(r)
-
-            step("V", "gap_rows", [], sort_gap)
-            step("V", ("sh", 0), [("lh", 0)], sort_h, 0)
-            step("V", "ginv", ["tgap"], invert_gap)
-            v_mb(0, 0)
-            step("V", ("shs", 0), [], sort_hs, 0)
-            v_mb(0, 1)
-            v_mb(1, 0)
-            v_qb(0)
-            v_mb(1, 1)
-            v_sh(1)
-            v_qb(1)
-            for i in range(2, 8):
-                v_mb(i, 0)
-                if i % 2 == 1 and i > 3:
-                    v_qd(i // 2 - 1, 0)
-                    v_qd(i // 2 - 1, 1)
-                v_mb(i, 1)
-                if i == 3:
-                    v_qd(0, 0)
-                    v_qd(0, 1)
-                    v_qb(3)
-                if i == 6:
-                    s_pd(i + 1, "V")
-                elif i + 2 in SORTED:
-                    s_pb(i + 2, "V")
-                if i != 3:
-                    v_qb(i)
-            s_pk(8, "V")
-            v_qd(3, 0)
-            v_qd(3, 1)
-            v_tk(8)
-            s_pk(9, "V")
-            v_qc(0, 0)
-            v_tk(9)
-            v_wp(0)
-            v_qc(1, 0)
-            v_qp(0)
-            v_qc(2, 0)
-            v_wp(1)
-            v_qd(4, 0)
-            v_qd(4, 1)
-            v_qp(1)
-            v_qc(0, 1)
-            v_tk(10)
-            v_qc(1, 1)
-            v_tk(11)
-            v_qc(2, 1)
-            v_eo(0)
-            v_qc(3, 0)
-            v_qc(3, 1)
-            v_eo(1)
-            v_qd(5, 0)
-            v_qd(5, 1)
-            v_eo(2)
-            v_eo(3)
-            v_qc(4, 0)
-            v_eo(4)
-            v_eo(5)
-            v_qc(4, 1)
-            v_eo(6)
-            v_qc(5, 0)
-            v_eo(7)
-            v_qc(5, 1)
-            for r in range(8, 12):
-                v_eo(r)
-            emit()
+            load_scales(x_s[:].bitcast(I32), x_scales)
+            emit({("load_b", 0), ("load_b", 1)})

@@ -25,35 +25,32 @@ NS = NB // 2
 ND = R // 128
 NQ = ND // 2
 FIRST_BLOCK = 8
-SORTED = (2, 4, 6)
+SORTED = {("b", 5), ("b", 6), ("b", 7), ("d", 5), ("d", 7), ("b", 1), ("b", 2), ("b", 3), ("d", 0), ("d", 1), ("d", 2), ("d", 3), ("d", 4), ("d", 6)}
+DEPTH = {"rows": 11, "sortedS": 4, "sortedV": 4, "sortedG": 2, "b_t": 3, "d_t": 6, "d_flip": 2, "pot": 1, "chi": 8, "res": 2}
+OWN = {tag: [f"{tag}{k}" for k in range(n)] for tag, n in DEPTH.items()}
+RINGS = {**OWN, "res": OWN["sortedV"] + OWN["res"], "d_flip": ["h_in0", "h_in1"], "pot": ["hs_in"], "chi": OWN["chi"] + ["h_w0", "h_w1"]}
 
 
 def tile_rpa_density_step_s12_kernel(tc, d, b, gap, h_words, h_scales, x_words, x_scales, coul, n0, out):
     nc = tc.nc
     with ExitStack() as ctx:
         keep = ctx.enter_context(tc.tile_pool(name="keep", bufs=1))
-        rows = ctx.enter_context(tc.tile_pool(name="rows", bufs=6))
-        work1 = ctx.enter_context(tc.tile_pool(name="work1", bufs=1))
-        work3 = ctx.enter_context(tc.tile_pool(name="work3", bufs=3))
-        work2 = ctx.enter_context(tc.tile_pool(name="work2", bufs=2))
-        work4 = ctx.enter_context(tc.tile_pool(name="work4", bufs=4))
-        work6 = ctx.enter_context(tc.tile_pool(name="work6", bufs=6))
         psum = ctx.enter_context(tc.psum_pool(name="psum", bufs=1))
 
         ident = keep.tile([128, 128], F32, name="ident")
-        gap_in = keep.tile([128, 512], BF16, name="gap_in")
-        gap_rows = keep.tile([128, 2, 128], F32, name="gap_rows")
+        gap_in = keep.tile([128, NJ, 4], BF16, name="gap_in")
+        coul_in = keep.tile([128, NG, 128], BF16, name="coul_in")
+        coul_rows = keep.tile([128, NG, 128], F32, name="coul_rows")
         ginv = keep.tile([128, NJ, 4], F32, name="ginv")
-        coul_in = keep.tile([128, NG, 4], BF16, name="coul_in")
         coul_col = keep.tile([128, NG, 4], F32, name="coul_col")
         x_w = keep.tile([128, NF, 2 * P], U8, name="x_w", align_bytes=64)
         x_s = keep.tile([128, NF, P], U8, name="x_s", align_bytes=64)
-        h_in = [keep.tile([128, NF, 256], I32, name=f"h_in{g}") for g in range(NG)]
-        hs_in = keep.tile([128, NF, A // 4], I32, name="hs_in")
-        h_w = [keep.tile([128, 4, NF, 256], U8, name=f"h_w{g}", align_bytes=64) for g in range(NG)]
-        h_s = [keep.tile([128, 4, NF, 128], U8, name=f"h_s{g}", align_bytes=64) for g in range(NG)]
-        bcodes = [keep.tile([128, NJ * 128], U32, name=f"bcodes{i}", align_bytes=64) for i in range(NB)]
-        bscale = [keep.tile([128, NJ * 128], U8, name=f"bscale{i}", align_bytes=64) for i in range(NB)]
+        h_in = [keep.tile([128, NF, 256], I32, name=f"h_in{g}", align_bytes=64) for g in range(NG)]
+        hs_in = keep.tile([128, NF, A // 4], I32, name="hs_in", align_bytes=64)
+        h_w = [keep.tile([128, NF, 4, 256], U8, name=f"h_w{g}", align_bytes=64) for g in range(NG)]
+        h_s = [keep.tile([128, NF, 4, 128], U8, name=f"h_s{g}", align_bytes=64) for g in range(NG)]
+        bcodes = [[keep.tile([128, 2, 4, 128], U32, name=f"bcodes{g}_{h}", align_bytes=64) for h in range(2)] for g in range(NG)]
+        bscale = [[keep.tile([128, 2, 4, 128], U8, name=f"bscale{g}_{h}", align_bytes=64) for h in range(2)] for g in range(NG)]
         dcodes = [[keep.tile([128, 2, 256], U32, name=f"dcodes{q}_{h}", align_bytes=64) for h in range(2)] for q in range(NQ)]
         dscale = [[keep.tile([128, 2, 256], U8, name=f"dscale{q}_{h}", align_bytes=64) for h in range(2)] for q in range(NQ)]
         pot_s = [keep.tile([128, 4, P], BF16, name=f"pot_s{g}") for g in range(NG)]
@@ -62,9 +59,11 @@ def tile_rpa_density_step_s12_kernel(tc, d, b, gap, h_words, h_scales, x_words, 
         ccodes = [[keep.tile([128, 256], U32, name=f"ccodes{q}_{g}", align_bytes=64) for g in range(NG)] for q in range(NQ)]
         cscale = [[keep.tile([128, 256], U8, name=f"cscale{q}_{g}", align_bytes=64) for g in range(NG)] for q in range(NQ)]
 
-        b_rows = b.rearrange("(g p t) k -> g t p k", p=128, t=4)
-        b_sb, d_sb, n0_sb, d_perm, b_t, d_t, pot, chi = {}, {}, {}, {}, {}, {}, {}, {}
-        tr_gap, tr_b, tr_d, ps_c, ps_o, ps_t, res, d_flip, b_perm, blocks = {}, {}, {}, {}, {}, {}, {}, {}, {}, {}
+        b_sb, d_sb, n0_sb, perm, b_t, d_t, pot, chi = {}, {}, {}, {}, {}, {}, {}, {}
+        tr_vec, tr_b, tr_d, ps_c, ps_o, ps_t, res, d_flip = {}, {}, {}, {}, {}, {}, {}, {}
+
+        def buf(name, shape, dtype):
+            return keep.tile(shape, dtype, name=name, align_bytes=64)
 
         def bank(n, shape):
             return psum.tile(shape, F32, name=f"bank{n}")
@@ -79,16 +78,16 @@ def tile_rpa_density_step_s12_kernel(tc, d, b, gap, h_words, h_scales, x_words, 
             pairs = tile[:].bitcast(F32)[:, 512 * h : 512 * (h + 1)]
             copy(eng, dst[:].rearrange("p u (c i) -> p c u i", i=4), pairs.rearrange("p (c i u) -> p c u i", u=2, i=4))
 
-        def load_b(i):
-            b_sb[i] = rows.tile([128, T], BF16, name="b_sb")
-            nc.sync.dma_start(out=b_sb[i][:], in_=b_rows[i // 4, i % 4])
+        def load_b(name, i):
+            b_sb[i] = buf(name, [128, T], BF16)
+            nc.sync.dma_start(out=b_sb[i][:], in_=b[i * 128 : (i + 1) * 128, :])
 
-        def load_d(r):
-            d_sb[r] = rows.tile([128, T], BF16, name="d_sb")
+        def load_d(name, r):
+            d_sb[r] = buf(name, [128, T], BF16)
             nc.sync.dma_start(out=d_sb[r][:], in_=d[r * 128 : (r + 1) * 128, :])
 
-        def load_n0(c):
-            n0_sb[c] = rows.tile([128, 4, P], BF16, name="b_sb")
+        def load_n0(name, c):
+            n0_sb[c] = buf(name, [128, 4, P], BF16)
             nc.sync.dma_start(out=n0_sb[c][:], in_=n0[c * 512 : (c + 1) * 512, :].rearrange("(c p) n -> p c n", p=128))
 
         def load_h(g):
@@ -97,47 +96,54 @@ def tile_rpa_density_step_s12_kernel(tc, d, b, gap, h_words, h_scales, x_words, 
         def load_x():
             nc.sync.dma_start(out=x_w[:].bitcast(I32), in_=x_words.bitcast(I32).rearrange("j p n -> p j n"))
 
-        def load_scales(plane, scales):
+        def load_scales(eng, plane, scales):
             for r in range(4):
-                nc.sync.dma_start(out=plane[r:128:32], in_=scales.bitcast(I32)[:, r:16:4, :].rearrange("j Q n -> Q j n"))
+                eng.dma_start(out=plane[r:128:32], in_=scales.bitcast(I32)[:, r:16:4, :].rearrange("j Q n -> Q j n"))
 
-        def perm_b(i, h, eng):
-            b_perm[i, h] = work4.tile([128, 2, T // 8], F32, name="b_perm")
-            sort_pairs(eng, b_perm[i, h], b_sb[i], h)
+        def sort_rows(name, what, n, h, eng):
+            perm[what, n, h] = buf(name, [128, 2, T // 8], F32)
+            sort_pairs(eng, perm[what, n, h], (b_sb if what == "b" else d_sb)[n], h)
+
+        def pairs_of(what, n, h, jj, u):
+            if (what, n, h) in perm:
+                return perm[what, n, h][:, u, 128 * jj : 128 * (jj + 1)]
+            return (b_sb if what == "b" else d_sb)[n][:].bitcast(F32)[:, 512 * h + 256 * jj + u : 512 * h + 256 * (jj + 1) : 2]
 
         def turn_b(banks, i, h):
             tr_b[i, h] = bank(banks[0], [128, 2, 2, 128])
             for jj in range(2):
                 for u in range(2):
-                    if i in SORTED:
-                        pairs = b_perm[i, h][:, u, 128 * jj : 128 * (jj + 1)]
-                    else:
-                        pairs = b_sb[i][:].bitcast(F32)[:, 512 * h + 256 * jj + u : 512 * h + 256 * (jj + 1) : 2]
-                    nc.tensor.transpose(tr_b[i, h][:, u, jj, :], pairs, ident[:])
+                    cols = tr_b[i, h][:, u, jj, :].rearrange("p (t q r) -> p q t r", t=4, r=8)
+                    nc.tensor.transpose(cols, pairs_of("b", i, h, jj, u), ident[:])
 
-        def scale_b(i, h):
-            if h == 0:
-                b_t[i] = work3.tile([128, NJ, 128, 2, 2], BF16, name="b_t", align_bytes=64)
+        def scale_b(name, i, h):
+            g, c = i // 4, i % 4
+            if c == 0:
+                b_t[g, h] = buf(name, [128, 2, 4, 128, 4], BF16)
             nc.vector.tensor_tensor(
-                out=b_t[i][:, 2 * h : 2 * h + 2],
-                in0=tr_b[i, h][:].bitcast(BF16).rearrange("p u j (a e) -> p j a u e", e=2),
-                in1=ginv[:, 2 * h : 2 * h + 2].rearrange("p j (u e) -> p j u e", e=2).unsqueeze(2).to_broadcast([128, 2, 128, 2, 2]),
+                out=b_t[g, h][:, :, :, 32 * c : 32 * (c + 1), :].rearrange("p j t m e -> p (j t) (m e)"),
+                in0=tr_b[i, h][:].bitcast(BF16).rearrange("p u j (a e) -> p (j a) u e", e=2),
+                in1=ginv[:, 2 * h : 2 * h + 2].unsqueeze(2).to_broadcast([128, 2, 128, 4]),
                 op=ALU.mult,
             )
 
-        def quant_b(i):
-            nc.vector.quantize_mx(out=bcodes[i][:].bitcast(FP8X4), scales=bscale[i][:], in_=b_t[i][:].rearrange("p j a u e -> p (j a u e)"))
+        def quant_b(g, h):
+            nc.vector.quantize_mx(
+                out=bcodes[g][h][:].rearrange("p j t m -> p (j t m)").bitcast(FP8X4),
+                scales=bscale[g][h][:].rearrange("p j t m -> p (j t m)"),
+                in_=b_t[g, h][:].rearrange("p j t m e -> p (j t m e)"),
+            )
 
         def sort_h(g):
             nc.vector.tensor_copy(
-                out=h_w[g][:].bitcast(U16).rearrange("p t j (c i) -> p j c t i", i=8),
-                in_=h_in[g][:].bitcast(U16).rearrange("p j (c i t) -> p j c t i", t=4, i=8),
+                out=h_w[g][:].bitcast(I32).rearrange("p j t (q w) -> p q j t w", w=4),
+                in_=h_in[g][:].rearrange("p j (q t w) -> p q j t w", t=4, w=4),
             )
 
         def sort_hs(g):
             nc.vector.tensor_copy(
-                out=h_s[g][:].rearrange("p t j (c i) -> p j c t i", i=16),
-                in_=hs_in[:, :, 128 * g : 128 * (g + 1)].bitcast(U8).rearrange("p j (c i t) -> p j c t i", t=4, i=16),
+                out=h_s[g][:].bitcast(I32).rearrange("p j t (q w) -> p j q t w", w=2),
+                in_=hs_in[:, :, 128 * g : 128 * (g + 1)].rearrange("p j (q t w) -> p j q t w", t=4, w=2),
             )
 
         def mul_t(banks, g, t):
@@ -145,8 +151,8 @@ def tile_rpa_density_step_s12_kernel(tc, d, b, gap, h_words, h_scales, x_words, 
             for j in range(NF):
                 nc.tensor.matmul_mx(
                     out=ps_t[g, t][:],
-                    lhsT=h_w[g][:, t, j, :].bitcast(FP4X4),
-                    lhsT_scale=h_s[g][:, t, j, :],
+                    lhsT=h_w[g][:, j, t, :].bitcast(FP4X4),
+                    lhsT_scale=h_s[g][:, j, t, :],
                     rhs=x_w[:, j, :].bitcast(FP4X4),
                     rhs_scale=x_s[:, j, :],
                     start=(j == 0),
@@ -156,52 +162,48 @@ def tile_rpa_density_step_s12_kernel(tc, d, b, gap, h_words, h_scales, x_words, 
         def scale_t(g, t):
             nc.scalar.activation(out=pot_s[g][:, t, :], in_=ps_t[g, t][:], func=ACT.Copy, scale=coul_col[:, g, t : t + 1])
 
-        def weave_p(g):
-            pot[g] = work1.tile([128, P, 4], BF16, name="pot", align_bytes=64)
+        def weave_p(name, g):
+            pot[g] = buf(name, [128, P, 4], BF16)
             nc.vector.tensor_copy(out=pot[g][:].rearrange("p (c i) t -> p c t i", i=4), in_=pot_s[g][:].rearrange("p t (c i) -> p c t i", i=4))
 
         def quant_p(g):
             nc.vector.quantize_mx(out=pcodes[g][:].bitcast(FP8X4), scales=pscale[g][:], in_=pot[g][:].rearrange("p n t -> p (n t)"))
-
-        def perm_d(r, h, eng):
-            d_perm[r, h] = work6.tile([128, 2, T // 8], F32, name="d_perm")
-            sort_pairs(eng, d_perm[r, h], d_sb[r], h)
 
         def turn_d(banks, r):
             for h in range(2):
                 tr_d[r, h] = bank(banks[h], [128, 2, 2, 128])
                 for jj in range(2):
                     for u in range(2):
-                        nc.tensor.transpose(tr_d[r, h][:, jj, u, :], d_perm[r, h][:, u, 128 * jj : 128 * (jj + 1)], ident[:])
+                        nc.tensor.transpose(tr_d[r, h][:, jj, u, :], pairs_of("d", r, h, jj, u), ident[:])
 
-        def evict_d(r, h):
+        def evict_d(name, r, h):
             q = r // 2
             if r % 2 == 0:
-                d_t[q, h] = work4.tile([128, 2, 256, 2], F32, name="d_t", align_bytes=64)
+                d_t[q, h] = buf(name, [128, 2, 256, 2], F32)
             nc.scalar.copy(out=d_t[q, h][:, :, 128 * (r % 2) : 128 * (r % 2) + 128, :], in_=tr_d[r, h][:].rearrange("p j u a -> p j a u"))
 
-        def load_blocks(r):
-            d_sb[r] = rows.tile([128, 4, NJ, 128], BF16, name="d_sb")
+        def load_blocks(name, r):
+            d_sb[r] = buf(name, [128, 4, NJ, 128], BF16)
             src = d[256 * (r // 2) : 256 * (r // 2 + 1), :].rearrange("(i c) (j s k) -> s i c j k", c=8, s=4, k=128)
             for s in (0, 2, 1, 3):
                 nc.sync.dma_start(out=d_sb[r][32 * s : 32 * (s + 1)], in_=src[s, :, 4 * (r % 2) : 4 * (r % 2) + 4])
 
-        def perm_blocks(r, eng):
-            blocks[r] = work3.tile([128, 16, 2, 32], F32, name="b_t", align_bytes=64)
+        def sort_blocks(name, r, eng):
+            perm["blocks", r] = buf(name, [128, 16, 2, 32], F32)
             copy(
                 eng,
-                blocks[r][:].rearrange("p n u (a i) -> p n a u i", i=4),
+                perm["blocks", r][:].rearrange("p n u (a i) -> p n a u i", i=4),
                 d_sb[r][:].rearrange("p c j k -> p (c j k)").bitcast(F32).rearrange("p (n a i u) -> p n a u i", n=16, i=4, u=2),
             )
 
-        def turn_blocks(r):
-            d_flip[r] = work2.tile([128, 4, NJ, 2, 32], F32, name="d_flip", align_bytes=64)
-            nc.vector.transpose(out=d_flip[r][:].rearrange("p c j u i -> p (c j u i)"), in_=blocks[r][:].rearrange("p n u w -> p (n u w)"))
+        def turn_blocks(name, r):
+            d_flip[r] = buf(name, [128, 4, NJ, 2, 32], F32)
+            nc.vector.transpose(out=d_flip[r][:].rearrange("p c j u i -> p (c j u i)"), in_=perm["blocks", r][:].rearrange("p n u w -> p (n u w)"))
 
-        def weave_blocks(r, h):
+        def weave_blocks(name, r, h):
             q = r // 2
             if r % 2 == 0:
-                d_t[q, h] = work4.tile([128, 2, 256, 2], F32, name="d_t", align_bytes=64)
+                d_t[q, h] = buf(name, [128, 2, 256, 2], F32)
             nc.scalar.copy(
                 out=d_t[q, h][:, :, 128 * (r % 2) : 128 * (r % 2) + 128, :].rearrange("p j (c i) u -> p j c i u", i=32),
                 in_=d_flip[r][:, :, 2 * h : 2 * h + 2].rearrange("p c j u i -> p j c i u"),
@@ -217,22 +219,22 @@ def tile_rpa_density_step_s12_kernel(tc, d, b, gap, h_words, h_scales, x_words, 
         def mul_c(banks, q, s):
             ps_c[q, s] = bank(banks[0], [128, 2, 256])
             for e in range(2):
-                i = 2 * s + e
+                g, t = s // 2, 2 * (s % 2) + e
                 for j in range(NJ):
                     nc.tensor.matmul_mx(
                         out=ps_c[q, s][:, e, :],
-                        lhsT=bcodes[i][:, 128 * j : 128 * (j + 1)].bitcast(FP8X4),
-                        lhsT_scale=bscale[i][:, 128 * j : 128 * (j + 1)],
+                        lhsT=bcodes[g][j // 2][:, j % 2, t, :].bitcast(FP8X4),
+                        lhsT_scale=bscale[g][j // 2][:, j % 2, t, :],
                         rhs=dcodes[q][j // 2][:, j % 2, :].bitcast(FP8X4),
                         rhs_scale=dscale[q][j // 2][:, j % 2, :],
                         start=(j == 0),
                         stop=(j == NJ - 1),
                     )
 
-        def evict_c(q, s):
+        def evict_c(name, q, s):
             g, tp = s // 2, s % 2
             if tp == 0:
-                chi[q, g] = work6.tile([128, 256, 4], BF16, name="chi", align_bytes=64)
+                chi[q, g] = buf(name, [128, 256, 4], BF16)
             order = "p e (c i) -> p i c e" if 2 * q >= FIRST_BLOCK else "p e (i c) -> p i c e"
             nc.scalar.copy(out=chi[q, g][:, :, 2 * tp : 2 * tp + 2].rearrange("p (i c) e -> p i c e", c=8), in_=ps_c[q, s][:].rearrange(order, c=8))
 
@@ -254,47 +256,67 @@ def tile_rpa_density_step_s12_kernel(tc, d, b, gap, h_words, h_scales, x_words, 
                     stop=(g == NG - 1),
                 )
 
-        def evict_o(r):
-            res[r] = work6.tile([128, P], F32, name="res")
+        def evict_o(name, r):
+            res[r] = buf(name, [128, P], F32)
             nc.vector.tensor_tensor(out=res[r][:], in0=n0_sb[r // 4][:, r % 4, :], in1=ps_o[r][:], op=ALU.subtract)
 
         def store(r):
             nc.sync.dma_start(out=out[r * 128 : (r + 1) * 128, :], in_=res[r][:])
 
-        def widen_coul():
-            nc.scalar.copy(out=coul_col[:], in_=coul_in[:])
+        def load_gap():
+            nc.scalar.dma_start(out=gap_in[:], in_=gap.rearrange("(j p t) -> p j t", p=128, t=4))
 
-        def sort_gap():
-            nc.vector.tensor_copy(out=gap_rows[0:NJ], in_=gap_in[0:NJ, :].bitcast(F32).rearrange("p (w u) -> p u w", u=2))
-
-        def turn_gap(banks):
-            tr_gap[0] = bank(banks[0], [128, 2, 128])
-            for u in range(2):
-                nc.tensor.transpose(tr_gap[0][:, u, :], gap_rows[:, u, :], ident[:])
+        def load_coul():
+            nc.gpsimd.dma_start(out=coul_in[0:4].rearrange("p g (q r) -> p (g q) r", r=8), in_=coul.rearrange("(q t r) -> t q r", t=4, r=8))
 
         def invert_gap():
-            gaps = tr_gap[0][:, :, 0:NJ].bitcast(BF16).rearrange("p u (j e) -> p u j e", e=2)
-            nc.vector.reciprocal(out=ginv[:].rearrange("p j (u e) -> p u j e", e=2), in_=gaps)
+            nc.vector.reciprocal(out=ginv[:], in_=gap_in[:])
 
-        queue = {"sync": [], "tensor": [], "scalar": [], "vector": []}
-        engine = {"S": "scalar", "V": "vector"}
+        def widen_coul():
+            nc.scalar.copy(out=coul_rows[0:4], in_=coul_in[0:4])
+
+        def turn_coul(banks):
+            tr_vec[0] = bank(banks[0], [128, NG, 128])
+            for g in range(NG):
+                nc.tensor.transpose(tr_vec[0][:, g, :], coul_rows[:, g, :], ident[:])
+
+        def evict_coul():
+            nc.scalar.copy(out=coul_col[:], in_=tr_vec[0][:, :, 0:4])
+
+        queue = {"sync": [], "tensor": [], "scalar": [], "vector": [], "gpsimd": []}
+        engine = {"S": "scalar", "V": "vector", "G": "gpsimd"}
         ring = {"b": [0, 1, 2, 3], "rest": [4, 5, 6, 7]}
-        turn = {"b": 0, "rest": 0}
-        holder = {}
+        turn = {}
+        holder = {"hs_in": [("sort_hs", g) for g in range(NG)]}
+        for g in range(NG):
+            holder[f"h_in{g}"] = [("sort_h", g)]
+            holder[f"h_w{g}"] = [("mul_t", g, 3)]
 
         def step(where, key, needs, fn, *args):
             queue[where].append((key, needs, fn, args))
 
+        def take(kind, place, last_readers):
+            n = turn.get(kind, 0)
+            turn[kind] = n + 1
+            name = place(n)
+            needs = holder.get(name, [])
+            holder[name] = last_readers
+            return name, needs
+
         def tensor_step(kind, key, needs, readers, fn, *args):
             banks = []
             for reader in readers:
-                n = ring[kind][turn[kind] % len(ring[kind])]
-                turn[kind] = turn[kind] + 1
-                if n in holder:
-                    needs = needs + [holder[n]]
-                holder[n] = reader
+                n, freed = take(kind, lambda k: ring[kind][k % len(ring[kind])], [reader])
+                needs = needs + freed
                 banks.append(n)
             step("tensor", key, needs, fn, banks, *args)
+
+        def buffered(where, key, needs, tag, last_readers, fn, *args):
+            name = None
+            if tag is not None:
+                name, freed = take(tag, lambda k: RINGS[tag][k % len(RINGS[tag])], last_readers)
+                needs = needs + freed
+            step(where, key, needs, fn, name, *args)
 
         def emit(done):
             at = {where: 0 for where in queue}
@@ -306,71 +328,74 @@ def tile_rpa_density_step_s12_kernel(tc, d, b, gap, h_words, h_scales, x_words, 
                         fn(*args)
                         done.add(key)
                         at[where] = at[where] + 1
-                assert len(done) > before
+                assert len(done) > before, [queue[w][at[w]][:2] for w in queue if at[w] < len(queue[w])]
 
-        def reuse(name, n, *rest):
-            return [(name, n) + rest] if n >= 0 else []
+        def rows_read(what, n):
+            if what == "d" and n >= FIRST_BLOCK:
+                return [("sort", what, n, 1)]
+            if (what, n) in SORTED:
+                return [("sort", what, n, 0), ("sort", what, n, 1)]
+            return [("turn_b", n, 1)] if what == "b" else [("turn_d", n)]
 
-        def plan_load_b(i):
-            step("sync", ("load_b", i), reuse("turn_b", i - 6, 1), load_b, i)
+        def plan_load(what, n):
+            fn = load_b if what == "b" else load_d if n < FIRST_BLOCK else load_blocks
+            buffered("sync", ("load", what, n), [], "rows", rows_read(what, n), fn, n)
 
-        def plan_load_d(r):
-            step("sync", ("load_d", r), reuse("perm_d", r - 6, 1), load_d if r < FIRST_BLOCK else load_blocks, r)
-
-        def plan_perm_b(i, eng):
+        def plan_sort(what, n, eng):
             for h in range(2):
-                step(engine[eng], ("perm_b", i, h), [("load_b", i), ("turn_b", i - 2, 1)], perm_b, i, h, eng)
+                reader = ("turn_b", n, h) if what == "b" else ("turn_d", n)
+                buffered(engine[eng], ("sort", what, n, h), [("load", what, n)], "sorted" + eng, [reader], sort_rows, what, n, h, eng)
 
-        def plan_turn_b(i, h):
-            tensor_step("b", ("turn_b", i, h), [("perm_b", i, h) if i in SORTED else ("load_b", i)], [("scale_b", i, h)], turn_b, i, h)
+        def ready(what, n, h):
+            return [("sort", what, n, h) if (what, n) in SORTED else ("load", what, n)]
+
+        def plan_turn_b(i, halves=(0, 1)):
+            for h in halves:
+                tensor_step("b", ("turn_b", i, h), ready("b", i, h), [("scale_b", i, h)], turn_b, i, h)
 
         def plan_scale_b(i, h):
-            step("vector", ("scale_b", i, h), [("turn_b", i, h), "ginv"] + reuse("quant_b", i - 3), scale_b, i, h)
+            tag = "b_t" if i % 4 == 0 else None
+            buffered("vector", ("scale_b", i, h), [("turn_b", i, h), "ginv"], tag, [("quant_b", i // 4, h)], scale_b, i, h)
 
-        def plan_quant_b(i):
-            step("vector", ("quant_b", i), [("scale_b", i, 0), ("scale_b", i, 1)], quant_b, i)
-
-        def plan_perm_d(r, eng):
-            for h in range(2):
-                step(engine[eng], ("perm_d", r, h), [("load_d", r)] + reuse("turn_d", r - 3), perm_d, r, h, eng)
+        def plan_quant_b(g, h):
+            step("vector", ("quant_b", g, h), [("scale_b", 4 * g + c, h) for c in range(4)], quant_b, g, h)
 
         def plan_turn_d(r):
-            tensor_step("rest", ("turn_d", r), [("perm_d", r, 0), ("perm_d", r, 1)], [("d_t", r, 0), ("d_t", r, 1)], turn_d, r)
+            tensor_step("rest", ("turn_d", r), ready("d", r, 0) + ready("d", r, 1), [("d_t", r, 0), ("d_t", r, 1)], turn_d, r)
 
-        def plan_evict_d(r):
+        def plan_fill_d(r):
+            fn, need = (evict_d, ("turn_d", r)) if r < FIRST_BLOCK else (weave_blocks, ("turn_blocks", r))
             for h in range(2):
-                step("scalar", ("d_t", r, h), [("turn_d", r)] + reuse("quant_d", r // 2 - 2, h), evict_d, r, h)
+                buffered("scalar", ("d_t", r, h), [need], "d_t" if r % 2 == 0 else None, [("quant_d", r // 2, h)], fn, r, h)
 
-        def plan_perm_blocks(r, eng):
-            freed = ("quant_b", r - 3) if r - 3 < NB else ("turn_blocks", r - 3)
-            step(engine[eng], ("perm_blocks", r), [("load_d", r), freed], perm_blocks, r, eng)
+        def plan_sort_blocks(r, eng):
+            buffered(engine[eng], ("sort", "d", r, 1), [("load", "d", r)], "b_t", [("turn_blocks", r)], sort_blocks, r, eng)
 
         def plan_turn_blocks(r):
-            freed = [("d_t", r - 2, 1)] if r - 2 >= FIRST_BLOCK else []
-            step("vector", ("turn_blocks", r), [("perm_blocks", r)] + freed, turn_blocks, r)
+            buffered("vector", ("turn_blocks", r), [("sort", "d", r, 1)], "d_flip", [("d_t", r, 0), ("d_t", r, 1)], turn_blocks, r)
 
-        def plan_weave_blocks(r):
-            for h in range(2):
-                step("scalar", ("d_t", r, h), [("turn_blocks", r), ("quant_d", r // 2 - 2, h)], weave_blocks, r, h)
-
-        def plan_quant_d(q):
-            for h in range(2):
+        def plan_quant_d(q, halves=(0, 1)):
+            for h in halves:
                 step("vector", ("quant_d", q, h), [("d_t", 2 * q, h), ("d_t", 2 * q + 1, h)], quant_d, q, h)
 
         def plan_trial(g, t):
             tensor_step("rest", ("mul_t", g, t), [("sort_h", g), ("sort_hs", g)], [("scale_t", g, t)], mul_t, g, t)
+
+        def plan_scale_t(g, t):
             step("scalar", ("scale_t", g, t), [("mul_t", g, t), "coul_col"], scale_t, g, t)
 
         def plan_weave_p(g):
-            step("vector", ("weave_p", g), [("scale_t", g, t) for t in range(4)] + reuse("quant_p", g - 1), weave_p, g)
+            buffered("vector", ("weave_p", g), [("scale_t", g, t) for t in range(4)], "pot", [("quant_p", g)], weave_p, g)
 
         def plan_quant_p(g):
             step("vector", ("quant_p", g), [("weave_p", g)], quant_p, g)
 
         def plan_response(q, s):
-            needs = [("quant_b", 2 * s), ("quant_b", 2 * s + 1), ("quant_d", q, 0), ("quant_d", q, 1)]
+            needs = [("quant_b", s // 2, 0), ("quant_b", s // 2, 1), ("quant_d", q, 0), ("quant_d", q, 1)]
             tensor_step("rest", ("mul_c", q, s), needs, [("evict_c", q, s)], mul_c, q, s)
-            step("scalar", ("evict_c", q, s), [("mul_c", q, s)], evict_c, q, s)
+
+        def plan_evict_c(q, s):
+            buffered("scalar", ("evict_c", q, s), [("mul_c", q, s)], "chi" if s % 2 == 0 else None, [("quant_c", q, s // 2)], evict_c, q, s)
 
         def plan_quant_c(q, g):
             step("vector", ("quant_c", q, g), [("evict_c", q, 2 * g), ("evict_c", q, 2 * g + 1)], quant_c, q, g)
@@ -380,141 +405,237 @@ def tile_rpa_density_step_s12_kernel(tc, d, b, gap, h_words, h_scales, x_words, 
             tensor_step("rest", ("mul_o", r), needs, [("evict_o", r)], mul_o, r)
 
         def plan_evict_o(r):
-            step("vector", ("evict_o", r), [("mul_o", r), ("load_n0", r // 4)] + reuse("store", r - 6), evict_o, r)
+            buffered("vector", ("evict_o", r), [("mul_o", r), ("load_n0", r // 4)], "res", [("store", r)], evict_o, r)
 
-        plan_load_b(2)
-        plan_load_d(0)
+        step("sync", "gap", [], load_gap)
+        step("gpsimd", "coul", [], load_coul)
+        plan_load("b", 0)
+        plan_load("b", 1)
+        step("sync", "load_hs", [], load_scales, nc.sync, hs_in, h_scales)
+        step("sync", "load_x", [], load_x)
+        step("sync", ("load_h", 0), [], load_h, 0)
+        step("sync", "load_xs", [], load_scales, nc.sync, x_s[:].bitcast(I32), x_scales)
+        plan_load("b", 2)
+        plan_load("b", 3)
         step("sync", ("load_h", 1), [], load_h, 1)
-        for i in range(3, NB):
-            plan_load_b(i)
-            plan_load_d(i - 2)
-        for r in range(NB - 2, ND):
-            plan_load_d(r)
-        for c in range(ND // 4):
-            step("sync", ("load_n0", c), [("turn_b", 2 + c, 1)], load_n0, c)
+        plan_load("d", 0)
+        plan_load("d", 1)
+        plan_load("b", 4)
+        plan_load("b", 5)
+        plan_load("d", 2)
+        plan_load("d", 3)
+        plan_load("b", 6)
+        plan_load("b", 7)
+        plan_load("d", 4)
+        plan_load("d", 5)
+        plan_load("d", 6)
+        plan_load("d", 7)
+        plan_load("d", 8)
+        plan_load("d", 9)
+        plan_load("d", 10)
+        plan_load("d", 11)
+        buffered("sync", ("load_n0", 0), [], "rows", [("evict_o", 3)], load_n0, 0)
+        buffered("sync", ("load_n0", 1), [], "rows", [("evict_o", 7)], load_n0, 1)
+        buffered("sync", ("load_n0", 2), [], "rows", [("evict_o", 11)], load_n0, 2)
         for r in range(ND):
             step("sync", ("store", r), [("evict_o", r)], store, r)
 
-        trials = [(plan_trial, g, t) for g in range(NG) for t in range(4)]
-        waves = [[(plan_response, q, s) for q in range(s)] + [(plan_response, s, t) for t in range(s + 1)] for s in range(NS)]
-        rounds = [trials[:3], trials[3:6], trials[6:], waves[0]]
-        for wave in waves[1:-1]:
-            rounds = rounds + [wave[: len(wave) // 2], wave[len(wave) // 2 :]]
-        last = len(rounds) - 1
+        plan_turn_b(0)
+        plan_turn_b(1)
+        tensor_step("rest", "turn_coul", ["coul_rows"], ["coul_col"], turn_coul)
+        plan_trial(0, 0)
+        plan_turn_b(2)
+        plan_trial(0, 1)
+        plan_turn_b(3)
+        plan_trial(0, 2)
+        plan_trial(0, 3)
+        plan_trial(1, 0)
+        plan_turn_d(0)
+        plan_turn_b(4)
+        plan_turn_d(1)
+        plan_trial(1, 1)
+        plan_trial(1, 2)
+        plan_trial(1, 3)
+        plan_turn_b(5)
+        plan_turn_d(2)
+        plan_turn_b(6)
+        plan_turn_d(3)
+        plan_response(0, 0)
+        plan_response(0, 1)
+        plan_turn_b(7)
+        plan_turn_d(4)
+        plan_turn_d(5)
+        plan_response(1, 0)
+        ring["rest"] = [0, 1] + [4 + (turn["rest"] + k) % 4 for k in range(4)] + [2, 3]
+        turn["rest"] = 0
+        plan_response(1, 1)
+        plan_turn_d(6)
+        plan_turn_d(7)
+        plan_response(2, 0)
+        plan_response(2, 1)
+        plan_response(3, 0)
+        plan_response(3, 1)
+        plan_response(0, 2)
+        plan_response(0, 3)
+        plan_response(1, 2)
+        plan_response(1, 3)
+        plan_response(2, 2)
+        plan_response(2, 3)
+        plan_response(3, 2)
+        plan_response(3, 3)
+        plan_response(4, 0)
+        plan_induced(0)
+        plan_response(4, 1)
+        plan_induced(1)
+        plan_response(4, 2)
+        plan_induced(2)
+        plan_response(4, 3)
+        plan_induced(3)
+        plan_induced(4)
+        plan_response(5, 0)
+        plan_induced(5)
+        plan_response(5, 1)
+        plan_induced(6)
+        plan_response(5, 2)
+        plan_response(5, 3)
+        plan_induced(7)
+        plan_induced(8)
+        plan_induced(9)
+        plan_induced(10)
+        plan_induced(11)
 
-        plan_turn_b(0, 0)
-        tensor_step("rest", "turn_gap", ["gap_rows"], ["ginv"], turn_gap)
-        plan_turn_b(0, 1)
-        plan_turn_b(1, 0)
-        plan_turn_b(1, 1)
-        plan_perm_b(2, "S")
-        step("scalar", "coul_col", [], widen_coul)
-        plan_perm_d(0, "S")
-        for n, products in enumerate(rounds):
-            tiles = [n - 1] if n > 0 else []
-            if 0 < n < last:
-                plan_turn_b(n + 1, 0)
-                plan_turn_b(n + 1, 1)
-            if n == last:
-                tiles = [n - 1, n]
-                ring["rest"] = [0, 1] + [4 + (turn["rest"] + k) % 4 for k in range(4)] + [2, 3]
-                turn["rest"] = 0
-            for r in tiles:
-                plan_turn_d(r)
-            for r in tiles:
-                plan_evict_d(r)
-            if n == 1:
-                plan_perm_d(1, "S")
-            for plan, u, v in products:
-                plan(u, v)
-            if 0 < n < last - 1:
-                plan_perm_d(n + 1, "S")
-
-        units = waves[-1] + [(plan_response, q, s) for q in range(NS, NQ) for s in range(NS)]
-        before = {(1, 3): [(plan_weave_blocks, 8)], (2, 3): [(plan_weave_blocks, 9)], (3, 2): [(plan_perm_blocks, 10, "S")]}
-        before[4, 0] = [(plan_weave_blocks, 10)]
-        before[4, 2] = [(plan_weave_blocks, 11)]
-        after = {(4, 0): [0], (4, 1): [1], (4, 2): [2], (4, 3): [3, 4, 5, 6], (5, 3): [7, 8, 9, 10, 11]}
-        for plan, q, s in units:
-            for job in before.get((q, s), []):
-                job[0](*job[1:])
-            plan(q, s)
-            for r in after.get((q, s), []):
-                plan_induced(r)
-
-        step("vector", "gap_rows", [], sort_gap)
-        step("vector", ("sort_h", 0), [], sort_h, 0)
-        step("vector", "ginv", ["turn_gap"], invert_gap)
+        step("vector", "ginv", ["gap"], invert_gap)
         plan_scale_b(0, 0)
-        step("vector", ("sort_hs", 0), [], sort_hs, 0)
         plan_scale_b(0, 1)
+        step("vector", ("sort_hs", 0), ["load_hs", "load_x", "load_xs"], sort_hs, 0)
+        step("vector", ("sort_h", 0), [("load_h", 0)], sort_h, 0)
         plan_scale_b(1, 0)
-        plan_quant_b(0)
+        step("vector", ("sort_hs", 1), ["load_hs", "load_x", "load_xs"], sort_hs, 1)
         plan_scale_b(1, 1)
+        plan_scale_b(2, 0)
         step("vector", ("sort_h", 1), [("load_h", 1)], sort_h, 1)
-        step("vector", ("sort_hs", 1), [], sort_hs, 1)
-        plan_quant_b(1)
-        for i in range(2, NB):
-            plan_scale_b(i, 0)
-            if i in (5, 7):
-                plan_quant_d(i // 2 - 1)
-            plan_scale_b(i, 1)
-            if i == 3:
-                plan_quant_d(0)
-            if i + 2 in SORTED:
-                plan_perm_b(i + 2, "V")
-            if i == NB - 2:
-                plan_perm_d(last, "V")
-            plan_quant_b(i)
-
-        plan_perm_blocks(8, "V")
+        plan_scale_b(2, 1)
+        plan_scale_b(3, 0)
+        plan_scale_b(3, 1)
+        plan_quant_b(0, 0)
+        plan_sort("b", 5, "V")
+        plan_quant_b(0, 1)
+        plan_scale_b(4, 0)
+        plan_sort("b", 6, "V")
+        plan_scale_b(4, 1)
+        plan_quant_d(0)
+        plan_scale_b(5, 0)
+        plan_scale_b(5, 1)
+        plan_sort("b", 7, "V")
+        plan_scale_b(6, 0)
+        plan_sort("d", 5, "V")
+        plan_scale_b(6, 1)
+        plan_quant_d(1)
+        plan_sort("d", 7, "V")
+        plan_scale_b(7, 0)
+        plan_scale_b(7, 1)
+        plan_quant_d(2)
+        plan_quant_b(1, 0)
+        plan_sort_blocks(8, "V")
         plan_quant_d(3)
+        plan_quant_b(1, 1)
         plan_turn_blocks(8)
-        plan_perm_blocks(9, "V")
-        plan_quant_c(0, 0)
-        plan_turn_blocks(9)
         plan_weave_p(0)
-        plan_quant_c(1, 0)
+        plan_turn_blocks(9)
         plan_quant_p(0)
-        plan_quant_c(2, 0)
-        plan_weave_p(1)
+        plan_sort_blocks(10, "V")
         plan_quant_d(4)
+        plan_turn_blocks(10)
+        plan_weave_p(1)
+        plan_quant_c(0, 0)
+        plan_turn_blocks(11)
         plan_quant_p(1)
         plan_quant_c(0, 1)
+        plan_quant_c(1, 0)
         plan_quant_c(1, 1)
-        plan_turn_blocks(10)
-        plan_quant_c(2, 1)
-        plan_quant_c(3, 0)
-        plan_perm_blocks(11, "V")
         plan_evict_o(0)
-        plan_turn_blocks(11)
-        plan_quant_c(3, 1)
-        plan_evict_o(1)
-        plan_evict_o(2)
         plan_quant_d(5)
+        plan_quant_c(2, 0)
+        plan_evict_o(1)
+        plan_quant_c(2, 1)
+        plan_evict_o(2)
+        plan_quant_c(3, 0)
         plan_evict_o(3)
-        plan_quant_c(4, 0)
+        plan_quant_c(3, 1)
         plan_evict_o(4)
+        plan_quant_c(4, 0)
         plan_evict_o(5)
         plan_quant_c(4, 1)
         plan_evict_o(6)
         plan_quant_c(5, 0)
         plan_evict_o(7)
+        plan_evict_o(8)
         plan_quant_c(5, 1)
-        for r in range(8, ND):
-            plan_evict_o(r)
+        plan_evict_o(9)
+        plan_evict_o(10)
+        plan_evict_o(11)
+
+        plan_sort("b", 1, "S")
+        step("scalar", "coul_rows", ["coul"], widen_coul)
+        step("scalar", "coul_col", ["turn_coul"], evict_coul)
+        plan_sort("b", 2, "S")
+        plan_sort("b", 3, "S")
+        plan_scale_t(0, 0)
+        plan_scale_t(0, 1)
+        plan_sort("d", 0, "S")
+        plan_sort("d", 1, "S")
+        plan_scale_t(0, 2)
+        plan_scale_t(0, 3)
+        plan_scale_t(1, 0)
+        plan_fill_d(0)
+        plan_sort("d", 2, "S")
+        plan_fill_d(1)
+        plan_scale_t(1, 1)
+        plan_sort("d", 3, "S")
+        plan_scale_t(1, 2)
+        plan_scale_t(1, 3)
+        plan_fill_d(2)
+        plan_sort("d", 4, "S")
+        plan_fill_d(3)
+        plan_evict_c(0, 0)
+        plan_evict_c(0, 1)
+        plan_fill_d(4)
+        plan_sort("d", 6, "S")
+        plan_fill_d(5)
+        plan_evict_c(1, 0)
+        plan_evict_c(1, 1)
+        plan_fill_d(6)
+        plan_fill_d(7)
+        plan_evict_c(2, 0)
+        plan_sort_blocks(9, "S")
+        plan_evict_c(2, 1)
+        plan_evict_c(3, 0)
+        plan_fill_d(8)
+        plan_evict_c(3, 1)
+        plan_fill_d(9)
+        plan_evict_c(0, 2)
+        plan_sort_blocks(11, "S")
+        plan_evict_c(0, 3)
+        plan_evict_c(1, 2)
+        plan_fill_d(10)
+        plan_evict_c(1, 3)
+        plan_evict_c(2, 2)
+        plan_fill_d(11)
+        plan_evict_c(2, 3)
+        plan_evict_c(3, 2)
+        plan_evict_c(3, 3)
+        plan_evict_c(4, 0)
+        plan_evict_c(4, 1)
+        plan_evict_c(4, 2)
+        plan_evict_c(4, 3)
+        plan_evict_c(5, 0)
+        plan_evict_c(5, 1)
+        plan_evict_c(5, 2)
+        plan_evict_c(5, 3)
 
         with tc.manual_schedule():
-            nc.scalar.dma_start(out=gap_in[0:NJ, :], in_=gap.rearrange("(j k) -> j k", k=512))
-            load_b(0)
-            load_h(0)
-            load_b(1)
             nc.vector.memset(hs_in[:], 0)
             nc.vector.memset(x_s[:].rearrange("p j n -> p (j n)").bitcast(I32), 0)
-            nc.vector.memset(gap_rows[:], 0.0)
+            nc.vector.memset(coul_rows[:], 0.0)
             make_identity(nc, ident[:])
-            nc.gpsimd.dma_start(out=coul_in[:], in_=coul.rearrange("(g p t) -> p g t", p=128, t=4))
-            load_scales(hs_in, h_scales)
-            load_x()
-            load_scales(x_s[:].bitcast(I32), x_scales)
-            emit({("load_b", 0), ("load_b", 1)})
+            emit(set())

@@ -25,10 +25,10 @@ NS = NB // 2
 ND = R // 128
 NQ = ND // 2
 FIRST_BLOCK = 8
-SORTED = {("b", 5), ("b", 6), ("b", 7), ("d", 5), ("d", 7), ("b", 1), ("b", 2), ("b", 3), ("d", 0), ("d", 1), ("d", 2), ("d", 3), ("d", 4), ("d", 6)}
-DEPTH = {"rows": 11, "sortedS": 4, "sortedV": 4, "sortedG": 2, "b_t": 3, "d_t": 6, "d_flip": 2, "pot": 1, "chi": 8, "res": 2}
+SORTED = {("b", 6), ("b", 7), ("b", 1), ("b", 2), ("b", 3), ("d", 0), ("d", 2), ("d", 4), ("d", 6)}
+DEPTH = {"rows": 9, "sortedS": 3, "sortedV": 2, "b_t": 3, "d_t": 3, "res": 3, "chi": 5}
 OWN = {tag: [f"{tag}{k}" for k in range(n)] for tag, n in DEPTH.items()}
-RINGS = {**OWN, "res": OWN["sortedV"] + OWN["res"], "d_flip": ["h_in0", "h_in1"], "pot": ["hs_in"], "chi": OWN["chi"] + ["h_w0", "h_w1"]}
+RINGS = {**OWN, "res": OWN["sortedV"] + OWN["res"], "d_flip": ["h_in0", "h_in1"], "pot": ["hs_in"], "chi": OWN["chi"] + ["h_w0"]}
 
 
 def tile_rpa_density_step_s12_kernel(tc, d, b, gap, h_words, h_scales, x_words, x_scales, coul, n0, out):
@@ -51,13 +51,13 @@ def tile_rpa_density_step_s12_kernel(tc, d, b, gap, h_words, h_scales, x_words, 
         h_s = [keep.tile([128, NF, 4, 128], U8, name=f"h_s{g}", align_bytes=64) for g in range(NG)]
         bcodes = [[keep.tile([128, 2, 4, 128], U32, name=f"bcodes{g}_{h}", align_bytes=64) for h in range(2)] for g in range(NG)]
         bscale = [[keep.tile([128, 2, 4, 128], U8, name=f"bscale{g}_{h}", align_bytes=64) for h in range(2)] for g in range(NG)]
-        dcodes = [[keep.tile([128, 2, 256], U32, name=f"dcodes{q}_{h}", align_bytes=64) for h in range(2)] for q in range(NQ)]
-        dscale = [[keep.tile([128, 2, 256], U8, name=f"dscale{q}_{h}", align_bytes=64) for h in range(2)] for q in range(NQ)]
+        dcodes = [keep.tile([128, NJ, 256], U32, name=f"dcodes{q}", align_bytes=64) for q in range(NQ)]
+        dscale = [keep.tile([128, NJ, 256], U8, name=f"dscale{q}", align_bytes=64) for q in range(NQ)]
         pot_s = [keep.tile([128, 4, P], BF16, name=f"pot_s{g}") for g in range(NG)]
         pcodes = [keep.tile([128, P], U32, name=f"pcodes{g}", align_bytes=64) for g in range(NG)]
         pscale = [keep.tile([128, P], U8, name=f"pscale{g}", align_bytes=64) for g in range(NG)]
-        ccodes = [[keep.tile([128, 256], U32, name=f"ccodes{q}_{g}", align_bytes=64) for g in range(NG)] for q in range(NQ)]
-        cscale = [[keep.tile([128, 256], U8, name=f"cscale{q}_{g}", align_bytes=64) for g in range(NG)] for q in range(NQ)]
+        ccodes = [keep.tile([128, NG, 256], U32, name=f"ccodes{q}", align_bytes=64) for q in range(NQ)]
+        cscale = [keep.tile([128, NG, 256], U8, name=f"cscale{q}", align_bytes=64) for q in range(NQ)]
 
         b_sb, d_sb, n0_sb, perm, b_t, d_t, pot, chi = {}, {}, {}, {}, {}, {}, {}, {}
         tr_vec, tr_b, tr_d, ps_c, ps_o, ps_t, res, d_flip = {}, {}, {}, {}, {}, {}, {}, {}
@@ -71,12 +71,19 @@ def tile_rpa_density_step_s12_kernel(tc, d, b, gap, h_words, h_scales, x_words, 
         def copy(eng, dst, src):
             if eng == "S":
                 nc.scalar.copy(out=dst, in_=src)
+            elif eng == "G":
+                nc.gpsimd.tensor_copy(out=dst, in_=src)
             else:
                 nc.vector.tensor_copy(out=dst, in_=src)
 
-        def sort_pairs(eng, dst, tile, h):
-            pairs = tile[:].bitcast(F32)[:, 512 * h : 512 * (h + 1)]
-            copy(eng, dst[:].rearrange("p u (c i) -> p c u i", i=4), pairs.rearrange("p (c i u) -> p c u i", u=2, i=4))
+        def sort_pairs(eng, dst, tile, first, count):
+            word = I32 if eng == "G" else F32
+            pairs = tile[:].bitcast(word)[:, 512 * first : 512 * (first + count)]
+            copy(
+                eng,
+                dst[:, first : first + count].bitcast(word).rearrange("p h u (c i) -> p h c u i", i=4),
+                pairs.rearrange("p (h c i u) -> p h c u i", h=count, u=2, i=4),
+            )
 
         def load_b(name, i):
             b_sb[i] = buf(name, [128, T], BF16)
@@ -100,13 +107,14 @@ def tile_rpa_density_step_s12_kernel(tc, d, b, gap, h_words, h_scales, x_words, 
             for r in range(4):
                 eng.dma_start(out=plane[r:128:32], in_=scales.bitcast(I32)[:, r:16:4, :].rearrange("j Q n -> Q j n"))
 
-        def sort_rows(name, what, n, h, eng):
-            perm[what, n, h] = buf(name, [128, 2, T // 8], F32)
-            sort_pairs(eng, perm[what, n, h], (b_sb if what == "b" else d_sb)[n], h)
+        def sort_rows(name, what, n, first, count, eng):
+            if first == 0:
+                perm[what, n] = buf(name, [128, 2, 2, T // 8], F32)
+            sort_pairs(eng, perm[what, n], (b_sb if what == "b" else d_sb)[n], first, count)
 
         def pairs_of(what, n, h, jj, u):
-            if (what, n, h) in perm:
-                return perm[what, n, h][:, u, 128 * jj : 128 * (jj + 1)]
+            if (what, n) in perm:
+                return perm[what, n][:, h, u, 128 * jj : 128 * (jj + 1)]
             return (b_sb if what == "b" else d_sb)[n][:].bitcast(F32)[:, 512 * h + 256 * jj + u : 512 * h + 256 * (jj + 1) : 2]
 
         def turn_b(banks, i, h):
@@ -178,9 +186,9 @@ def tile_rpa_density_step_s12_kernel(tc, d, b, gap, h_words, h_scales, x_words, 
 
         def evict_d(name, r, h):
             q = r // 2
-            if r % 2 == 0:
-                d_t[q, h] = buf(name, [128, 2, 256, 2], F32)
-            nc.scalar.copy(out=d_t[q, h][:, :, 128 * (r % 2) : 128 * (r % 2) + 128, :], in_=tr_d[r, h][:].rearrange("p j u a -> p j a u"))
+            if r % 2 == 0 and h == 0:
+                d_t[q] = buf(name, [128, NJ, 256, 2], F32)
+            nc.scalar.copy(out=d_t[q][:, 2 * h : 2 * h + 2, 128 * (r % 2) : 128 * (r % 2) + 128, :], in_=tr_d[r, h][:].rearrange("p j u a -> p j a u"))
 
         def load_blocks(name, r):
             d_sb[r] = buf(name, [128, 4, NJ, 128], BF16)
@@ -189,31 +197,35 @@ def tile_rpa_density_step_s12_kernel(tc, d, b, gap, h_words, h_scales, x_words, 
                 nc.sync.dma_start(out=d_sb[r][32 * s : 32 * (s + 1)], in_=src[s, :, 4 * (r % 2) : 4 * (r % 2) + 4])
 
         def sort_blocks(name, r, eng):
+            word = I32 if eng == "G" else F32
             perm["blocks", r] = buf(name, [128, 16, 2, 32], F32)
             copy(
                 eng,
-                perm["blocks", r][:].rearrange("p n u (a i) -> p n a u i", i=4),
-                d_sb[r][:].rearrange("p c j k -> p (c j k)").bitcast(F32).rearrange("p (n a i u) -> p n a u i", n=16, i=4, u=2),
+                perm["blocks", r][:].bitcast(word).rearrange("p n u (a i) -> p n a u i", i=4),
+                d_sb[r][:].rearrange("p c j k -> p (c j k)").bitcast(word).rearrange("p (n a i u) -> p n a u i", n=16, i=4, u=2),
             )
 
         def turn_blocks(name, r):
             d_flip[r] = buf(name, [128, 4, NJ, 2, 32], F32)
             nc.vector.transpose(out=d_flip[r][:].rearrange("p c j u i -> p (c j u i)"), in_=perm["blocks", r][:].rearrange("p n u w -> p (n u w)"))
 
-        def weave_blocks(name, r, h):
+        def weave_blocks(name, r, eng):
             q = r // 2
             if r % 2 == 0:
-                d_t[q, h] = buf(name, [128, 2, 256, 2], F32)
-            nc.scalar.copy(
-                out=d_t[q, h][:, :, 128 * (r % 2) : 128 * (r % 2) + 128, :].rearrange("p j (c i) u -> p j c i u", i=32),
-                in_=d_flip[r][:, :, 2 * h : 2 * h + 2].rearrange("p c j u i -> p j c i u"),
+                d_t[q] = buf(name, [128, NJ, 256, 2], F32)
+            word = I32 if eng == "G" else F32
+            copy(
+                eng,
+                d_t[q][:].bitcast(word)[:, :, 128 * (r % 2) : 128 * (r % 2) + 128, :].rearrange("p j (c i) u -> p j c i u", i=32),
+                d_flip[r][:].bitcast(word).rearrange("p c j u i -> p j c i u"),
             )
 
-        def quant_d(q, h):
+        def quant_d(q, first, count):
+            js = slice(2 * first, 2 * (first + count))
             nc.vector.quantize_mx(
-                out=dcodes[q][h][:].rearrange("p j a -> p (j a)").bitcast(FP8X4),
-                scales=dscale[q][h][:].rearrange("p j a -> p (j a)"),
-                in_=d_t[q, h][:].rearrange("p j a u -> p (j a u)").bitcast(BF16),
+                out=dcodes[q][:, js].rearrange("p j a -> p (j a)").bitcast(FP8X4),
+                scales=dscale[q][:, js].rearrange("p j a -> p (j a)"),
+                in_=d_t[q][:, js].rearrange("p j a u -> p (j a u)").bitcast(BF16),
             )
 
         def mul_c(banks, q, s):
@@ -225,21 +237,26 @@ def tile_rpa_density_step_s12_kernel(tc, d, b, gap, h_words, h_scales, x_words, 
                         out=ps_c[q, s][:, e, :],
                         lhsT=bcodes[g][j // 2][:, j % 2, t, :].bitcast(FP8X4),
                         lhsT_scale=bscale[g][j // 2][:, j % 2, t, :],
-                        rhs=dcodes[q][j // 2][:, j % 2, :].bitcast(FP8X4),
-                        rhs_scale=dscale[q][j // 2][:, j % 2, :],
+                        rhs=dcodes[q][:, j, :].bitcast(FP8X4),
+                        rhs_scale=dscale[q][:, j, :],
                         start=(j == 0),
                         stop=(j == NJ - 1),
                     )
 
         def evict_c(name, q, s):
             g, tp = s // 2, s % 2
-            if tp == 0:
-                chi[q, g] = buf(name, [128, 256, 4], BF16)
+            if s == 0:
+                chi[q] = buf(name, [128, NG, 256, 4], BF16)
             order = "p e (c i) -> p i c e" if 2 * q >= FIRST_BLOCK else "p e (i c) -> p i c e"
-            nc.scalar.copy(out=chi[q, g][:, :, 2 * tp : 2 * tp + 2].rearrange("p (i c) e -> p i c e", c=8), in_=ps_c[q, s][:].rearrange(order, c=8))
+            nc.scalar.copy(out=chi[q][:, g, :, 2 * tp : 2 * tp + 2].rearrange("p (i c) e -> p i c e", c=8), in_=ps_c[q, s][:].rearrange(order, c=8))
 
-        def quant_c(q, g):
-            nc.vector.quantize_mx(out=ccodes[q][g][:].bitcast(FP8X4), scales=cscale[q][g][:], in_=chi[q, g][:].rearrange("p a t -> p (a t)"))
+        def quant_c(q, first, count):
+            gs = slice(first, first + count)
+            nc.vector.quantize_mx(
+                out=ccodes[q][:, gs].rearrange("p g a -> p (g a)").bitcast(FP8X4),
+                scales=cscale[q][:, gs].rearrange("p g a -> p (g a)"),
+                in_=chi[q][:, gs].rearrange("p g a t -> p (g a t)"),
+            )
 
         def mul_o(banks, r):
             q = r // 2
@@ -248,8 +265,8 @@ def tile_rpa_density_step_s12_kernel(tc, d, b, gap, h_words, h_scales, x_words, 
             for g in range(NG):
                 nc.tensor.matmul_mx(
                     out=ps_o[r][:],
-                    lhsT=ccodes[q][g][:, cols].bitcast(FP8X4),
-                    lhsT_scale=cscale[q][g][:, cols],
+                    lhsT=ccodes[q][:, g, cols].bitcast(FP8X4),
+                    lhsT_scale=cscale[q][:, g, cols],
                     rhs=pcodes[g][:].bitcast(FP8X4),
                     rhs_scale=pscale[g][:],
                     start=(g == 0),
@@ -326,7 +343,8 @@ def tile_rpa_density_step_s12_kernel(tc, d, b, gap, h_words, h_scales, x_words, 
                     while at[where] < len(queue[where]) and all(n in done for n in queue[where][at[where]][1]):
                         key, needs, fn, args = queue[where][at[where]]
                         fn(*args)
-                        done.add(key)
+                        for name in key if isinstance(key, list) else [key]:
+                            done.add(name)
                         at[where] = at[where] + 1
                 assert len(done) > before, [queue[w][at[w]][:2] for w in queue if at[w] < len(queue[w])]
 
@@ -341,10 +359,11 @@ def tile_rpa_density_step_s12_kernel(tc, d, b, gap, h_words, h_scales, x_words, 
             fn = load_b if what == "b" else load_d if n < FIRST_BLOCK else load_blocks
             buffered("sync", ("load", what, n), [], "rows", rows_read(what, n), fn, n)
 
-        def plan_sort(what, n, eng):
-            for h in range(2):
-                reader = ("turn_b", n, h) if what == "b" else ("turn_d", n)
-                buffered(engine[eng], ("sort", what, n, h), [("load", what, n)], "sorted" + eng, [reader], sort_rows, what, n, h, eng)
+        def plan_sort(what, n, eng, pieces=((0, 2),)):
+            readers = [("turn_b", n, 1)] if what == "b" else [("turn_d", n)]
+            for first, count in pieces:
+                keys = [("sort", what, n, h) for h in range(first, first + count)]
+                buffered(engine[eng], keys, [("load", what, n)], "sorted" + eng if first == 0 else None, readers, sort_rows, what, n, first, count, eng)
 
         def ready(what, n, h):
             return [("sort", what, n, h) if (what, n) in SORTED else ("load", what, n)]
@@ -364,19 +383,24 @@ def tile_rpa_density_step_s12_kernel(tc, d, b, gap, h_words, h_scales, x_words, 
             tensor_step("rest", ("turn_d", r), ready("d", r, 0) + ready("d", r, 1), [("d_t", r, 0), ("d_t", r, 1)], turn_d, r)
 
         def plan_fill_d(r):
-            fn, need = (evict_d, ("turn_d", r)) if r < FIRST_BLOCK else (weave_blocks, ("turn_blocks", r))
             for h in range(2):
-                buffered("scalar", ("d_t", r, h), [need], "d_t" if r % 2 == 0 else None, [("quant_d", r // 2, h)], fn, r, h)
+                tag = "d_t" if r % 2 == 0 and h == 0 else None
+                buffered("scalar", ("d_t", r, h), [("turn_d", r)], tag, [("quant_d", r // 2, 0), ("quant_d", r // 2, 1)], evict_d, r, h)
+
+        def plan_weave_blocks(r, eng):
+            needs = [("turn_blocks", r)] + ([("d_t", r - 1, 0)] if r % 2 else [])
+            tag = ("d_t" if eng == "S" else "b_t") if r % 2 == 0 else None
+            buffered(engine[eng], [("d_t", r, 0), ("d_t", r, 1)], needs, tag, [("quant_d", r // 2, 0), ("quant_d", r // 2, 1)], weave_blocks, r, eng)
 
         def plan_sort_blocks(r, eng):
-            buffered(engine[eng], ("sort", "d", r, 1), [("load", "d", r)], "b_t", [("turn_blocks", r)], sort_blocks, r, eng)
+            buffered(engine[eng], ("sort", "d", r, 1), [("load", "d", r)], "sorted" + eng, [("turn_blocks", r)], sort_blocks, r, eng)
 
         def plan_turn_blocks(r):
             buffered("vector", ("turn_blocks", r), [("sort", "d", r, 1)], "d_flip", [("d_t", r, 0), ("d_t", r, 1)], turn_blocks, r)
 
-        def plan_quant_d(q, halves=(0, 1)):
-            for h in halves:
-                step("vector", ("quant_d", q, h), [("d_t", 2 * q, h), ("d_t", 2 * q + 1, h)], quant_d, q, h)
+        def plan_quant_d(q, first=0, count=2):
+            halves = range(first, first + count)
+            step("vector", [("quant_d", q, h) for h in halves], [("d_t", 2 * q + e, h) for e in range(2) for h in halves], quant_d, q, first, count)
 
         def plan_trial(g, t):
             tensor_step("rest", ("mul_t", g, t), [("sort_h", g), ("sort_hs", g)], [("scale_t", g, t)], mul_t, g, t)
@@ -395,10 +419,11 @@ def tile_rpa_density_step_s12_kernel(tc, d, b, gap, h_words, h_scales, x_words, 
             tensor_step("rest", ("mul_c", q, s), needs, [("evict_c", q, s)], mul_c, q, s)
 
         def plan_evict_c(q, s):
-            buffered("scalar", ("evict_c", q, s), [("mul_c", q, s)], "chi" if s % 2 == 0 else None, [("quant_c", q, s // 2)], evict_c, q, s)
+            buffered("scalar", ("evict_c", q, s), [("mul_c", q, s)], "chi" if s == 0 else None, [("quant_c", q, 0), ("quant_c", q, 1)], evict_c, q, s)
 
-        def plan_quant_c(q, g):
-            step("vector", ("quant_c", q, g), [("evict_c", q, 2 * g), ("evict_c", q, 2 * g + 1)], quant_c, q, g)
+        def plan_quant_c(q, first=0, count=NG):
+            groups = range(first, first + count)
+            step("vector", [("quant_c", q, g) for g in groups], [("evict_c", q, 2 * g + e) for g in groups for e in range(2)], quant_c, q, first, count)
 
         def plan_induced(r):
             needs = [("quant_c", r // 2, 0), ("quant_c", r // 2, 1), ("quant_p", 0), ("quant_p", 1)]
@@ -471,32 +496,32 @@ def tile_rpa_density_step_s12_kernel(tc, d, b, gap, h_words, h_scales, x_words, 
         plan_response(1, 1)
         plan_turn_d(6)
         plan_turn_d(7)
-        plan_response(2, 0)
-        plan_response(2, 1)
-        plan_response(3, 0)
-        plan_response(3, 1)
         plan_response(0, 2)
         plan_response(0, 3)
+        plan_response(2, 0)
+        plan_response(2, 1)
         plan_response(1, 2)
         plan_response(1, 3)
         plan_response(2, 2)
         plan_response(2, 3)
+        plan_response(3, 0)
+        plan_response(3, 1)
         plan_response(3, 2)
         plan_response(3, 3)
         plan_response(4, 0)
-        plan_induced(0)
         plan_response(4, 1)
-        plan_induced(1)
         plan_response(4, 2)
-        plan_induced(2)
+        plan_induced(0)
         plan_response(4, 3)
+        plan_induced(1)
+        plan_induced(2)
+        plan_response(5, 0)
         plan_induced(3)
         plan_induced(4)
-        plan_response(5, 0)
-        plan_induced(5)
         plan_response(5, 1)
-        plan_induced(6)
+        plan_induced(5)
         plan_response(5, 2)
+        plan_induced(6)
         plan_response(5, 3)
         plan_induced(7)
         plan_induced(8)
@@ -518,7 +543,6 @@ def tile_rpa_density_step_s12_kernel(tc, d, b, gap, h_words, h_scales, x_words, 
         plan_scale_b(3, 0)
         plan_scale_b(3, 1)
         plan_quant_b(0, 0)
-        plan_sort("b", 5, "V")
         plan_quant_b(0, 1)
         plan_scale_b(4, 0)
         plan_sort("b", 6, "V")
@@ -526,64 +550,59 @@ def tile_rpa_density_step_s12_kernel(tc, d, b, gap, h_words, h_scales, x_words, 
         plan_quant_d(0)
         plan_scale_b(5, 0)
         plan_scale_b(5, 1)
-        plan_sort("b", 7, "V")
         plan_scale_b(6, 0)
-        plan_sort("d", 5, "V")
+        plan_sort("b", 7, "V")
         plan_scale_b(6, 1)
         plan_quant_d(1)
-        plan_sort("d", 7, "V")
         plan_scale_b(7, 0)
         plan_scale_b(7, 1)
-        plan_quant_d(2)
         plan_quant_b(1, 0)
-        plan_sort_blocks(8, "V")
-        plan_quant_d(3)
         plan_quant_b(1, 1)
-        plan_turn_blocks(8)
+        plan_quant_d(2)
+        plan_sort_blocks(8, "V")
         plan_weave_p(0)
+        plan_turn_blocks(8)
+        plan_quant_d(3)
         plan_turn_blocks(9)
         plan_quant_p(0)
         plan_sort_blocks(10, "V")
-        plan_quant_d(4)
-        plan_turn_blocks(10)
         plan_weave_p(1)
-        plan_quant_c(0, 0)
-        plan_turn_blocks(11)
+        plan_turn_blocks(10)
+        plan_quant_d(4)
+        plan_sort_blocks(11, "V")
         plan_quant_p(1)
-        plan_quant_c(0, 1)
-        plan_quant_c(1, 0)
-        plan_quant_c(1, 1)
-        plan_evict_o(0)
+        plan_turn_blocks(11)
+        plan_weave_blocks(10, "V")
+        plan_quant_c(0)
+        plan_weave_blocks(11, "V")
+        plan_quant_c(1)
         plan_quant_d(5)
-        plan_quant_c(2, 0)
+        plan_evict_o(0)
+        plan_quant_c(2)
         plan_evict_o(1)
-        plan_quant_c(2, 1)
         plan_evict_o(2)
-        plan_quant_c(3, 0)
+        plan_quant_c(3)
         plan_evict_o(3)
-        plan_quant_c(3, 1)
         plan_evict_o(4)
-        plan_quant_c(4, 0)
+        plan_quant_c(4)
         plan_evict_o(5)
-        plan_quant_c(4, 1)
         plan_evict_o(6)
-        plan_quant_c(5, 0)
+        plan_quant_c(5, 0, 1)
         plan_evict_o(7)
         plan_evict_o(8)
-        plan_quant_c(5, 1)
+        plan_quant_c(5, 1, 1)
         plan_evict_o(9)
         plan_evict_o(10)
         plan_evict_o(11)
 
-        plan_sort("b", 1, "S")
+        plan_sort("b", 1, "S", ((0, 1), (1, 1)))
         step("scalar", "coul_rows", ["coul"], widen_coul)
         step("scalar", "coul_col", ["turn_coul"], evict_coul)
-        plan_sort("b", 2, "S")
+        plan_sort("b", 2, "S", ((0, 1), (1, 1)))
         plan_sort("b", 3, "S")
         plan_scale_t(0, 0)
         plan_scale_t(0, 1)
         plan_sort("d", 0, "S")
-        plan_sort("d", 1, "S")
         plan_scale_t(0, 2)
         plan_scale_t(0, 3)
         plan_scale_t(1, 0)
@@ -591,11 +610,10 @@ def tile_rpa_density_step_s12_kernel(tc, d, b, gap, h_words, h_scales, x_words, 
         plan_sort("d", 2, "S")
         plan_fill_d(1)
         plan_scale_t(1, 1)
-        plan_sort("d", 3, "S")
         plan_scale_t(1, 2)
         plan_scale_t(1, 3)
-        plan_fill_d(2)
         plan_sort("d", 4, "S")
+        plan_fill_d(2)
         plan_fill_d(3)
         plan_evict_c(0, 0)
         plan_evict_c(0, 1)
@@ -606,22 +624,19 @@ def tile_rpa_density_step_s12_kernel(tc, d, b, gap, h_words, h_scales, x_words, 
         plan_evict_c(1, 1)
         plan_fill_d(6)
         plan_fill_d(7)
-        plan_evict_c(2, 0)
         plan_sort_blocks(9, "S")
-        plan_evict_c(2, 1)
-        plan_evict_c(3, 0)
-        plan_fill_d(8)
-        plan_evict_c(3, 1)
-        plan_fill_d(9)
         plan_evict_c(0, 2)
-        plan_sort_blocks(11, "S")
+        plan_weave_blocks(8, "S")
         plan_evict_c(0, 3)
+        plan_evict_c(2, 0)
+        plan_weave_blocks(9, "S")
+        plan_evict_c(2, 1)
         plan_evict_c(1, 2)
-        plan_fill_d(10)
         plan_evict_c(1, 3)
         plan_evict_c(2, 2)
-        plan_fill_d(11)
         plan_evict_c(2, 3)
+        plan_evict_c(3, 0)
+        plan_evict_c(3, 1)
         plan_evict_c(3, 2)
         plan_evict_c(3, 3)
         plan_evict_c(4, 0)

@@ -24,11 +24,11 @@ NB = A // 128
 NS = NB // 2
 ND = R // 128
 NQ = ND // 2
-FIRST_BLOCK = 8
-SORTED = {("b", 6), ("b", 7), ("b", 1), ("b", 2), ("b", 3), ("d", 0), ("d", 2), ("d", 4), ("d", 6)}
+FIRST_BLOCK = 6
+SORTED = {("b", 6), ("b", 7), ("b", 1), ("b", 2), ("b", 3), ("d", 0), ("d", 1), ("d", 2), ("d", 3), ("d", 4)}
 DEPTH = {"rows": 9, "sortedS": 3, "sortedV": 2, "b_t": 3, "d_t": 3, "res": 3, "chi": 5}
 OWN = {tag: [f"{tag}{k}" for k in range(n)] for tag, n in DEPTH.items()}
-RINGS = {**OWN, "res": OWN["sortedV"] + OWN["res"], "d_flip": ["h_in0", "h_in1"], "pot": ["hs_in"], "chi": OWN["chi"] + ["h_w0"]}
+RINGS = {**OWN, "res": OWN["sortedV"] + OWN["res"], "d_flip": ["h_in0", "h_in1"], "pot": ["hs_in"], "chi": OWN["chi"] + ["h_w0"], "first": OWN["res"][:2]}
 
 
 def tile_rpa_density_step_s12_kernel(tc, d, b, gap, h_words, h_scales, x_words, x_scales, coul, n0, out):
@@ -60,7 +60,7 @@ def tile_rpa_density_step_s12_kernel(tc, d, b, gap, h_words, h_scales, x_words, 
         cscale = [keep.tile([128, NG, 256], U8, name=f"cscale{q}", align_bytes=64) for q in range(NQ)]
 
         b_sb, d_sb, n0_sb, perm, b_t, d_t, pot, chi = {}, {}, {}, {}, {}, {}, {}, {}
-        tr_vec, tr_b, tr_d, ps_c, ps_o, ps_t, res, d_flip = {}, {}, {}, {}, {}, {}, {}, {}
+        tr_vec, tr_b, tr_d, ps_c, ps_o, ps_t, res, d_flip, halves = {}, {}, {}, {}, {}, {}, {}, {}, {}
 
         def buf(name, shape, dtype):
             return keep.tile(shape, dtype, name=name, align_bytes=64)
@@ -89,6 +89,10 @@ def tile_rpa_density_step_s12_kernel(tc, d, b, gap, h_words, h_scales, x_words, 
             b_sb[i] = buf(name, [128, T], BF16)
             nc.sync.dma_start(out=b_sb[i][:], in_=b[i * 128 : (i + 1) * 128, :])
 
+        def load_half(name, h):
+            halves[h] = buf(name, [128, T // 2], BF16)
+            nc.sync.dma_start(out=halves[h][:], in_=b[0:128, 1024 * h : 1024 * (h + 1)])
+
         def load_d(name, r):
             d_sb[r] = buf(name, [128, T], BF16)
             nc.sync.dma_start(out=d_sb[r][:], in_=d[r * 128 : (r + 1) * 128, :])
@@ -113,6 +117,8 @@ def tile_rpa_density_step_s12_kernel(tc, d, b, gap, h_words, h_scales, x_words, 
             sort_pairs(eng, perm[what, n], (b_sb if what == "b" else d_sb)[n], first, count)
 
         def pairs_of(what, n, h, jj, u):
+            if (what, n) == ("b", 0):
+                return halves[h][:].bitcast(F32)[:, 256 * jj + u : 256 * (jj + 1) : 2]
             if (what, n) in perm:
                 return perm[what, n][:, h, u, 128 * jj : 128 * (jj + 1)]
             return (b_sb if what == "b" else d_sb)[n][:].bitcast(F32)[:, 512 * h + 256 * jj + u : 512 * h + 256 * (jj + 1) : 2]
@@ -243,19 +249,21 @@ def tile_rpa_density_step_s12_kernel(tc, d, b, gap, h_words, h_scales, x_words, 
                         stop=(j == NJ - 1),
                     )
 
-        def evict_c(name, q, s):
+        def evict_c(name, q, s, first, count):
             g, tp = s // 2, s % 2
-            if s == 0:
+            if name is not None:
                 chi[q] = buf(name, [128, NG, 256, 4], BF16)
             order = "p e (c i) -> p i c e" if 2 * q >= FIRST_BLOCK else "p e (i c) -> p i c e"
-            nc.scalar.copy(out=chi[q][:, g, :, 2 * tp : 2 * tp + 2].rearrange("p (i c) e -> p i c e", c=8), in_=ps_c[q, s][:].rearrange(order, c=8))
+            rows = slice(16 * first, 16 * (first + count))
+            words = chi[q][:, g, :, 2 * tp : 2 * tp + 2].rearrange("p (i c) e -> p i c e", c=8)
+            nc.scalar.copy(out=words[:, rows], in_=ps_c[q, s][:].rearrange(order, c=8)[:, rows])
 
         def quant_c(q, first, count):
-            gs = slice(first, first + count)
+            cols = slice(128 * first, 128 * (first + count))
             nc.vector.quantize_mx(
-                out=ccodes[q][:, gs].rearrange("p g a -> p (g a)").bitcast(FP8X4),
-                scales=cscale[q][:, gs].rearrange("p g a -> p (g a)"),
-                in_=chi[q][:, gs].rearrange("p g a t -> p (g a t)"),
+                out=ccodes[q][:].rearrange("p g a -> p (g a)")[:, cols].bitcast(FP8X4),
+                scales=cscale[q][:].rearrange("p g a -> p (g a)")[:, cols],
+                in_=chi[q][:].rearrange("p g a t -> p (g a) t")[:, cols].rearrange("p a t -> p (a t)"),
             )
 
         def mul_o(banks, r):
@@ -273,12 +281,15 @@ def tile_rpa_density_step_s12_kernel(tc, d, b, gap, h_words, h_scales, x_words, 
                     stop=(g == NG - 1),
                 )
 
-        def evict_o(name, r):
-            res[r] = buf(name, [128, P], F32)
-            nc.vector.tensor_tensor(out=res[r][:], in0=n0_sb[r // 4][:, r % 4, :], in1=ps_o[r][:], op=ALU.subtract)
+        def evict_o(name, r, first, count):
+            if name is not None:
+                res[r] = buf(name, [128, P], F32)
+            cols = slice(256 * first, 256 * (first + count))
+            nc.vector.tensor_tensor(out=res[r][:, cols], in0=n0_sb[r // 4][:, r % 4, cols], in1=ps_o[r][:, cols], op=ALU.subtract)
 
-        def store(r):
-            nc.sync.dma_start(out=out[r * 128 : (r + 1) * 128, :], in_=res[r][:])
+        def store(r, first, count):
+            cols = slice(256 * first, 256 * (first + count))
+            nc.sync.dma_start(out=out[r * 128 : (r + 1) * 128, cols], in_=res[r][:, cols])
 
         def load_gap():
             nc.scalar.dma_start(out=gap_in[:], in_=gap.rearrange("(j p t) -> p j t", p=128, t=4))
@@ -366,6 +377,8 @@ def tile_rpa_density_step_s12_kernel(tc, d, b, gap, h_words, h_scales, x_words, 
                 buffered(engine[eng], keys, [("load", what, n)], "sorted" + eng if first == 0 else None, readers, sort_rows, what, n, first, count, eng)
 
         def ready(what, n, h):
+            if (what, n) == ("b", 0):
+                return [("load_half", h)]
             return [("sort", what, n, h) if (what, n) in SORTED else ("load", what, n)]
 
         def plan_turn_b(i, halves=(0, 1)):
@@ -416,25 +429,34 @@ def tile_rpa_density_step_s12_kernel(tc, d, b, gap, h_words, h_scales, x_words, 
 
         def plan_response(q, s):
             needs = [("quant_b", s // 2, 0), ("quant_b", s // 2, 1), ("quant_d", q, 0), ("quant_d", q, 1)]
-            tensor_step("rest", ("mul_c", q, s), needs, [("evict_c", q, s)], mul_c, q, s)
+            tensor_step("rest", ("mul_c", q, s), needs, [("evict_c", q, s, 1)], mul_c, q, s)
 
-        def plan_evict_c(q, s):
-            buffered("scalar", ("evict_c", q, s), [("mul_c", q, s)], "chi" if s == 0 else None, [("quant_c", q, 0), ("quant_c", q, 1)], evict_c, q, s)
+        def plan_evict_c(q, s, first=0, count=2):
+            keys = [("evict_c", q, s, e) for e in range(first, first + count)]
+            tag = "chi" if s == 0 and first == 0 else None
+            buffered("scalar", keys, [("mul_c", q, s)], tag, [("quant_c", q, n) for n in range(4)], evict_c, q, s, first, count)
 
-        def plan_quant_c(q, first=0, count=NG):
-            groups = range(first, first + count)
-            step("vector", [("quant_c", q, g) for g in groups], [("evict_c", q, 2 * g + e) for g in groups for e in range(2)], quant_c, q, first, count)
+        def plan_quant_c(q, first=0, count=4):
+            pieces = range(first, first + count)
+            needs = [("evict_c", q, 2 * (n // 2) + tp, n % 2) for n in pieces for tp in range(2)]
+            step("vector", [("quant_c", q, n) for n in pieces], needs, quant_c, q, first, count)
 
         def plan_induced(r):
-            needs = [("quant_c", r // 2, 0), ("quant_c", r // 2, 1), ("quant_p", 0), ("quant_p", 1)]
-            tensor_step("rest", ("mul_o", r), needs, [("evict_o", r)], mul_o, r)
+            needs = [("quant_c", r // 2, r % 2), ("quant_c", r // 2, 2 + r % 2), ("quant_p", 0), ("quant_p", 1)]
+            tensor_step("rest", ("mul_o", r), needs, [("evict_o", r, 1)], mul_o, r)
 
-        def plan_evict_o(r):
-            buffered("vector", ("evict_o", r), [("mul_o", r), ("load_n0", r // 4)], "res", [("store", r)], evict_o, r)
+        def plan_evict_o(r, first=0, count=2):
+            keys = [("evict_o", r, n) for n in range(first, first + count)]
+            buffered("vector", keys, [("mul_o", r), ("load_n0", r // 4)], "res" if first == 0 else None, [("store", r, 1)], evict_o, r, first, count)
+
+        def plan_store(r, first=0, count=2):
+            halves_of_row = range(first, first + count)
+            step("sync", [("store", r, n) for n in halves_of_row], [("evict_o", r, n) for n in halves_of_row], store, r, first, count)
 
         step("sync", "gap", [], load_gap)
         step("gpsimd", "coul", [], load_coul)
-        plan_load("b", 0)
+        buffered("sync", ("load_half", 0), [], "first", [("turn_b", 0, 0)], load_half, 0)
+        buffered("sync", ("load_half", 1), [], "first", [("turn_b", 0, 1)], load_half, 1)
         plan_load("b", 1)
         step("sync", "load_hs", [], load_scales, nc.sync, hs_in, h_scales)
         step("sync", "load_x", [], load_x)
@@ -443,13 +465,13 @@ def tile_rpa_density_step_s12_kernel(tc, d, b, gap, h_words, h_scales, x_words, 
         plan_load("b", 2)
         plan_load("b", 3)
         step("sync", ("load_h", 1), [], load_h, 1)
-        plan_load("d", 0)
-        plan_load("d", 1)
         plan_load("b", 4)
+        plan_load("d", 0)
         plan_load("b", 5)
+        plan_load("d", 1)
+        plan_load("b", 6)
         plan_load("d", 2)
         plan_load("d", 3)
-        plan_load("b", 6)
         plan_load("b", 7)
         plan_load("d", 4)
         plan_load("d", 5)
@@ -459,31 +481,33 @@ def tile_rpa_density_step_s12_kernel(tc, d, b, gap, h_words, h_scales, x_words, 
         plan_load("d", 9)
         plan_load("d", 10)
         plan_load("d", 11)
-        buffered("sync", ("load_n0", 0), [], "rows", [("evict_o", 3)], load_n0, 0)
-        buffered("sync", ("load_n0", 1), [], "rows", [("evict_o", 7)], load_n0, 1)
-        buffered("sync", ("load_n0", 2), [], "rows", [("evict_o", 11)], load_n0, 2)
-        for r in range(ND):
-            step("sync", ("store", r), [("evict_o", r)], store, r)
+        buffered("sync", ("load_n0", 0), [], "rows", [("evict_o", 3, 1)], load_n0, 0)
+        buffered("sync", ("load_n0", 1), [], "rows", [("evict_o", 7, 1)], load_n0, 1)
+        buffered("sync", ("load_n0", 2), [], "rows", [("evict_o", 11, 1)], load_n0, 2)
+        for r in range(ND - 1):
+            plan_store(r)
+        plan_store(ND - 1, 0, 1)
+        plan_store(ND - 1, 1, 1)
 
         plan_turn_b(0)
         plan_turn_b(1)
-        tensor_step("rest", "turn_coul", ["coul_rows"], ["coul_col"], turn_coul)
         plan_trial(0, 0)
         plan_turn_b(2)
+        tensor_step("rest", "turn_coul", ["coul_rows"], ["coul_col"], turn_coul)
         plan_trial(0, 1)
         plan_turn_b(3)
         plan_trial(0, 2)
         plan_trial(0, 3)
-        plan_trial(1, 0)
-        plan_turn_d(0)
         plan_turn_b(4)
-        plan_turn_d(1)
+        plan_turn_d(0)
+        plan_trial(1, 0)
         plan_trial(1, 1)
+        plan_turn_b(5)
+        plan_turn_d(1)
         plan_trial(1, 2)
         plan_trial(1, 3)
-        plan_turn_b(5)
-        plan_turn_d(2)
         plan_turn_b(6)
+        plan_turn_d(2)
         plan_turn_d(3)
         plan_response(0, 0)
         plan_response(0, 1)
@@ -494,14 +518,12 @@ def tile_rpa_density_step_s12_kernel(tc, d, b, gap, h_words, h_scales, x_words, 
         ring["rest"] = [0, 1] + [4 + (turn["rest"] + k) % 4 for k in range(4)] + [2, 3]
         turn["rest"] = 0
         plan_response(1, 1)
-        plan_turn_d(6)
-        plan_turn_d(7)
         plan_response(0, 2)
         plan_response(0, 3)
-        plan_response(2, 0)
-        plan_response(2, 1)
         plan_response(1, 2)
         plan_response(1, 3)
+        plan_response(2, 0)
+        plan_response(2, 1)
         plan_response(2, 2)
         plan_response(2, 3)
         plan_response(3, 0)
@@ -511,19 +533,19 @@ def tile_rpa_density_step_s12_kernel(tc, d, b, gap, h_words, h_scales, x_words, 
         plan_response(4, 0)
         plan_response(4, 1)
         plan_response(4, 2)
-        plan_induced(0)
         plan_response(4, 3)
+        plan_induced(0)
         plan_induced(1)
-        plan_induced(2)
         plan_response(5, 0)
+        plan_induced(2)
         plan_induced(3)
-        plan_induced(4)
         plan_response(5, 1)
+        plan_induced(4)
         plan_induced(5)
         plan_response(5, 2)
         plan_induced(6)
-        plan_response(5, 3)
         plan_induced(7)
+        plan_response(5, 3)
         plan_induced(8)
         plan_induced(9)
         plan_induced(10)
@@ -547,9 +569,9 @@ def tile_rpa_density_step_s12_kernel(tc, d, b, gap, h_words, h_scales, x_words, 
         plan_scale_b(4, 0)
         plan_sort("b", 6, "V")
         plan_scale_b(4, 1)
-        plan_quant_d(0)
         plan_scale_b(5, 0)
         plan_scale_b(5, 1)
+        plan_quant_d(0)
         plan_scale_b(6, 0)
         plan_sort("b", 7, "V")
         plan_scale_b(6, 1)
@@ -559,80 +581,87 @@ def tile_rpa_density_step_s12_kernel(tc, d, b, gap, h_words, h_scales, x_words, 
         plan_quant_b(1, 0)
         plan_quant_b(1, 1)
         plan_quant_d(2)
-        plan_sort_blocks(8, "V")
+        plan_turn_blocks(6)
         plan_weave_p(0)
+        plan_turn_blocks(7)
+        plan_weave_blocks(6, "V")
+        plan_quant_p(0)
+        plan_weave_blocks(7, "V")
         plan_turn_blocks(8)
         plan_quant_d(3)
         plan_turn_blocks(9)
-        plan_quant_p(0)
-        plan_sort_blocks(10, "V")
-        plan_weave_p(1)
+        plan_weave_blocks(8, "V")
+        plan_quant_c(0)
+        plan_weave_blocks(9, "V")
         plan_turn_blocks(10)
         plan_quant_d(4)
-        plan_sort_blocks(11, "V")
-        plan_quant_p(1)
         plan_turn_blocks(11)
         plan_weave_blocks(10, "V")
-        plan_quant_c(0)
+        plan_weave_p(1)
         plan_weave_blocks(11, "V")
-        plan_quant_c(1)
+        plan_quant_p(1)
         plan_quant_d(5)
+        plan_quant_c(1)
         plan_evict_o(0)
         plan_quant_c(2)
         plan_evict_o(1)
-        plan_evict_o(2)
         plan_quant_c(3)
+        plan_evict_o(2)
         plan_evict_o(3)
-        plan_evict_o(4)
         plan_quant_c(4)
+        plan_evict_o(4)
         plan_evict_o(5)
+        plan_quant_c(5, 0, 2)
         plan_evict_o(6)
-        plan_quant_c(5, 0, 1)
         plan_evict_o(7)
+        plan_quant_c(5, 2, 1)
         plan_evict_o(8)
-        plan_quant_c(5, 1, 1)
+        plan_quant_c(5, 3, 1)
         plan_evict_o(9)
         plan_evict_o(10)
-        plan_evict_o(11)
+        plan_evict_o(11, 0, 1)
+        plan_evict_o(11, 1, 1)
 
         plan_sort("b", 1, "S", ((0, 1), (1, 1)))
-        step("scalar", "coul_rows", ["coul"], widen_coul)
-        step("scalar", "coul_col", ["turn_coul"], evict_coul)
         plan_sort("b", 2, "S", ((0, 1), (1, 1)))
+        step("scalar", "coul_rows", ["coul"], widen_coul)
         plan_sort("b", 3, "S")
+        step("scalar", "coul_col", ["turn_coul"], evict_coul)
         plan_scale_t(0, 0)
         plan_scale_t(0, 1)
         plan_sort("d", 0, "S")
         plan_scale_t(0, 2)
         plan_scale_t(0, 3)
-        plan_scale_t(1, 0)
+        plan_sort("d", 1, "S")
         plan_fill_d(0)
+        plan_scale_t(1, 0)
+        plan_scale_t(1, 1)
         plan_sort("d", 2, "S")
         plan_fill_d(1)
-        plan_scale_t(1, 1)
+        plan_sort("d", 3, "S")
         plan_scale_t(1, 2)
         plan_scale_t(1, 3)
-        plan_sort("d", 4, "S")
         plan_fill_d(2)
         plan_fill_d(3)
+        plan_sort("d", 4, "S")
         plan_evict_c(0, 0)
         plan_evict_c(0, 1)
         plan_fill_d(4)
-        plan_sort("d", 6, "S")
         plan_fill_d(5)
+        plan_sort_blocks(6, "S")
         plan_evict_c(1, 0)
+        plan_sort_blocks(7, "S")
         plan_evict_c(1, 1)
-        plan_fill_d(6)
-        plan_fill_d(7)
-        plan_sort_blocks(9, "S")
         plan_evict_c(0, 2)
-        plan_weave_blocks(8, "S")
+        plan_sort_blocks(8, "S")
         plan_evict_c(0, 3)
-        plan_evict_c(2, 0)
-        plan_weave_blocks(9, "S")
-        plan_evict_c(2, 1)
+        plan_sort_blocks(9, "S")
         plan_evict_c(1, 2)
         plan_evict_c(1, 3)
+        plan_sort_blocks(10, "S")
+        plan_evict_c(2, 0)
+        plan_sort_blocks(11, "S")
+        plan_evict_c(2, 1)
         plan_evict_c(2, 2)
         plan_evict_c(2, 3)
         plan_evict_c(3, 0)
@@ -646,7 +675,8 @@ def tile_rpa_density_step_s12_kernel(tc, d, b, gap, h_words, h_scales, x_words, 
         plan_evict_c(5, 0)
         plan_evict_c(5, 1)
         plan_evict_c(5, 2)
-        plan_evict_c(5, 3)
+        plan_evict_c(5, 3, 0, 1)
+        plan_evict_c(5, 3, 1, 1)
 
         with tc.manual_schedule():
             nc.vector.memset(hs_in[:], 0)

@@ -25,7 +25,9 @@ NS = NB // 2
 ND = R // 128
 NQ = ND // 2
 FIRST_BLOCK = 6
-SORTED = {("b", 6), ("b", 7), ("b", 1), ("b", 2), ("b", 3), ("d", 0), ("d", 1), ("d", 2), ("d", 3), ("d", 4)}
+SORTED = {("b", 6), ("b", 1), ("b", 2), ("b", 3), ("d", 0), ("d", 1), ("d", 2), ("d", 4)}
+POOL_TILES = ()
+WARM_UPS = 3
 DEPTH = {"rows": 9, "sortedS": 3, "sortedV": 2, "b_t": 3, "d_t": 3, "res": 3, "chi": 5}
 OWN = {tag: [f"{tag}{k}" for k in range(n)] for tag, n in DEPTH.items()}
 RINGS = {**OWN, "res": OWN["sortedV"] + OWN["res"], "d_flip": ["h_in0", "h_in1"], "pot": ["hs_in"], "chi": OWN["chi"] + ["h_w0"], "first": OWN["res"][:2]}
@@ -60,7 +62,7 @@ def tile_rpa_density_step_s12_kernel(tc, d, b, gap, h_words, h_scales, x_words, 
         cscale = [keep.tile([128, NG, 256], U8, name=f"cscale{q}", align_bytes=64) for q in range(NQ)]
 
         b_sb, d_sb, n0_sb, perm, b_t, d_t, pot, chi = {}, {}, {}, {}, {}, {}, {}, {}
-        tr_vec, tr_b, tr_d, ps_c, ps_o, ps_t, res, d_flip, halves = {}, {}, {}, {}, {}, {}, {}, {}, {}
+        tr_vec, tr_b, tr_d, ps_c, ps_o, ps_t, res, d_flip, halves, b_raw, chi_pairs = {}, {}, {}, {}, {}, {}, {}, {}, {}, {}, {}
 
         def buf(name, shape, dtype):
             return keep.tile(shape, dtype, name=name, align_bytes=64)
@@ -77,11 +79,20 @@ def tile_rpa_density_step_s12_kernel(tc, d, b, gap, h_words, h_scales, x_words, 
                 nc.vector.tensor_copy(out=dst, in_=src)
 
         def sort_pairs(eng, dst, tile, first, count):
-            word = I32 if eng == "G" else F32
-            pairs = tile[:].bitcast(word)[:, 512 * first : 512 * (first + count)]
+            if eng == "G":
+                nc.gpsimd.tensor_scalar(
+                    out=dst[:, first].rearrange("p u w -> p (u w)").bitcast(BF16),
+                    in0=tile[:, 1024 * first : 1024 * (first + 1)].rearrange("p (w u e) -> p u w e", u=2, e=2),
+                    scalar1=1.0,
+                    scalar2=0.0,
+                    op0=ALU.mult,
+                    op1=ALU.add,
+                )
+                return
+            pairs = tile[:].bitcast(F32)[:, 512 * first : 512 * (first + count)]
             copy(
                 eng,
-                dst[:, first : first + count].bitcast(word).rearrange("p h u (c i) -> p h c u i", i=4),
+                dst[:, first : first + count].rearrange("p h u (c i) -> p h c u i", i=4),
                 pairs.rearrange("p (h c i u) -> p h c u i", h=count, u=2, i=4),
             )
 
@@ -141,6 +152,20 @@ def tile_rpa_density_step_s12_kernel(tc, d, b, gap, h_words, h_scales, x_words, 
                 op=ALU.mult,
             )
 
+        def evict_b(name, i, h):
+            if name is not None:
+                b_raw[i] = buf(name, [128, NJ, 128, 2], F32)
+            nc.scalar.copy(out=b_raw[i][:, 2 * h : 2 * h + 2], in_=tr_b[i, h][:].rearrange("p u j a -> p j a u"))
+
+        def scale_raw(i, j):
+            g, c = i // 4, i % 4
+            nc.gpsimd.tensor_tensor(
+                out=b_t[g, j // 2][:, j % 2, :, 32 * c : 32 * (c + 1), :].rearrange("p t m e -> p t (m e)"),
+                in0=b_raw[i][:, j].rearrange("p a u -> p (a u)").bitcast(BF16),
+                in1=ginv[:, j].unsqueeze(1).to_broadcast([128, 128, 4]),
+                op=ALU.mult,
+            )
+
         def quant_b(g, h):
             nc.vector.quantize_mx(
                 out=bcodes[g][h][:].rearrange("p j t m -> p (j t m)").bitcast(FP8X4),
@@ -173,12 +198,34 @@ def tile_rpa_density_step_s12_kernel(tc, d, b, gap, h_words, h_scales, x_words, 
                     stop=(j == NF - 1),
                 )
 
+        def warm_up(banks):
+            spare = bank(banks[0], [128, 512])
+            planes = h_s[0][:].rearrange("p j t m -> p (j t m)")
+            for n in range(WARM_UPS):
+                nc.tensor.matmul_mx(
+                    out=spare[:],
+                    lhsT=x_w[:, 0, 0:256].bitcast(FP4X4),
+                    lhsT_scale=planes[:, 0:128],
+                    rhs=x_w[:, 0, :].bitcast(FP4X4),
+                    rhs_scale=planes[:, 0:512],
+                    start=True,
+                    stop=True,
+                )
+
         def scale_t(g, t):
             nc.scalar.activation(out=pot_s[g][:, t, :], in_=ps_t[g, t][:], func=ACT.Copy, scale=coul_col[:, g, t : t + 1])
 
-        def weave_p(name, g):
-            pot[g] = buf(name, [128, P, 4], BF16)
-            nc.vector.tensor_copy(out=pot[g][:].rearrange("p (c i) t -> p c t i", i=4), in_=pot_s[g][:].rearrange("p t (c i) -> p c t i", i=4))
+        def weave_p(name, g, first, count, eng):
+            if name is not None:
+                pot[g] = buf(name, [128, P, 4], BF16)
+            cols = slice(128 * first, 128 * (first + count))
+            if eng == "G":
+                nc.gpsimd.tensor_scalar(
+                    out=pot[g][:, cols], in0=pot_s[g][:, :, cols].rearrange("p t n -> p n t"), scalar1=1.0, scalar2=0.0, op0=ALU.mult, op1=ALU.add
+                )
+            else:
+                src = pot_s[g][:, :, cols].rearrange("p t (c i) -> p c t i", i=4)
+                nc.vector.tensor_copy(out=pot[g][:, cols].rearrange("p (c i) t -> p c t i", i=4), in_=src)
 
         def quant_p(g):
             nc.vector.quantize_mx(out=pcodes[g][:].bitcast(FP8X4), scales=pscale[g][:], in_=pot[g][:].rearrange("p n t -> p (n t)"))
@@ -257,6 +304,20 @@ def tile_rpa_density_step_s12_kernel(tc, d, b, gap, h_words, h_scales, x_words, 
             rows = slice(16 * first, 16 * (first + count))
             words = chi[q][:, g, :, 2 * tp : 2 * tp + 2].rearrange("p (i c) e -> p i c e", c=8)
             nc.scalar.copy(out=words[:, rows], in_=ps_c[q, s][:].rearrange(order, c=8)[:, rows])
+
+        def evict_pairs(name, q, s):
+            g, tp = s // 2, s % 2
+            if name is not None:
+                chi_pairs[q] = buf(name, [128, 2, NG, 256, 2], BF16)
+            order = "p e (c i) -> p i c e" if 2 * q >= FIRST_BLOCK else "p e (i c) -> p i c e"
+            nc.scalar.copy(out=chi_pairs[q][:, tp, g].rearrange("p (i c) e -> p i c e", c=8), in_=ps_c[q, s][:].rearrange(order, c=8))
+
+        def weave_c(name, q):
+            chi[q] = buf(name, [128, NG, 256, 4], BF16)
+            nc.vector.tensor_copy(
+                out=chi[q][:].rearrange("p g a t -> p (g a t)").bitcast(F32).rearrange("p (c i u) -> p c u i", i=4, u=2),
+                in_=chi_pairs[q][:].rearrange("p u g a e -> p u (g a e)").bitcast(F32).rearrange("p u (c i) -> p c u i", i=4),
+            )
 
         def quant_c(q, first, count):
             cols = slice(128 * first, 128 * (first + count))
@@ -383,11 +444,20 @@ def tile_rpa_density_step_s12_kernel(tc, d, b, gap, h_words, h_scales, x_words, 
 
         def plan_turn_b(i, halves=(0, 1)):
             for h in halves:
-                tensor_step("b", ("turn_b", i, h), ready("b", i, h), [("scale_b", i, h)], turn_b, i, h)
+                tensor_step("b", ("turn_b", i, h), ready("b", i, h), [("evict_b" if i in POOL_TILES else "scale_b", i, h)], turn_b, i, h)
 
         def plan_scale_b(i, h):
             tag = "b_t" if i % 4 == 0 else None
             buffered("vector", ("scale_b", i, h), [("turn_b", i, h), "ginv"], tag, [("quant_b", i // 4, h)], scale_b, i, h)
+
+        def plan_evict_b(i):
+            for h in range(2):
+                buffered("scalar", ("evict_b", i, h), [("turn_b", i, h)], "b_raw" if h == 0 else None, [("scale_b", i, 1)], evict_b, i, h)
+
+        def plan_scale_raw(i):
+            for j in range(NJ):
+                key = ("scale_b", i, j // 2) if j % 2 else ("scale_raw", i, j)
+                step("gpsimd", key, [("evict_b", i, j // 2), ("scale_b", i - i % 4, j // 2)], scale_raw, i, j)
 
         def plan_quant_b(g, h):
             step("vector", ("quant_b", g, h), [("scale_b", 4 * g + c, h) for c in range(4)], quant_b, g, h)
@@ -421,11 +491,13 @@ def tile_rpa_density_step_s12_kernel(tc, d, b, gap, h_words, h_scales, x_words, 
         def plan_scale_t(g, t):
             step("scalar", ("scale_t", g, t), [("mul_t", g, t), "coul_col"], scale_t, g, t)
 
-        def plan_weave_p(g):
-            buffered("vector", ("weave_p", g), [("scale_t", g, t) for t in range(4)], "pot", [("quant_p", g)], weave_p, g)
+        def plan_weave_p(g, eng="V", first=0, count=4, behind=()):
+            keys = [("weave_p", g, n) for n in range(first, first + count)]
+            needs = [("scale_t", g, t) for t in range(4)] + list(behind)
+            buffered(engine[eng], keys, needs, "pot" if first == 0 else None, [("quant_p", g)], weave_p, g, first, count, eng)
 
         def plan_quant_p(g):
-            step("vector", ("quant_p", g), [("weave_p", g)], quant_p, g)
+            step("vector", ("quant_p", g), [("weave_p", g, n) for n in range(4)], quant_p, g)
 
         def plan_response(q, s):
             needs = [("quant_b", s // 2, 0), ("quant_b", s // 2, 1), ("quant_d", q, 0), ("quant_d", q, 1)]
@@ -436,9 +508,16 @@ def tile_rpa_density_step_s12_kernel(tc, d, b, gap, h_words, h_scales, x_words, 
             tag = "chi" if s == 0 and first == 0 else None
             buffered("scalar", keys, [("mul_c", q, s)], tag, [("quant_c", q, n) for n in range(4)], evict_c, q, s, first, count)
 
+        def plan_evict_pairs(q, s):
+            keys = [("evict_c", q, s, e) for e in range(2)]
+            buffered("scalar", keys, [("mul_c", q, s)], "chi" if s == 0 else None, [("weave_c", q)], evict_pairs, q, s)
+
+        def plan_weave_c(q):
+            buffered("vector", ("weave_c", q), [("evict_c", q, s, 1) for s in range(NS)], "b_t", [("quant_c", q, 0)], weave_c, q)
+
         def plan_quant_c(q, first=0, count=4):
             pieces = range(first, first + count)
-            needs = [("evict_c", q, 2 * (n // 2) + tp, n % 2) for n in pieces for tp in range(2)]
+            needs = ([("weave_c", q)] if q < NQ - 1 else []) + [("evict_c", q, 2 * (n // 2) + tp, n % 2) for n in pieces for tp in range(2)]
             step("vector", [("quant_c", q, n) for n in pieces], needs, quant_c, q, first, count)
 
         def plan_induced(r):
@@ -509,9 +588,9 @@ def tile_rpa_density_step_s12_kernel(tc, d, b, gap, h_words, h_scales, x_words, 
         plan_turn_b(6)
         plan_turn_d(2)
         plan_turn_d(3)
+        plan_turn_b(7)
         plan_response(0, 0)
         plan_response(0, 1)
-        plan_turn_b(7)
         plan_turn_d(4)
         plan_turn_d(5)
         plan_response(1, 0)
@@ -573,10 +652,9 @@ def tile_rpa_density_step_s12_kernel(tc, d, b, gap, h_words, h_scales, x_words, 
         plan_scale_b(5, 1)
         plan_quant_d(0)
         plan_scale_b(6, 0)
-        plan_sort("b", 7, "V")
         plan_scale_b(6, 1)
-        plan_quant_d(1)
         plan_scale_b(7, 0)
+        plan_quant_d(1)
         plan_scale_b(7, 1)
         plan_quant_b(1, 0)
         plan_quant_b(1, 1)
@@ -590,26 +668,27 @@ def tile_rpa_density_step_s12_kernel(tc, d, b, gap, h_words, h_scales, x_words, 
         plan_turn_blocks(8)
         plan_quant_d(3)
         plan_turn_blocks(9)
-        plan_weave_blocks(8, "V")
-        plan_quant_c(0)
-        plan_weave_blocks(9, "V")
+        plan_weave_p(1)
         plan_turn_blocks(10)
         plan_quant_d(4)
         plan_turn_blocks(11)
-        plan_weave_blocks(10, "V")
-        plan_weave_p(1)
-        plan_weave_blocks(11, "V")
         plan_quant_p(1)
+        plan_weave_c(0)
+        plan_weave_c(1)
+        plan_quant_c(0)
         plan_quant_d(5)
         plan_quant_c(1)
+        plan_weave_c(2)
         plan_evict_o(0)
         plan_quant_c(2)
         plan_evict_o(1)
-        plan_quant_c(3)
+        plan_weave_c(3)
         plan_evict_o(2)
+        plan_quant_c(3)
         plan_evict_o(3)
-        plan_quant_c(4)
+        plan_weave_c(4)
         plan_evict_o(4)
+        plan_quant_c(4)
         plan_evict_o(5)
         plan_quant_c(5, 0, 2)
         plan_evict_o(6)
@@ -638,40 +717,43 @@ def tile_rpa_density_step_s12_kernel(tc, d, b, gap, h_words, h_scales, x_words, 
         plan_scale_t(1, 1)
         plan_sort("d", 2, "S")
         plan_fill_d(1)
-        plan_sort("d", 3, "S")
         plan_scale_t(1, 2)
         plan_scale_t(1, 3)
         plan_fill_d(2)
         plan_fill_d(3)
         plan_sort("d", 4, "S")
-        plan_evict_c(0, 0)
-        plan_evict_c(0, 1)
+        plan_evict_pairs(0, 0)
+        plan_evict_pairs(0, 1)
         plan_fill_d(4)
         plan_fill_d(5)
         plan_sort_blocks(6, "S")
-        plan_evict_c(1, 0)
+        plan_evict_pairs(1, 0)
         plan_sort_blocks(7, "S")
-        plan_evict_c(1, 1)
-        plan_evict_c(0, 2)
+        plan_evict_pairs(1, 1)
+        plan_evict_pairs(0, 2)
         plan_sort_blocks(8, "S")
-        plan_evict_c(0, 3)
+        plan_evict_pairs(0, 3)
         plan_sort_blocks(9, "S")
-        plan_evict_c(1, 2)
-        plan_evict_c(1, 3)
+        plan_evict_pairs(1, 2)
+        plan_evict_pairs(1, 3)
         plan_sort_blocks(10, "S")
-        plan_evict_c(2, 0)
+        plan_weave_blocks(8, "S")
+        plan_evict_pairs(2, 0)
+        plan_weave_blocks(9, "S")
         plan_sort_blocks(11, "S")
-        plan_evict_c(2, 1)
-        plan_evict_c(2, 2)
-        plan_evict_c(2, 3)
-        plan_evict_c(3, 0)
-        plan_evict_c(3, 1)
-        plan_evict_c(3, 2)
-        plan_evict_c(3, 3)
-        plan_evict_c(4, 0)
-        plan_evict_c(4, 1)
-        plan_evict_c(4, 2)
-        plan_evict_c(4, 3)
+        plan_evict_pairs(2, 1)
+        plan_evict_pairs(2, 2)
+        plan_weave_blocks(10, "S")
+        plan_evict_pairs(2, 3)
+        plan_weave_blocks(11, "S")
+        plan_evict_pairs(3, 0)
+        plan_evict_pairs(3, 1)
+        plan_evict_pairs(3, 2)
+        plan_evict_pairs(3, 3)
+        plan_evict_pairs(4, 0)
+        plan_evict_pairs(4, 1)
+        plan_evict_pairs(4, 2)
+        plan_evict_pairs(4, 3)
         plan_evict_c(5, 0)
         plan_evict_c(5, 1)
         plan_evict_c(5, 2)

@@ -25,9 +25,9 @@ NS = NB // 2
 ND = R // 128
 NQ = ND // 2
 FIRST_BLOCK = 6
-SORTED = {("b", 6), ("b", 1), ("b", 2), ("b", 3), ("d", 0), ("d", 1), ("d", 2), ("d", 4)}
+SORTED = {("b", 5), ("b", 6), ("b", 1), ("b", 3), ("b", 4), ("d", 0), ("d", 1), ("d", 2), ("d", 4)}
 POOL_TILES = ()
-WARM_UPS = 3
+WARM_UPS = 2
 DEPTH = {"rows": 9, "sortedS": 3, "sortedV": 2, "b_t": 3, "d_t": 3, "res": 3, "chi": 5}
 OWN = {tag: [f"{tag}{k}" for k in range(n)] for tag, n in DEPTH.items()}
 RINGS = {**OWN, "res": OWN["sortedV"] + OWN["res"], "d_flip": ["h_in0", "h_in1"], "pot": ["hs_in"], "chi": OWN["chi"] + ["h_w0"], "first": OWN["res"][:2]}
@@ -173,8 +173,8 @@ def tile_rpa_density_step_s12_kernel(tc, d, b, gap, h_words, h_scales, x_words, 
                 in_=b_t[g, h][:].rearrange("p j t m e -> p (j t m e)"),
             )
 
-        def sort_h(g):
-            nc.vector.tensor_copy(
+        def sort_h(g, eng=nc.vector):
+            eng.tensor_copy(
                 out=h_w[g][:].bitcast(I32).rearrange("p j t (q w) -> p q j t w", w=4),
                 in_=h_in[g][:].rearrange("p j (q t w) -> p q j t w", t=4, w=4),
             )
@@ -200,14 +200,13 @@ def tile_rpa_density_step_s12_kernel(tc, d, b, gap, h_words, h_scales, x_words, 
 
         def warm_up(banks):
             spare = bank(banks[0], [128, 512])
-            planes = h_s[0][:].rearrange("p j t m -> p (j t m)")
             for n in range(WARM_UPS):
                 nc.tensor.matmul_mx(
                     out=spare[:],
-                    lhsT=x_w[:, 0, 0:256].bitcast(FP4X4),
-                    lhsT_scale=planes[:, 0:128],
-                    rhs=x_w[:, 0, :].bitcast(FP4X4),
-                    rhs_scale=planes[:, 0:512],
+                    lhsT=h_w[0][:, 0, 0, :].bitcast(FP4X4),
+                    lhsT_scale=h_s[0][:, 0, 0, :],
+                    rhs=h_w[0][:, 0].rearrange("p t m -> p (t m)").bitcast(FP4X4),
+                    rhs_scale=h_s[0][:, 0].rearrange("p t m -> p (t m)"),
                     start=True,
                     stop=True,
                 )
@@ -245,9 +244,9 @@ def tile_rpa_density_step_s12_kernel(tc, d, b, gap, h_words, h_scales, x_words, 
 
         def load_blocks(name, r):
             d_sb[r] = buf(name, [128, 4, NJ, 128], BF16)
-            src = d[256 * (r // 2) : 256 * (r // 2 + 1), :].rearrange("(i c) (j s k) -> s i c j k", c=8, s=4, k=128)
+            src = d[128 * r : 128 * (r + 1), :].rearrange("(i c) (j s k) -> s i c j k", c=4, s=4, k=128)
             for s in (0, 2, 1, 3):
-                nc.sync.dma_start(out=d_sb[r][32 * s : 32 * (s + 1)], in_=src[s, :, 4 * (r % 2) : 4 * (r % 2) + 4])
+                nc.sync.dma_start(out=d_sb[r][32 * s : 32 * (s + 1)], in_=src[s])
 
         def sort_blocks(name, r, eng):
             word = I32 if eng == "G" else F32
@@ -281,36 +280,43 @@ def tile_rpa_density_step_s12_kernel(tc, d, b, gap, h_words, h_scales, x_words, 
                 in_=d_t[q][:, js].rearrange("p j a u -> p (j a u)").bitcast(BF16),
             )
 
-        def mul_c(banks, q, s):
-            ps_c[q, s] = bank(banks[0], [128, 2, 256])
+        def mul_c(banks, q, s, first, count):
+            cols = slice(128 * first, 128 * (first + count))
+            acc = bank(banks[0], [128, 2, 128 * count])
+            for n in range(count):
+                ps_c[q, s, first + n] = acc[:, :, 128 * n : 128 * (n + 1)]
+            ps_c[q, s] = acc[:]
             for e in range(2):
                 g, t = s // 2, 2 * (s % 2) + e
                 for j in range(NJ):
                     nc.tensor.matmul_mx(
-                        out=ps_c[q, s][:, e, :],
+                        out=acc[:, e, :],
                         lhsT=bcodes[g][j // 2][:, j % 2, t, :].bitcast(FP8X4),
                         lhsT_scale=bscale[g][j // 2][:, j % 2, t, :],
-                        rhs=dcodes[q][:, j, :].bitcast(FP8X4),
-                        rhs_scale=dscale[q][:, j, :],
+                        rhs=dcodes[q][:, j, cols].bitcast(FP8X4),
+                        rhs_scale=dscale[q][:, j, cols],
                         start=(j == 0),
                         stop=(j == NJ - 1),
                     )
+
+        def in_row_order(q, sums):
+            if 2 * q >= FIRST_BLOCK:
+                return sums.rearrange("p e (n c i) -> p n i c e", c=4, i=32)
+            return sums.rearrange("p e (n i c) -> p n i c e", c=4, i=32)
 
         def evict_c(name, q, s, first, count):
             g, tp = s // 2, s % 2
             if name is not None:
                 chi[q] = buf(name, [128, NG, 256, 4], BF16)
-            order = "p e (c i) -> p i c e" if 2 * q >= FIRST_BLOCK else "p e (i c) -> p i c e"
-            rows = slice(16 * first, 16 * (first + count))
-            words = chi[q][:, g, :, 2 * tp : 2 * tp + 2].rearrange("p (i c) e -> p i c e", c=8)
-            nc.scalar.copy(out=words[:, rows], in_=ps_c[q, s][:].rearrange(order, c=8)[:, rows])
+            words = chi[q][:, g, 128 * first : 128 * (first + count), 2 * tp : 2 * tp + 2]
+            sums = ps_c[q, s] if count == 2 else ps_c[q, s, first]
+            nc.scalar.copy(out=words.rearrange("p (n i c) e -> p n i c e", c=4, i=32), in_=in_row_order(q, sums))
 
         def evict_pairs(name, q, s):
             g, tp = s // 2, s % 2
             if name is not None:
                 chi_pairs[q] = buf(name, [128, 2, NG, 256, 2], BF16)
-            order = "p e (c i) -> p i c e" if 2 * q >= FIRST_BLOCK else "p e (i c) -> p i c e"
-            nc.scalar.copy(out=chi_pairs[q][:, tp, g].rearrange("p (i c) e -> p i c e", c=8), in_=ps_c[q, s][:].rearrange(order, c=8))
+            nc.scalar.copy(out=chi_pairs[q][:, tp, g].rearrange("p (n i c) e -> p n i c e", c=4, i=32), in_=in_row_order(q, ps_c[q, s]))
 
         def weave_c(name, q):
             chi[q] = buf(name, [128, NG, 256, 4], BF16)
@@ -499,18 +505,19 @@ def tile_rpa_density_step_s12_kernel(tc, d, b, gap, h_words, h_scales, x_words, 
         def plan_quant_p(g):
             step("vector", ("quant_p", g), [("weave_p", g, n) for n in range(4)], quant_p, g)
 
-        def plan_response(q, s):
+        def plan_response(q, s, first=0, count=2):
             needs = [("quant_b", s // 2, 0), ("quant_b", s // 2, 1), ("quant_d", q, 0), ("quant_d", q, 1)]
-            tensor_step("rest", ("mul_c", q, s), needs, [("evict_c", q, s, 1)], mul_c, q, s)
+            keys = [("mul_c", q, s, e) for e in range(first, first + count)]
+            tensor_step("rest", keys, needs, [("evict_c", q, s, first + count - 1)], mul_c, q, s, first, count)
 
         def plan_evict_c(q, s, first=0, count=2):
             keys = [("evict_c", q, s, e) for e in range(first, first + count)]
             tag = "chi" if s == 0 and first == 0 else None
-            buffered("scalar", keys, [("mul_c", q, s)], tag, [("quant_c", q, n) for n in range(4)], evict_c, q, s, first, count)
+            buffered("scalar", keys, [("mul_c", q, s, first)], tag, [("quant_c", q, n) for n in range(4)], evict_c, q, s, first, count)
 
         def plan_evict_pairs(q, s):
             keys = [("evict_c", q, s, e) for e in range(2)]
-            buffered("scalar", keys, [("mul_c", q, s)], "chi" if s == 0 else None, [("weave_c", q)], evict_pairs, q, s)
+            buffered("scalar", keys, [("mul_c", q, s, 0)], "chi" if s == 0 else None, [("weave_c", q)], evict_pairs, q, s)
 
         def plan_weave_c(q):
             buffered("vector", ("weave_c", q), [("evict_c", q, s, 1) for s in range(NS)], "b_t", [("quant_c", q, 0)], weave_c, q)
@@ -538,10 +545,10 @@ def tile_rpa_density_step_s12_kernel(tc, d, b, gap, h_words, h_scales, x_words, 
         buffered("sync", ("load_half", 1), [], "first", [("turn_b", 0, 1)], load_half, 1)
         plan_load("b", 1)
         step("sync", "load_hs", [], load_scales, nc.sync, hs_in, h_scales)
-        step("sync", "load_x", [], load_x)
         step("sync", ("load_h", 0), [], load_h, 0)
-        step("sync", "load_xs", [], load_scales, nc.sync, x_s[:].bitcast(I32), x_scales)
+        step("sync", "load_x", [], load_x)
         plan_load("b", 2)
+        step("sync", "load_xs", [], load_scales, nc.sync, x_s[:].bitcast(I32), x_scales)
         plan_load("b", 3)
         step("sync", ("load_h", 1), [], load_h, 1)
         plan_load("b", 4)
@@ -570,17 +577,18 @@ def tile_rpa_density_step_s12_kernel(tc, d, b, gap, h_words, h_scales, x_words, 
 
         plan_turn_b(0)
         plan_turn_b(1)
-        plan_trial(0, 0)
-        plan_turn_b(2)
         tensor_step("rest", "turn_coul", ["coul_rows"], ["coul_col"], turn_coul)
+        tensor_step("rest", "warm_up", [("sort_h", 0), ("sort_hs", 0)], ["warm_up"], warm_up)
+        plan_turn_b(2)
+        plan_trial(0, 0)
         plan_trial(0, 1)
         plan_turn_b(3)
         plan_trial(0, 2)
         plan_trial(0, 3)
         plan_turn_b(4)
-        plan_turn_d(0)
         plan_trial(1, 0)
         plan_trial(1, 1)
+        plan_turn_d(0)
         plan_turn_b(5)
         plan_turn_d(1)
         plan_trial(1, 2)
@@ -624,8 +632,9 @@ def tile_rpa_density_step_s12_kernel(tc, d, b, gap, h_words, h_scales, x_words, 
         plan_response(5, 2)
         plan_induced(6)
         plan_induced(7)
-        plan_response(5, 3)
         plan_induced(8)
+        plan_response(5, 3, 0, 1)
+        plan_response(5, 3, 1, 1)
         plan_induced(9)
         plan_induced(10)
         plan_induced(11)
@@ -634,16 +643,17 @@ def tile_rpa_density_step_s12_kernel(tc, d, b, gap, h_words, h_scales, x_words, 
         plan_scale_b(0, 0)
         plan_scale_b(0, 1)
         step("vector", ("sort_hs", 0), ["load_hs", "load_x", "load_xs"], sort_hs, 0)
+        step("vector", ("sort_hs", 1), ["load_hs", "load_x", "load_xs"], sort_hs, 1)
         step("vector", ("sort_h", 0), [("load_h", 0)], sort_h, 0)
         plan_scale_b(1, 0)
-        step("vector", ("sort_hs", 1), ["load_hs", "load_x", "load_xs"], sort_hs, 1)
         plan_scale_b(1, 1)
         plan_scale_b(2, 0)
-        step("vector", ("sort_h", 1), [("load_h", 1)], sort_h, 1)
         plan_scale_b(2, 1)
+        step("vector", ("sort_h", 1), [("load_h", 1)], sort_h, 1)
         plan_scale_b(3, 0)
         plan_scale_b(3, 1)
         plan_quant_b(0, 0)
+        plan_sort("b", 5, "V")
         plan_quant_b(0, 1)
         plan_scale_b(4, 0)
         plan_sort("b", 6, "V")
@@ -693,28 +703,28 @@ def tile_rpa_density_step_s12_kernel(tc, d, b, gap, h_words, h_scales, x_words, 
         plan_quant_c(5, 0, 2)
         plan_evict_o(6)
         plan_evict_o(7)
-        plan_quant_c(5, 2, 1)
         plan_evict_o(8)
-        plan_quant_c(5, 3, 1)
+        plan_quant_c(5, 2, 1)
         plan_evict_o(9)
+        plan_quant_c(5, 3, 1)
         plan_evict_o(10)
         plan_evict_o(11, 0, 1)
         plan_evict_o(11, 1, 1)
 
         plan_sort("b", 1, "S", ((0, 1), (1, 1)))
-        plan_sort("b", 2, "S", ((0, 1), (1, 1)))
         step("scalar", "coul_rows", ["coul"], widen_coul)
-        plan_sort("b", 3, "S")
         step("scalar", "coul_col", ["turn_coul"], evict_coul)
+        plan_sort("b", 3, "S", ((0, 1), (1, 1)))
         plan_scale_t(0, 0)
         plan_scale_t(0, 1)
-        plan_sort("d", 0, "S")
+        plan_sort("b", 4, "S")
         plan_scale_t(0, 2)
+        plan_sort("d", 0, "S")
         plan_scale_t(0, 3)
-        plan_sort("d", 1, "S")
-        plan_fill_d(0)
         plan_scale_t(1, 0)
+        plan_sort("d", 1, "S")
         plan_scale_t(1, 1)
+        plan_fill_d(0)
         plan_sort("d", 2, "S")
         plan_fill_d(1)
         plan_scale_t(1, 2)

@@ -10,7 +10,6 @@ F32 = mybir.dt.float32
 BF16 = mybir.dt.bfloat16
 U32 = mybir.dt.uint32
 I32 = mybir.dt.int32
-U16 = mybir.dt.uint16
 U8 = mybir.dt.uint8
 FP8X4 = mybir.dt.float8_e4m3fn_x4
 FP4X4 = mybir.dt.float4_e2m1fn_x4
@@ -20,17 +19,22 @@ ACT = mybir.ActivationFunctionType
 NJ = T // 512
 NF = F // 512
 NG = A // 512
-NB = A // 128
-NS = NB // 2
+NS = 2 * NG
 ND = R // 128
 NQ = ND // 2
 FIRST_BLOCK = 6
-SORTED = {("b", 5), ("b", 6), ("b", 1), ("b", 3), ("b", 4), ("d", 0), ("d", 1), ("d", 2), ("d", 4)}
-POOL_TILES = ()
-WARM_UPS = 2
+SORTED = {("b", i) for i in (1, 3, 4, 5, 6)} | {("d", r) for r in (0, 1, 2, 4)}
+WARM_UPS = 3
 DEPTH = {"rows": 9, "sortedS": 3, "sortedV": 2, "b_t": 3, "d_t": 3, "res": 3, "chi": 5}
 OWN = {tag: [f"{tag}{k}" for k in range(n)] for tag, n in DEPTH.items()}
-RINGS = {**OWN, "res": OWN["sortedV"] + OWN["res"], "d_flip": ["h_in0", "h_in1"], "pot": ["hs_in"], "chi": OWN["chi"] + ["h_w0"], "first": OWN["res"][:2]}
+RINGS = {
+    **OWN,
+    "first": OWN["res"][:2],
+    "res": OWN["sortedV"] + OWN["res"],
+    "d_flip": ["h_in0", "h_in1"],
+    "pot": ["hs_in"],
+    "chi": OWN["chi"] + ["h_w0"],
+}
 
 
 def tile_rpa_density_step_s12_kernel(tc, d, b, gap, h_words, h_scales, x_words, x_scales, coul, n0, out):
@@ -61,8 +65,8 @@ def tile_rpa_density_step_s12_kernel(tc, d, b, gap, h_words, h_scales, x_words, 
         ccodes = [keep.tile([128, NG, 256], U32, name=f"ccodes{q}", align_bytes=64) for q in range(NQ)]
         cscale = [keep.tile([128, NG, 256], U8, name=f"cscale{q}", align_bytes=64) for q in range(NQ)]
 
-        b_sb, d_sb, n0_sb, perm, b_t, d_t, pot, chi = {}, {}, {}, {}, {}, {}, {}, {}
-        tr_vec, tr_b, tr_d, ps_c, ps_o, ps_t, res, d_flip, halves, b_raw, chi_pairs = {}, {}, {}, {}, {}, {}, {}, {}, {}, {}, {}
+        halves, rows, n0_sb, perm, b_t, d_t, d_flip, pot, chi_pairs, chi, res = {}, {}, {}, {}, {}, {}, {}, {}, {}, {}, {}
+        tr_coul, tr_b, tr_d, ps_t, ps_c, ps_o = {}, {}, {}, {}, {}, {}
 
         def buf(name, shape, dtype):
             return keep.tile(shape, dtype, name=name, align_bytes=64)
@@ -73,40 +77,16 @@ def tile_rpa_density_step_s12_kernel(tc, d, b, gap, h_words, h_scales, x_words, 
         def copy(eng, dst, src):
             if eng == "S":
                 nc.scalar.copy(out=dst, in_=src)
-            elif eng == "G":
-                nc.gpsimd.tensor_copy(out=dst, in_=src)
             else:
                 nc.vector.tensor_copy(out=dst, in_=src)
 
-        def sort_pairs(eng, dst, tile, first, count):
-            if eng == "G":
-                nc.gpsimd.tensor_scalar(
-                    out=dst[:, first].rearrange("p u w -> p (u w)").bitcast(BF16),
-                    in0=tile[:, 1024 * first : 1024 * (first + 1)].rearrange("p (w u e) -> p u w e", u=2, e=2),
-                    scalar1=1.0,
-                    scalar2=0.0,
-                    op0=ALU.mult,
-                    op1=ALU.add,
-                )
-                return
-            pairs = tile[:].bitcast(F32)[:, 512 * first : 512 * (first + count)]
-            copy(
-                eng,
-                dst[:, first : first + count].rearrange("p h u (c i) -> p h c u i", i=4),
-                pairs.rearrange("p (h c i u) -> p h c u i", h=count, u=2, i=4),
-            )
-
-        def load_b(name, i):
-            b_sb[i] = buf(name, [128, T], BF16)
-            nc.sync.dma_start(out=b_sb[i][:], in_=b[i * 128 : (i + 1) * 128, :])
+        def load_rows(name, what, n):
+            rows[what, n] = buf(name, [128, T], BF16)
+            nc.sync.dma_start(out=rows[what, n][:], in_=(b if what == "b" else d)[n * 128 : (n + 1) * 128, :])
 
         def load_half(name, h):
             halves[h] = buf(name, [128, T // 2], BF16)
             nc.sync.dma_start(out=halves[h][:], in_=b[0:128, 1024 * h : 1024 * (h + 1)])
-
-        def load_d(name, r):
-            d_sb[r] = buf(name, [128, T], BF16)
-            nc.sync.dma_start(out=d_sb[r][:], in_=d[r * 128 : (r + 1) * 128, :])
 
         def load_n0(name, c):
             n0_sb[c] = buf(name, [128, 4, P], BF16)
@@ -118,21 +98,26 @@ def tile_rpa_density_step_s12_kernel(tc, d, b, gap, h_words, h_scales, x_words, 
         def load_x():
             nc.sync.dma_start(out=x_w[:].bitcast(I32), in_=x_words.bitcast(I32).rearrange("j p n -> p j n"))
 
-        def load_scales(eng, plane, scales):
+        def load_scales(plane, scales):
             for r in range(4):
-                eng.dma_start(out=plane[r:128:32], in_=scales.bitcast(I32)[:, r:16:4, :].rearrange("j Q n -> Q j n"))
+                nc.sync.dma_start(out=plane[r:128:32], in_=scales.bitcast(I32)[:, r:16:4, :].rearrange("j Q n -> Q j n"))
 
         def sort_rows(name, what, n, first, count, eng):
-            if first == 0:
+            if name is not None:
                 perm[what, n] = buf(name, [128, 2, 2, T // 8], F32)
-            sort_pairs(eng, perm[what, n], (b_sb if what == "b" else d_sb)[n], first, count)
+            pairs = rows[what, n][:].bitcast(F32)[:, 512 * first : 512 * (first + count)]
+            copy(
+                eng,
+                perm[what, n][:, first : first + count].rearrange("p h u (c i) -> p h c u i", i=4),
+                pairs.rearrange("p (h c i u) -> p h c u i", h=count, u=2, i=4),
+            )
 
         def pairs_of(what, n, h, jj, u):
             if (what, n) == ("b", 0):
                 return halves[h][:].bitcast(F32)[:, 256 * jj + u : 256 * (jj + 1) : 2]
-            if (what, n) in perm:
+            if (what, n) in SORTED:
                 return perm[what, n][:, h, u, 128 * jj : 128 * (jj + 1)]
-            return (b_sb if what == "b" else d_sb)[n][:].bitcast(F32)[:, 512 * h + 256 * jj + u : 512 * h + 256 * (jj + 1) : 2]
+            return rows[what, n][:].bitcast(F32)[:, 512 * h + 256 * jj + u : 512 * h + 256 * (jj + 1) : 2]
 
         def turn_b(banks, i, h):
             tr_b[i, h] = bank(banks[0], [128, 2, 2, 128])
@@ -143,26 +128,12 @@ def tile_rpa_density_step_s12_kernel(tc, d, b, gap, h_words, h_scales, x_words, 
 
         def scale_b(name, i, h):
             g, c = i // 4, i % 4
-            if c == 0:
+            if name is not None:
                 b_t[g, h] = buf(name, [128, 2, 4, 128, 4], BF16)
             nc.vector.tensor_tensor(
                 out=b_t[g, h][:, :, :, 32 * c : 32 * (c + 1), :].rearrange("p j t m e -> p (j t) (m e)"),
                 in0=tr_b[i, h][:].bitcast(BF16).rearrange("p u j (a e) -> p (j a) u e", e=2),
                 in1=ginv[:, 2 * h : 2 * h + 2].unsqueeze(2).to_broadcast([128, 2, 128, 4]),
-                op=ALU.mult,
-            )
-
-        def evict_b(name, i, h):
-            if name is not None:
-                b_raw[i] = buf(name, [128, NJ, 128, 2], F32)
-            nc.scalar.copy(out=b_raw[i][:, 2 * h : 2 * h + 2], in_=tr_b[i, h][:].rearrange("p u j a -> p j a u"))
-
-        def scale_raw(i, j):
-            g, c = i // 4, i % 4
-            nc.gpsimd.tensor_tensor(
-                out=b_t[g, j // 2][:, j % 2, :, 32 * c : 32 * (c + 1), :].rearrange("p t m e -> p t (m e)"),
-                in0=b_raw[i][:, j].rearrange("p a u -> p (a u)").bitcast(BF16),
-                in1=ginv[:, j].unsqueeze(1).to_broadcast([128, 128, 4]),
                 op=ALU.mult,
             )
 
@@ -173,8 +144,8 @@ def tile_rpa_density_step_s12_kernel(tc, d, b, gap, h_words, h_scales, x_words, 
                 in_=b_t[g, h][:].rearrange("p j t m e -> p (j t m e)"),
             )
 
-        def sort_h(g, eng=nc.vector):
-            eng.tensor_copy(
+        def sort_h(g):
+            nc.vector.tensor_copy(
                 out=h_w[g][:].bitcast(I32).rearrange("p j t (q w) -> p q j t w", w=4),
                 in_=h_in[g][:].rearrange("p j (q t w) -> p q j t w", t=4, w=4),
             )
@@ -214,17 +185,9 @@ def tile_rpa_density_step_s12_kernel(tc, d, b, gap, h_words, h_scales, x_words, 
         def scale_t(g, t):
             nc.scalar.activation(out=pot_s[g][:, t, :], in_=ps_t[g, t][:], func=ACT.Copy, scale=coul_col[:, g, t : t + 1])
 
-        def weave_p(name, g, first, count, eng):
-            if name is not None:
-                pot[g] = buf(name, [128, P, 4], BF16)
-            cols = slice(128 * first, 128 * (first + count))
-            if eng == "G":
-                nc.gpsimd.tensor_scalar(
-                    out=pot[g][:, cols], in0=pot_s[g][:, :, cols].rearrange("p t n -> p n t"), scalar1=1.0, scalar2=0.0, op0=ALU.mult, op1=ALU.add
-                )
-            else:
-                src = pot_s[g][:, :, cols].rearrange("p t (c i) -> p c t i", i=4)
-                nc.vector.tensor_copy(out=pot[g][:, cols].rearrange("p (c i) t -> p c t i", i=4), in_=src)
+        def weave_p(name, g):
+            pot[g] = buf(name, [128, P, 4], BF16)
+            nc.vector.tensor_copy(out=pot[g][:].rearrange("p (c i) t -> p c t i", i=4), in_=pot_s[g][:].rearrange("p t (c i) -> p c t i", i=4))
 
         def quant_p(g):
             nc.vector.quantize_mx(out=pcodes[g][:].bitcast(FP8X4), scales=pscale[g][:], in_=pot[g][:].rearrange("p n t -> p (n t)"))
@@ -238,54 +201,48 @@ def tile_rpa_density_step_s12_kernel(tc, d, b, gap, h_words, h_scales, x_words, 
 
         def evict_d(name, r, h):
             q = r // 2
-            if r % 2 == 0 and h == 0:
+            if name is not None:
                 d_t[q] = buf(name, [128, NJ, 256, 2], F32)
             nc.scalar.copy(out=d_t[q][:, 2 * h : 2 * h + 2, 128 * (r % 2) : 128 * (r % 2) + 128, :], in_=tr_d[r, h][:].rearrange("p j u a -> p j a u"))
 
         def load_blocks(name, r):
-            d_sb[r] = buf(name, [128, 4, NJ, 128], BF16)
+            rows["d", r] = buf(name, [128, 4, NJ, 128], BF16)
             src = d[128 * r : 128 * (r + 1), :].rearrange("(i c) (j s k) -> s i c j k", c=4, s=4, k=128)
             for s in (0, 2, 1, 3):
-                nc.sync.dma_start(out=d_sb[r][32 * s : 32 * (s + 1)], in_=src[s])
+                nc.sync.dma_start(out=rows["d", r][32 * s : 32 * (s + 1)], in_=src[s])
 
-        def sort_blocks(name, r, eng):
-            word = I32 if eng == "G" else F32
-            perm["blocks", r] = buf(name, [128, 16, 2, 32], F32)
-            copy(
-                eng,
-                perm["blocks", r][:].bitcast(word).rearrange("p n u (a i) -> p n a u i", i=4),
-                d_sb[r][:].rearrange("p c j k -> p (c j k)").bitcast(word).rearrange("p (n a i u) -> p n a u i", n=16, i=4, u=2),
+        def sort_blocks(name, r):
+            perm["d", r] = buf(name, [128, 16, 2, 32], F32)
+            nc.scalar.copy(
+                out=perm["d", r][:].rearrange("p n u (a i) -> p n a u i", i=4),
+                in_=rows["d", r][:].rearrange("p c j k -> p (c j k)").bitcast(F32).rearrange("p (n a i u) -> p n a u i", n=16, i=4, u=2),
             )
 
         def turn_blocks(name, r):
             d_flip[r] = buf(name, [128, 4, NJ, 2, 32], F32)
-            nc.vector.transpose(out=d_flip[r][:].rearrange("p c j u i -> p (c j u i)"), in_=perm["blocks", r][:].rearrange("p n u w -> p (n u w)"))
+            nc.vector.transpose(out=d_flip[r][:].rearrange("p c j u i -> p (c j u i)"), in_=perm["d", r][:].rearrange("p n u w -> p (n u w)"))
 
         def weave_blocks(name, r, eng):
             q = r // 2
-            if r % 2 == 0:
+            if name is not None:
                 d_t[q] = buf(name, [128, NJ, 256, 2], F32)
-            word = I32 if eng == "G" else F32
             copy(
                 eng,
-                d_t[q][:].bitcast(word)[:, :, 128 * (r % 2) : 128 * (r % 2) + 128, :].rearrange("p j (c i) u -> p j c i u", i=32),
-                d_flip[r][:].bitcast(word).rearrange("p c j u i -> p j c i u"),
+                d_t[q][:, :, 128 * (r % 2) : 128 * (r % 2) + 128, :].rearrange("p j (c i) u -> p j c i u", i=32),
+                d_flip[r][:].rearrange("p c j u i -> p j c i u"),
             )
 
-        def quant_d(q, first, count):
-            js = slice(2 * first, 2 * (first + count))
+        def quant_d(q):
             nc.vector.quantize_mx(
-                out=dcodes[q][:, js].rearrange("p j a -> p (j a)").bitcast(FP8X4),
-                scales=dscale[q][:, js].rearrange("p j a -> p (j a)"),
-                in_=d_t[q][:, js].rearrange("p j a u -> p (j a u)").bitcast(BF16),
+                out=dcodes[q][:].rearrange("p j a -> p (j a)").bitcast(FP8X4),
+                scales=dscale[q][:].rearrange("p j a -> p (j a)"),
+                in_=d_t[q][:].rearrange("p j a u -> p (j a u)").bitcast(BF16),
             )
 
         def mul_c(banks, q, s, first, count):
             cols = slice(128 * first, 128 * (first + count))
             acc = bank(banks[0], [128, 2, 128 * count])
-            for n in range(count):
-                ps_c[q, s, first + n] = acc[:, :, 128 * n : 128 * (n + 1)]
-            ps_c[q, s] = acc[:]
+            ps_c[q, s, first] = acc
             for e in range(2):
                 g, t = s // 2, 2 * (s % 2) + e
                 for j in range(NJ):
@@ -309,14 +266,13 @@ def tile_rpa_density_step_s12_kernel(tc, d, b, gap, h_words, h_scales, x_words, 
             if name is not None:
                 chi[q] = buf(name, [128, NG, 256, 4], BF16)
             words = chi[q][:, g, 128 * first : 128 * (first + count), 2 * tp : 2 * tp + 2]
-            sums = ps_c[q, s] if count == 2 else ps_c[q, s, first]
-            nc.scalar.copy(out=words.rearrange("p (n i c) e -> p n i c e", c=4, i=32), in_=in_row_order(q, sums))
+            nc.scalar.copy(out=words.rearrange("p (n i c) e -> p n i c e", c=4, i=32), in_=in_row_order(q, ps_c[q, s, first][:]))
 
         def evict_pairs(name, q, s):
             g, tp = s // 2, s % 2
             if name is not None:
                 chi_pairs[q] = buf(name, [128, 2, NG, 256, 2], BF16)
-            nc.scalar.copy(out=chi_pairs[q][:, tp, g].rearrange("p (n i c) e -> p n i c e", c=4, i=32), in_=in_row_order(q, ps_c[q, s]))
+            nc.scalar.copy(out=chi_pairs[q][:, tp, g].rearrange("p (n i c) e -> p n i c e", c=4, i=32), in_=in_row_order(q, ps_c[q, s, 0][:]))
 
         def weave_c(name, q):
             chi[q] = buf(name, [128, NG, 256, 4], BF16)
@@ -371,15 +327,15 @@ def tile_rpa_density_step_s12_kernel(tc, d, b, gap, h_words, h_scales, x_words, 
             nc.scalar.copy(out=coul_rows[0:4], in_=coul_in[0:4])
 
         def turn_coul(banks):
-            tr_vec[0] = bank(banks[0], [128, NG, 128])
+            tr_coul[0] = bank(banks[0], [128, NG, 128])
             for g in range(NG):
-                nc.tensor.transpose(tr_vec[0][:, g, :], coul_rows[:, g, :], ident[:])
+                nc.tensor.transpose(tr_coul[0][:, g, :], coul_rows[:, g, :], ident[:])
 
         def evict_coul():
-            nc.scalar.copy(out=coul_col[:], in_=tr_vec[0][:, :, 0:4])
+            nc.scalar.copy(out=coul_col[:], in_=tr_coul[0][:, :, 0:4])
 
         queue = {"sync": [], "tensor": [], "scalar": [], "vector": [], "gpsimd": []}
-        engine = {"S": "scalar", "V": "vector", "G": "gpsimd"}
+        engine = {"S": "scalar", "V": "vector"}
         ring = {"b": [0, 1, 2, 3], "rest": [4, 5, 6, 7]}
         turn = {}
         holder = {"hs_in": [("sort_hs", g) for g in range(NG)]}
@@ -434,8 +390,16 @@ def tile_rpa_density_step_s12_kernel(tc, d, b, gap, h_words, h_scales, x_words, 
             return [("turn_b", n, 1)] if what == "b" else [("turn_d", n)]
 
         def plan_load(what, n):
-            fn = load_b if what == "b" else load_d if n < FIRST_BLOCK else load_blocks
-            buffered("sync", ("load", what, n), [], "rows", rows_read(what, n), fn, n)
+            if what == "d" and n >= FIRST_BLOCK:
+                buffered("sync", ("load", what, n), [], "rows", rows_read(what, n), load_blocks, n)
+            else:
+                buffered("sync", ("load", what, n), [], "rows", rows_read(what, n), load_rows, what, n)
+
+        def plan_load_h(g):
+            step("sync", ("load_h", g), [], load_h, g)
+
+        def plan_sort_h(g):
+            step("vector", ("sort_h", g), [("load_h", g)], sort_h, g)
 
         def plan_sort(what, n, eng, pieces=((0, 2),)):
             readers = [("turn_b", n, 1)] if what == "b" else [("turn_d", n)]
@@ -448,22 +412,14 @@ def tile_rpa_density_step_s12_kernel(tc, d, b, gap, h_words, h_scales, x_words, 
                 return [("load_half", h)]
             return [("sort", what, n, h) if (what, n) in SORTED else ("load", what, n)]
 
-        def plan_turn_b(i, halves=(0, 1)):
-            for h in halves:
-                tensor_step("b", ("turn_b", i, h), ready("b", i, h), [("evict_b" if i in POOL_TILES else "scale_b", i, h)], turn_b, i, h)
-
-        def plan_scale_b(i, h):
-            tag = "b_t" if i % 4 == 0 else None
-            buffered("vector", ("scale_b", i, h), [("turn_b", i, h), "ginv"], tag, [("quant_b", i // 4, h)], scale_b, i, h)
-
-        def plan_evict_b(i):
+        def plan_turn_b(i):
             for h in range(2):
-                buffered("scalar", ("evict_b", i, h), [("turn_b", i, h)], "b_raw" if h == 0 else None, [("scale_b", i, 1)], evict_b, i, h)
+                tensor_step("b", ("turn_b", i, h), ready("b", i, h), [("scale_b", i, h)], turn_b, i, h)
 
-        def plan_scale_raw(i):
-            for j in range(NJ):
-                key = ("scale_b", i, j // 2) if j % 2 else ("scale_raw", i, j)
-                step("gpsimd", key, [("evict_b", i, j // 2), ("scale_b", i - i % 4, j // 2)], scale_raw, i, j)
+        def plan_scale_b(i, which=(0, 1)):
+            for h in which:
+                tag = "b_t" if i % 4 == 0 else None
+                buffered("vector", ("scale_b", i, h), [("turn_b", i, h), "ginv"], tag, [("quant_b", i // 4, h)], scale_b, i, h)
 
         def plan_quant_b(g, h):
             step("vector", ("quant_b", g, h), [("scale_b", 4 * g + c, h) for c in range(4)], quant_b, g, h)
@@ -474,39 +430,36 @@ def tile_rpa_density_step_s12_kernel(tc, d, b, gap, h_words, h_scales, x_words, 
         def plan_fill_d(r):
             for h in range(2):
                 tag = "d_t" if r % 2 == 0 and h == 0 else None
-                buffered("scalar", ("d_t", r, h), [("turn_d", r)], tag, [("quant_d", r // 2, 0), ("quant_d", r // 2, 1)], evict_d, r, h)
+                buffered("scalar", ("d_t", r, h), [("turn_d", r)], tag, [("quant_d", r // 2)], evict_d, r, h)
 
         def plan_weave_blocks(r, eng):
             needs = [("turn_blocks", r)] + ([("d_t", r - 1, 0)] if r % 2 else [])
             tag = ("d_t" if eng == "S" else "b_t") if r % 2 == 0 else None
-            buffered(engine[eng], [("d_t", r, 0), ("d_t", r, 1)], needs, tag, [("quant_d", r // 2, 0), ("quant_d", r // 2, 1)], weave_blocks, r, eng)
+            buffered(engine[eng], [("d_t", r, 0), ("d_t", r, 1)], needs, tag, [("quant_d", r // 2)], weave_blocks, r, eng)
 
-        def plan_sort_blocks(r, eng):
-            buffered(engine[eng], ("sort", "d", r, 1), [("load", "d", r)], "sorted" + eng, [("turn_blocks", r)], sort_blocks, r, eng)
+        def plan_sort_blocks(r):
+            buffered("scalar", ("sort", "d", r, 1), [("load", "d", r)], "sortedS", [("turn_blocks", r)], sort_blocks, r)
 
         def plan_turn_blocks(r):
             buffered("vector", ("turn_blocks", r), [("sort", "d", r, 1)], "d_flip", [("d_t", r, 0), ("d_t", r, 1)], turn_blocks, r)
 
-        def plan_quant_d(q, first=0, count=2):
-            halves = range(first, first + count)
-            step("vector", [("quant_d", q, h) for h in halves], [("d_t", 2 * q + e, h) for e in range(2) for h in halves], quant_d, q, first, count)
+        def plan_quant_d(q):
+            step("vector", ("quant_d", q), [("d_t", 2 * q + e, h) for e in range(2) for h in range(2)], quant_d, q)
 
         def plan_trial(g, t):
-            tensor_step("rest", ("mul_t", g, t), [("sort_h", g), ("sort_hs", g)], [("scale_t", g, t)], mul_t, g, t)
+            tensor_step("rest", ("mul_t", g, t), [("sort_h", g), ("sort_hs", g), "load_x", "load_xs"], [("scale_t", g, t)], mul_t, g, t)
 
         def plan_scale_t(g, t):
             step("scalar", ("scale_t", g, t), [("mul_t", g, t), "coul_col"], scale_t, g, t)
 
-        def plan_weave_p(g, eng="V", first=0, count=4, behind=()):
-            keys = [("weave_p", g, n) for n in range(first, first + count)]
-            needs = [("scale_t", g, t) for t in range(4)] + list(behind)
-            buffered(engine[eng], keys, needs, "pot" if first == 0 else None, [("quant_p", g)], weave_p, g, first, count, eng)
+        def plan_weave_p(g):
+            buffered("vector", ("weave_p", g), [("scale_t", g, t) for t in range(4)], "pot", [("quant_p", g)], weave_p, g)
 
         def plan_quant_p(g):
-            step("vector", ("quant_p", g), [("weave_p", g, n) for n in range(4)], quant_p, g)
+            step("vector", ("quant_p", g), [("weave_p", g)], quant_p, g)
 
         def plan_response(q, s, first=0, count=2):
-            needs = [("quant_b", s // 2, 0), ("quant_b", s // 2, 1), ("quant_d", q, 0), ("quant_d", q, 1)]
+            needs = [("quant_b", s // 2, 0), ("quant_b", s // 2, 1), ("quant_d", q)]
             keys = [("mul_c", q, s, e) for e in range(first, first + count)]
             tensor_step("rest", keys, needs, [("evict_c", q, s, first + count - 1)], mul_c, q, s, first, count)
 
@@ -539,133 +492,86 @@ def tile_rpa_density_step_s12_kernel(tc, d, b, gap, h_words, h_scales, x_words, 
             halves_of_row = range(first, first + count)
             step("sync", [("store", r, n) for n in halves_of_row], [("evict_o", r, n) for n in halves_of_row], store, r, first, count)
 
+        last = NQ - 1
+        in_halves = ((0, 1), (1, 1))
+
         step("sync", "gap", [], load_gap)
         step("gpsimd", "coul", [], load_coul)
-        buffered("sync", ("load_half", 0), [], "first", [("turn_b", 0, 0)], load_half, 0)
-        buffered("sync", ("load_half", 1), [], "first", [("turn_b", 0, 1)], load_half, 1)
+        for h in range(2):
+            buffered("sync", ("load_half", h), [], "first", [("turn_b", 0, h)], load_half, h)
         plan_load("b", 1)
-        step("sync", "load_hs", [], load_scales, nc.sync, hs_in, h_scales)
-        step("sync", ("load_h", 0), [], load_h, 0)
+        step("sync", "load_hs", [], load_scales, hs_in, h_scales)
+        plan_load_h(0)
         step("sync", "load_x", [], load_x)
         plan_load("b", 2)
-        step("sync", "load_xs", [], load_scales, nc.sync, x_s[:].bitcast(I32), x_scales)
+        step("sync", "load_xs", [], load_scales, x_s[:].bitcast(I32), x_scales)
         plan_load("b", 3)
-        step("sync", ("load_h", 1), [], load_h, 1)
-        plan_load("b", 4)
-        plan_load("d", 0)
-        plan_load("b", 5)
-        plan_load("d", 1)
-        plan_load("b", 6)
-        plan_load("d", 2)
-        plan_load("d", 3)
-        plan_load("b", 7)
-        plan_load("d", 4)
-        plan_load("d", 5)
-        plan_load("d", 6)
-        plan_load("d", 7)
-        plan_load("d", 8)
-        plan_load("d", 9)
-        plan_load("d", 10)
-        plan_load("d", 11)
-        buffered("sync", ("load_n0", 0), [], "rows", [("evict_o", 3, 1)], load_n0, 0)
-        buffered("sync", ("load_n0", 1), [], "rows", [("evict_o", 7, 1)], load_n0, 1)
-        buffered("sync", ("load_n0", 2), [], "rows", [("evict_o", 11, 1)], load_n0, 2)
+        plan_load_h(1)
+        for what, n in [("b", 4), ("d", 0), ("b", 5), ("d", 1), ("b", 6), ("d", 2), ("d", 3), ("b", 7)]:
+            plan_load(what, n)
+        for r in range(4, ND):
+            plan_load("d", r)
+        for c in range(ND // 4):
+            buffered("sync", ("load_n0", c), [], "rows", [("evict_o", 4 * c + 3, 1)], load_n0, c)
         for r in range(ND - 1):
             plan_store(r)
-        plan_store(ND - 1, 0, 1)
-        plan_store(ND - 1, 1, 1)
+        for first, count in in_halves:
+            plan_store(ND - 1, first, count)
 
         plan_turn_b(0)
         plan_turn_b(1)
         tensor_step("rest", "turn_coul", ["coul_rows"], ["coul_col"], turn_coul)
         tensor_step("rest", "warm_up", [("sort_h", 0), ("sort_hs", 0)], ["warm_up"], warm_up)
         plan_turn_b(2)
-        plan_trial(0, 0)
-        plan_trial(0, 1)
-        plan_turn_b(3)
-        plan_trial(0, 2)
-        plan_trial(0, 3)
-        plan_turn_b(4)
-        plan_trial(1, 0)
-        plan_trial(1, 1)
-        plan_turn_d(0)
-        plan_turn_b(5)
-        plan_turn_d(1)
-        plan_trial(1, 2)
-        plan_trial(1, 3)
-        plan_turn_b(6)
-        plan_turn_d(2)
-        plan_turn_d(3)
-        plan_turn_b(7)
-        plan_response(0, 0)
-        plan_response(0, 1)
-        plan_turn_d(4)
-        plan_turn_d(5)
+        runs = [[("b", 3)], [("b", 4)], [("d", 0), ("b", 5), ("d", 1)], [("b", 6), ("d", 2), ("d", 3), ("b", 7)], [("d", 4), ("d", 5)]]
+        for n, run in enumerate(runs):
+            for e in range(2):
+                if n < 2 * NG:
+                    plan_trial(n // 2, 2 * (n % 2) + e)
+                else:
+                    plan_response(0, e)
+            for what, tile in run:
+                (plan_turn_b if what == "b" else plan_turn_d)(tile)
         plan_response(1, 0)
         ring["rest"] = [0, 1] + [4 + (turn["rest"] + k) % 4 for k in range(4)] + [2, 3]
         turn["rest"] = 0
         plan_response(1, 1)
-        plan_response(0, 2)
-        plan_response(0, 3)
-        plan_response(1, 2)
-        plan_response(1, 3)
-        plan_response(2, 0)
-        plan_response(2, 1)
-        plan_response(2, 2)
-        plan_response(2, 3)
-        plan_response(3, 0)
-        plan_response(3, 1)
-        plan_response(3, 2)
-        plan_response(3, 3)
-        plan_response(4, 0)
-        plan_response(4, 1)
-        plan_response(4, 2)
-        plan_response(4, 3)
-        plan_induced(0)
-        plan_induced(1)
-        plan_response(5, 0)
-        plan_induced(2)
-        plan_induced(3)
-        plan_response(5, 1)
-        plan_induced(4)
-        plan_induced(5)
-        plan_response(5, 2)
-        plan_induced(6)
-        plan_induced(7)
-        plan_induced(8)
-        plan_response(5, 3, 0, 1)
-        plan_response(5, 3, 1, 1)
-        plan_induced(9)
-        plan_induced(10)
-        plan_induced(11)
+        early = [(q, s) for q in range(2) for s in (2, 3)]
+        whole = [(q, s) for q in range(2, last) for s in range(NS)]
+        for q, s in early + whole:
+            plan_response(q, s)
+        for s in range(NS - 1):
+            plan_induced(2 * s)
+            plan_induced(2 * s + 1)
+            plan_response(last, s)
+        for r in range(2 * NS - 2, ND - 3):
+            plan_induced(r)
+        for first, count in in_halves:
+            plan_response(last, NS - 1, first, count)
+        for r in range(ND - 3, ND):
+            plan_induced(r)
 
         step("vector", "ginv", ["gap"], invert_gap)
-        plan_scale_b(0, 0)
-        plan_scale_b(0, 1)
-        step("vector", ("sort_hs", 0), ["load_hs", "load_x", "load_xs"], sort_hs, 0)
-        step("vector", ("sort_hs", 1), ["load_hs", "load_x", "load_xs"], sort_hs, 1)
-        step("vector", ("sort_h", 0), [("load_h", 0)], sort_h, 0)
-        plan_scale_b(1, 0)
-        plan_scale_b(1, 1)
-        plan_scale_b(2, 0)
-        plan_scale_b(2, 1)
-        step("vector", ("sort_h", 1), [("load_h", 1)], sort_h, 1)
-        plan_scale_b(3, 0)
-        plan_scale_b(3, 1)
+        plan_scale_b(0)
+        for g in range(NG):
+            step("vector", ("sort_hs", g), ["load_hs"], sort_hs, g)
+        plan_sort_h(0)
+        plan_scale_b(1)
+        plan_scale_b(2)
+        plan_sort_h(1)
+        plan_scale_b(3)
         plan_quant_b(0, 0)
         plan_sort("b", 5, "V")
         plan_quant_b(0, 1)
-        plan_scale_b(4, 0)
+        plan_scale_b(4, (0,))
         plan_sort("b", 6, "V")
-        plan_scale_b(4, 1)
-        plan_scale_b(5, 0)
-        plan_scale_b(5, 1)
+        plan_scale_b(4, (1,))
+        plan_scale_b(5)
         plan_quant_d(0)
-        plan_scale_b(6, 0)
-        plan_scale_b(6, 1)
-        plan_scale_b(7, 0)
+        plan_scale_b(6)
+        plan_scale_b(7, (0,))
         plan_quant_d(1)
-        plan_scale_b(7, 1)
+        plan_scale_b(7, (1,))
         plan_quant_b(1, 0)
         plan_quant_b(1, 1)
         plan_quant_d(2)
@@ -686,35 +592,30 @@ def tile_rpa_density_step_s12_kernel(tc, d, b, gap, h_words, h_scales, x_words, 
         plan_weave_c(0)
         plan_weave_c(1)
         plan_quant_c(0)
-        plan_quant_d(5)
+        plan_quant_d(last)
         plan_quant_c(1)
         plan_weave_c(2)
         plan_evict_o(0)
         plan_quant_c(2)
-        plan_evict_o(1)
-        plan_weave_c(3)
-        plan_evict_o(2)
-        plan_quant_c(3)
-        plan_evict_o(3)
-        plan_weave_c(4)
-        plan_evict_o(4)
-        plan_quant_c(4)
+        for q in range(3, last):
+            plan_evict_o(2 * q - 5)
+            plan_weave_c(q)
+            plan_evict_o(2 * q - 4)
+            plan_quant_c(q)
         plan_evict_o(5)
-        plan_quant_c(5, 0, 2)
-        plan_evict_o(6)
-        plan_evict_o(7)
-        plan_evict_o(8)
-        plan_quant_c(5, 2, 1)
-        plan_evict_o(9)
-        plan_quant_c(5, 3, 1)
-        plan_evict_o(10)
-        plan_evict_o(11, 0, 1)
-        plan_evict_o(11, 1, 1)
+        plan_quant_c(last, 0, 2)
+        for r in range(6, ND - 3):
+            plan_evict_o(r)
+        for e in range(2):
+            plan_quant_c(last, 2 + e, 1)
+            plan_evict_o(ND - 3 + e)
+        for first, count in in_halves:
+            plan_evict_o(ND - 1, first, count)
 
-        plan_sort("b", 1, "S", ((0, 1), (1, 1)))
+        plan_sort("b", 1, "S", in_halves)
         step("scalar", "coul_rows", ["coul"], widen_coul)
         step("scalar", "coul_col", ["turn_coul"], evict_coul)
-        plan_sort("b", 3, "S", ((0, 1), (1, 1)))
+        plan_sort("b", 3, "S", in_halves)
         plan_scale_t(0, 0)
         plan_scale_t(0, 1)
         plan_sort("b", 4, "S")
@@ -736,39 +637,24 @@ def tile_rpa_density_step_s12_kernel(tc, d, b, gap, h_words, h_scales, x_words, 
         plan_evict_pairs(0, 1)
         plan_fill_d(4)
         plan_fill_d(5)
-        plan_sort_blocks(6, "S")
-        plan_evict_pairs(1, 0)
-        plan_sort_blocks(7, "S")
-        plan_evict_pairs(1, 1)
-        plan_evict_pairs(0, 2)
-        plan_sort_blocks(8, "S")
-        plan_evict_pairs(0, 3)
-        plan_sort_blocks(9, "S")
-        plan_evict_pairs(1, 2)
-        plan_evict_pairs(1, 3)
-        plan_sort_blocks(10, "S")
-        plan_weave_blocks(8, "S")
-        plan_evict_pairs(2, 0)
-        plan_weave_blocks(9, "S")
-        plan_sort_blocks(11, "S")
-        plan_evict_pairs(2, 1)
-        plan_evict_pairs(2, 2)
-        plan_weave_blocks(10, "S")
-        plan_evict_pairs(2, 3)
-        plan_weave_blocks(11, "S")
-        plan_evict_pairs(3, 0)
-        plan_evict_pairs(3, 1)
-        plan_evict_pairs(3, 2)
-        plan_evict_pairs(3, 3)
-        plan_evict_pairs(4, 0)
-        plan_evict_pairs(4, 1)
-        plan_evict_pairs(4, 2)
-        plan_evict_pairs(4, 3)
-        plan_evict_c(5, 0)
-        plan_evict_c(5, 1)
-        plan_evict_c(5, 2)
-        plan_evict_c(5, 3, 0, 1)
-        plan_evict_c(5, 3, 1, 1)
+        ahead = {
+            (1, 0): [(plan_sort_blocks, 6)],
+            (1, 1): [(plan_sort_blocks, 7)],
+            (0, 3): [(plan_sort_blocks, 8)],
+            (1, 2): [(plan_sort_blocks, 9)],
+            (2, 0): [(plan_sort_blocks, 10), (plan_weave_blocks, 8, "S")],
+            (2, 1): [(plan_weave_blocks, 9, "S"), (plan_sort_blocks, 11)],
+            (2, 3): [(plan_weave_blocks, 10, "S")],
+            (3, 0): [(plan_weave_blocks, 11, "S")],
+        }
+        for q, s in [(1, 0), (1, 1)] + early + whole:
+            for job in ahead.get((q, s), []):
+                job[0](*job[1:])
+            plan_evict_pairs(q, s)
+        for s in range(NS - 1):
+            plan_evict_c(last, s)
+        for first, count in in_halves:
+            plan_evict_c(last, NS - 1, first, count)
 
         with tc.manual_schedule():
             nc.vector.memset(hs_in[:], 0)

@@ -19,22 +19,26 @@ ACT = mybir.ActivationFunctionType
 NJ = T // 512
 NF = F // 512
 NG = A // 512
-NS = 2 * NG
+NB = A // 128
+NS = NB // 2
 ND = R // 128
 NQ = ND // 2
 FIRST_BLOCK = 6
-SORTED = {("b", i) for i in (1, 3, 4, 5, 6)} | {("d", r) for r in (0, 1, 2, 4)}
+FIRST_DIRECT = 5
 WARM_UPS = 3
-DEPTH = {"rows": 9, "sortedS": 3, "sortedV": 2, "b_t": 3, "d_t": 3, "res": 3, "chi": 5}
+SORTER = {**{("b", i): "S" for i in (1, 3, 4)}, ("b", 5): "V", **{("d", r): "S" for r in range(ND) if r not in (3, 5)}}
+DEPTH = {"rows": 9, "sortedS": 4, "sortedV": 2, "wide": 3, "d_t": 3, "chi": 5, "first": 2}
 OWN = {tag: [f"{tag}{k}" for k in range(n)] for tag, n in DEPTH.items()}
 RINGS = {
     **OWN,
-    "first": OWN["res"][:2],
-    "res": OWN["sortedV"] + OWN["res"],
-    "d_flip": ["h_in0", "h_in1"],
-    "pot": ["hs_in"],
+    "res": OWN["first"] + OWN["sortedV"] + ["x_w", "pot_s0", "pot_s1"],
+    "d_flip": ["h_in0", "h_in1", "flip2"],
     "chi": OWN["chi"] + ["h_w0"],
+    "woven": OWN["wide"],
+    "ccodes": ["dcodes0", "dcodes1", "dcodes2"],
 }
+POT_PLACE = [("wide1", ("quant_b", 0, 1)), ("d_t0", ("quant_d", 0))]
+POT_FIRST = {"V": [("quant_p", 0)], "S": [("quant_p", 1)]}
 
 
 def tile_rpa_density_step_s12_kernel(tc, d, b, gap, h_words, h_scales, x_words, x_scales, coul, n0, out):
@@ -43,36 +47,35 @@ def tile_rpa_density_step_s12_kernel(tc, d, b, gap, h_words, h_scales, x_words, 
         keep = ctx.enter_context(tc.tile_pool(name="keep", bufs=1))
         psum = ctx.enter_context(tc.psum_pool(name="psum", bufs=1))
 
-        ident = keep.tile([128, 128], F32, name="ident")
-        gap_in = keep.tile([128, NJ, 4], BF16, name="gap_in")
-        coul_in = keep.tile([128, NG, 128], BF16, name="coul_in")
-        coul_rows = keep.tile([128, NG, 128], F32, name="coul_rows")
-        ginv = keep.tile([128, NJ, 4], F32, name="ginv")
-        coul_col = keep.tile([128, NG, 4], F32, name="coul_col")
-        x_w = keep.tile([128, NF, 2 * P], U8, name="x_w", align_bytes=64)
-        x_s = keep.tile([128, NF, P], U8, name="x_s", align_bytes=64)
-        h_in = [keep.tile([128, NF, 256], I32, name=f"h_in{g}", align_bytes=64) for g in range(NG)]
-        hs_in = keep.tile([128, NF, A // 4], I32, name="hs_in", align_bytes=64)
-        h_w = [keep.tile([128, NF, 4, 256], U8, name=f"h_w{g}", align_bytes=64) for g in range(NG)]
-        h_s = [keep.tile([128, NF, 4, 128], U8, name=f"h_s{g}", align_bytes=64) for g in range(NG)]
-        bcodes = [[keep.tile([128, 2, 4, 128], U32, name=f"bcodes{g}_{h}", align_bytes=64) for h in range(2)] for g in range(NG)]
-        bscale = [[keep.tile([128, 2, 4, 128], U8, name=f"bscale{g}_{h}", align_bytes=64) for h in range(2)] for g in range(NG)]
-        dcodes = [keep.tile([128, NJ, 256], U32, name=f"dcodes{q}", align_bytes=64) for q in range(NQ)]
-        dscale = [keep.tile([128, NJ, 256], U8, name=f"dscale{q}", align_bytes=64) for q in range(NQ)]
-        pot_s = [keep.tile([128, 4, P], BF16, name=f"pot_s{g}") for g in range(NG)]
-        pcodes = [keep.tile([128, P], U32, name=f"pcodes{g}", align_bytes=64) for g in range(NG)]
-        pscale = [keep.tile([128, P], U8, name=f"pscale{g}", align_bytes=64) for g in range(NG)]
-        ccodes = [keep.tile([128, NG, 256], U32, name=f"ccodes{q}", align_bytes=64) for q in range(NQ)]
-        cscale = [keep.tile([128, NG, 256], U8, name=f"cscale{q}", align_bytes=64) for q in range(NQ)]
-
-        halves, rows, n0_sb, perm, b_t, d_t, d_flip, pot, chi_pairs, chi, res = {}, {}, {}, {}, {}, {}, {}, {}, {}, {}, {}
-        tr_coul, tr_b, tr_d, ps_t, ps_c, ps_o = {}, {}, {}, {}, {}, {}
-
         def buf(name, shape, dtype):
             return keep.tile(shape, dtype, name=name, align_bytes=64)
 
         def bank(n, shape):
             return psum.tile(shape, F32, name=f"bank{n}")
+
+        ident = buf("ident", [128, 128], F32)
+        gap_in = buf("gap_in", [128, NJ, 4], BF16)
+        coul_in = buf("coul_in", [128, NG, 128], BF16)
+        coul_rows = buf("coul_rows", [128, NG, 128], F32)
+        ginv = buf("ginv", [128, NJ, 4], F32)
+        coul_col = buf("coul_col", [128, NG, 4], F32)
+        x_w = buf("x_w", [128, NF, 2 * P], U8)
+        x_s = buf("x_s", [128, NF, P], U8)
+        h_in = [buf(f"h_in{g}", [128, NF, 256], I32) for g in range(NG)]
+        hs_in = buf("hs_in", [128, NF, 256], I32)
+        h_w = [buf(f"h_w{g}", [128, NF, 4, 256], U8) for g in range(NG)]
+        h_s = [buf(f"h_s{g}", [128, NF, 4, 128], U8) for g in range(NG)]
+        bcodes = [[buf(f"bcodes{g}_{h}", [128, 2, 4, 128], U32) for h in range(2)] for g in range(NG)]
+        bscale = [[buf(f"bscale{g}_{h}", [128, 2, 4, 128], U8) for h in range(2)] for g in range(NG)]
+        dcodes = [buf(f"dcodes{q}", [128, NJ, 256], U32) for q in range(NQ)]
+        dscale = [buf(f"dscale{q}", [128, NJ, 256], U8) for q in range(NQ)]
+        pot_s = [buf(f"pot_s{g}", [128, 4, P], BF16) for g in range(NG)]
+        pcodes = [buf(f"pcodes{g}", [128, P], U32) for g in range(NG)]
+        pscale = [buf(f"pscale{g}", [128, P], U8) for g in range(NG)]
+        cscale = [buf(f"cscale{q}", [128, NG, 256], U8) for q in range(NQ)]
+
+        halves, rows, n0_sb, perm, b_t, d_t, d_flip, pot, chi_pairs, chi, ccodes, res = {}, {}, {}, {}, {}, {}, {}, {}, {}, {}, {}, {}
+        tr_coul, tr_b, tr_d, ps_t, ps_c, ps_o = {}, {}, {}, {}, {}, {}
 
         def copy(eng, dst, src):
             if eng == "S":
@@ -100,9 +103,9 @@ def tile_rpa_density_step_s12_kernel(tc, d, b, gap, h_words, h_scales, x_words, 
 
         def load_scales(plane, scales):
             for r in range(4):
-                nc.sync.dma_start(out=plane[r:128:32], in_=scales.bitcast(I32)[:, r:16:4, :].rearrange("j Q n -> Q j n"))
+                nc.sync.dma_start(out=plane[r:128:32], in_=scales[:, r:16:4, :].rearrange("j Q n -> Q j n"))
 
-        def sort_rows(name, what, n, first, count, eng):
+        def sort_rows(name, what, n, eng, first, count):
             if name is not None:
                 perm[what, n] = buf(name, [128, 2, 2, T // 8], F32)
             pairs = rows[what, n][:].bitcast(F32)[:, 512 * first : 512 * (first + count)]
@@ -115,7 +118,7 @@ def tile_rpa_density_step_s12_kernel(tc, d, b, gap, h_words, h_scales, x_words, 
         def pairs_of(what, n, h, jj, u):
             if (what, n) == ("b", 0):
                 return halves[h][:].bitcast(F32)[:, 256 * jj + u : 256 * (jj + 1) : 2]
-            if (what, n) in SORTED:
+            if (what, n) in SORTER:
                 return perm[what, n][:, h, u, 128 * jj : 128 * (jj + 1)]
             return rows[what, n][:].bitcast(F32)[:, 512 * h + 256 * jj + u : 512 * h + 256 * (jj + 1) : 2]
 
@@ -144,16 +147,18 @@ def tile_rpa_density_step_s12_kernel(tc, d, b, gap, h_words, h_scales, x_words, 
                 in_=b_t[g, h][:].rearrange("p j t m e -> p (j t m e)"),
             )
 
-        def sort_h(g):
-            nc.vector.tensor_copy(
-                out=h_w[g][:].bitcast(I32).rearrange("p j t (q w) -> p q j t w", w=4),
-                in_=h_in[g][:].rearrange("p j (q t w) -> p q j t w", t=4, w=4),
+        def sort_h(g, eng):
+            copy(
+                eng,
+                h_w[g][:].bitcast(U32 if eng == "S" else I32).rearrange("p j t (q w) -> p q j t w", w=4),
+                h_in[g][:].bitcast(U32 if eng == "S" else I32).rearrange("p j (q t w) -> p q j t w", t=4, w=4),
             )
 
-        def sort_hs(g):
-            nc.vector.tensor_copy(
-                out=h_s[g][:].bitcast(I32).rearrange("p j t (q w) -> p j q t w", w=2),
-                in_=hs_in[:, :, 128 * g : 128 * (g + 1)].rearrange("p j (q t w) -> p j q t w", t=4, w=2),
+        def sort_hs(g, eng):
+            copy(
+                eng,
+                h_s[g][:].bitcast(U32 if eng == "S" else I32).rearrange("p j t (q w) -> p j q t w", w=2),
+                hs_in[:, :, 128 * g : 128 * (g + 1)].bitcast(U32 if eng == "S" else I32).rearrange("p j (q t w) -> p j q t w", t=4, w=2),
             )
 
         def mul_t(banks, g, t):
@@ -176,8 +181,8 @@ def tile_rpa_density_step_s12_kernel(tc, d, b, gap, h_words, h_scales, x_words, 
                     out=spare[:],
                     lhsT=h_w[0][:, 0, 0, :].bitcast(FP4X4),
                     lhsT_scale=h_s[0][:, 0, 0, :],
-                    rhs=h_w[0][:, 0].rearrange("p t m -> p (t m)").bitcast(FP4X4),
-                    rhs_scale=h_s[0][:, 0].rearrange("p t m -> p (t m)"),
+                    rhs=h_w[0][:, 0].rearrange("p t n -> p (t n)").bitcast(FP4X4),
+                    rhs_scale=h_s[0][:, 0].rearrange("p t n -> p (t n)"),
                     start=True,
                     stop=True,
                 )
@@ -185,9 +190,12 @@ def tile_rpa_density_step_s12_kernel(tc, d, b, gap, h_words, h_scales, x_words, 
         def scale_t(g, t):
             nc.scalar.activation(out=pot_s[g][:, t, :], in_=ps_t[g, t][:], func=ACT.Copy, scale=coul_col[:, g, t : t + 1])
 
-        def weave_p(name, g):
+        def weave_p(name, g, eng):
             pot[g] = buf(name, [128, P, 4], BF16)
-            nc.vector.tensor_copy(out=pot[g][:].rearrange("p (c i) t -> p c t i", i=4), in_=pot_s[g][:].rearrange("p t (c i) -> p c t i", i=4))
+            if eng == "G":
+                nc.gpsimd.tensor_scalar(out=pot[g][:], in0=pot_s[g][:].rearrange("p t n -> p n t"), scalar1=1.0, scalar2=0.0, op0=ALU.mult, op1=ALU.add)
+            else:
+                copy(eng, pot[g][:].rearrange("p (c i) t -> p c t i", i=4), pot_s[g][:].rearrange("p t (c i) -> p c t i", i=4))
 
         def quant_p(g):
             nc.vector.quantize_mx(out=pcodes[g][:].bitcast(FP8X4), scales=pscale[g][:], in_=pot[g][:].rearrange("p n t -> p (n t)"))
@@ -203,7 +211,11 @@ def tile_rpa_density_step_s12_kernel(tc, d, b, gap, h_words, h_scales, x_words, 
             q = r // 2
             if name is not None:
                 d_t[q] = buf(name, [128, NJ, 256, 2], F32)
-            nc.scalar.copy(out=d_t[q][:, 2 * h : 2 * h + 2, 128 * (r % 2) : 128 * (r % 2) + 128, :], in_=tr_d[r, h][:].rearrange("p j u a -> p j a u"))
+            words = d_t[q][:, 2 * h : 2 * h + 2, 128 * (r % 2) : 128 * (r % 2) + 128, :]
+            if 2 * q + 1 >= FIRST_BLOCK:
+                nc.scalar.copy(out=words.rearrange("p j (c i) u -> p j c i u", c=4), in_=tr_d[r, h][:].rearrange("p j u (i c) -> p j c i u", c=4))
+            else:
+                nc.scalar.copy(out=words, in_=tr_d[r, h][:].rearrange("p j u a -> p j a u"))
 
         def load_blocks(name, r):
             rows["d", r] = buf(name, [128, 4, NJ, 128], BF16)
@@ -211,11 +223,12 @@ def tile_rpa_density_step_s12_kernel(tc, d, b, gap, h_words, h_scales, x_words, 
             for s in (0, 2, 1, 3):
                 nc.sync.dma_start(out=rows["d", r][32 * s : 32 * (s + 1)], in_=src[s])
 
-        def sort_blocks(name, r):
+        def sort_blocks(name, r, eng):
             perm["d", r] = buf(name, [128, 16, 2, 32], F32)
-            nc.scalar.copy(
-                out=perm["d", r][:].rearrange("p n u (a i) -> p n a u i", i=4),
-                in_=rows["d", r][:].rearrange("p c j k -> p (c j k)").bitcast(F32).rearrange("p (n a i u) -> p n a u i", n=16, i=4, u=2),
+            copy(
+                eng,
+                perm["d", r][:].rearrange("p n u (a i) -> p n a u i", i=4),
+                rows["d", r][:].rearrange("p c j k -> p (c j k)").bitcast(F32).rearrange("p (n a i u) -> p n a u i", n=16, i=4, u=2),
             )
 
         def turn_blocks(name, r):
@@ -257,7 +270,7 @@ def tile_rpa_density_step_s12_kernel(tc, d, b, gap, h_words, h_scales, x_words, 
                     )
 
         def in_row_order(q, sums):
-            if 2 * q >= FIRST_BLOCK:
+            if 2 * q + 1 >= FIRST_BLOCK:
                 return sums.rearrange("p e (n c i) -> p n i c e", c=4, i=32)
             return sums.rearrange("p e (n i c) -> p n i c e", c=4, i=32)
 
@@ -274,14 +287,17 @@ def tile_rpa_density_step_s12_kernel(tc, d, b, gap, h_words, h_scales, x_words, 
                 chi_pairs[q] = buf(name, [128, 2, NG, 256, 2], BF16)
             nc.scalar.copy(out=chi_pairs[q][:, tp, g].rearrange("p (n i c) e -> p n i c e", c=4, i=32), in_=in_row_order(q, ps_c[q, s, 0][:]))
 
-        def weave_c(name, q):
+        def weave_c(name, q, eng):
             chi[q] = buf(name, [128, NG, 256, 4], BF16)
-            nc.vector.tensor_copy(
-                out=chi[q][:].rearrange("p g a t -> p (g a t)").bitcast(F32).rearrange("p (c i u) -> p c u i", i=4, u=2),
-                in_=chi_pairs[q][:].rearrange("p u g a e -> p u (g a e)").bitcast(F32).rearrange("p u (c i) -> p c u i", i=4),
+            copy(
+                eng,
+                chi[q][:].rearrange("p g a t -> p (g a t)").bitcast(F32).rearrange("p (c i u) -> p c u i", i=4, u=2),
+                chi_pairs[q][:].rearrange("p u g a e -> p u (g a e)").bitcast(F32).rearrange("p u (c i) -> p c u i", i=4),
             )
 
-        def quant_c(q, first, count):
+        def quant_c(name, q, first, count):
+            if name is not None:
+                ccodes[q] = buf(name, [128, NG, 256], U32)
             cols = slice(128 * first, 128 * (first + count))
             nc.vector.quantize_mx(
                 out=ccodes[q][:].rearrange("p g a -> p (g a)")[:, cols].bitcast(FP8X4),
@@ -338,10 +354,14 @@ def tile_rpa_density_step_s12_kernel(tc, d, b, gap, h_words, h_scales, x_words, 
         engine = {"S": "scalar", "V": "vector"}
         ring = {"b": [0, 1, 2, 3], "rest": [4, 5, 6, 7]}
         turn = {}
-        holder = {"hs_in": [("sort_hs", g) for g in range(NG)]}
+        holder = {}
         for g in range(NG):
             holder[f"h_in{g}"] = [("sort_h", g)]
             holder[f"h_w{g}"] = [("mul_t", g, 3)]
+            holder[f"pot_s{g}"] = [("weave_p", g)]
+        holder["x_w"] = [("mul_t", NG - 1, 3)]
+        for q in range(NQ):
+            holder[f"dcodes{q}"] = [("mul_c", q, NS - 1, 1)]
 
         def step(where, key, needs, fn, *args):
             queue[where].append((key, needs, fn, args))
@@ -382,50 +402,62 @@ def tile_rpa_density_step_s12_kernel(tc, d, b, gap, h_words, h_scales, x_words, 
                         at[where] = at[where] + 1
                 assert len(done) > before, [queue[w][at[w]][:2] for w in queue if at[w] < len(queue[w])]
 
-        def rows_read(what, n):
-            if what == "d" and n >= FIRST_BLOCK:
-                return [("sort", what, n, 1)]
-            if (what, n) in SORTED:
-                return [("sort", what, n, 0), ("sort", what, n, 1)]
+        def by_vector(what, n):
+            return what == "d" and n >= FIRST_BLOCK
+
+        def turned(what, n):
+            if by_vector(what, n):
+                return [("turn_blocks", n)]
             return [("turn_b", n, 1)] if what == "b" else [("turn_d", n)]
 
         def plan_load(what, n):
-            if what == "d" and n >= FIRST_BLOCK:
-                buffered("sync", ("load", what, n), [], "rows", rows_read(what, n), load_blocks, n)
+            readers = [("sort", what, n, 1)] if (what, n) in SORTER else turned(what, n)
+            if by_vector(what, n):
+                buffered("sync", ("load", what, n), [], "rows", readers, load_blocks, n)
             else:
-                buffered("sync", ("load", what, n), [], "rows", rows_read(what, n), load_rows, what, n)
+                buffered("sync", ("load", what, n), [], "rows", readers, load_rows, what, n)
 
         def plan_load_h(g):
             step("sync", ("load_h", g), [], load_h, g)
 
-        def plan_sort_h(g):
-            step("vector", ("sort_h", g), [("load_h", g)], sort_h, g)
+        def plan_load_hs():
+            step("sync", "load_hs", [], load_scales, hs_in, h_scales.bitcast(I32))
 
-        def plan_sort(what, n, eng, pieces=((0, 2),)):
-            readers = [("turn_b", n, 1)] if what == "b" else [("turn_d", n)]
+        def plan_sort_h(g, eng):
+            step(engine[eng], ("sort_h", g), [("load_h", g)], sort_h, g, eng)
+
+        def plan_sort_hs(g, eng):
+            step(engine[eng], ("sort_hs", g), ["load_hs"], sort_hs, g, eng)
+
+        def plan_sort(what, n, pieces=((0, 2),)):
+            eng = SORTER[what, n]
+            if by_vector(what, n):
+                buffered(engine[eng], ("sort", what, n, 1), [("load", what, n)], "sorted" + eng, turned(what, n), sort_blocks, n, eng)
+                return
             for first, count in pieces:
                 keys = [("sort", what, n, h) for h in range(first, first + count)]
-                buffered(engine[eng], keys, [("load", what, n)], "sorted" + eng if first == 0 else None, readers, sort_rows, what, n, first, count, eng)
+                tag = "sorted" + eng if first == 0 else None
+                buffered(engine[eng], keys, [("load", what, n)], tag, turned(what, n), sort_rows, what, n, eng, first, count)
 
         def ready(what, n, h):
             if (what, n) == ("b", 0):
                 return [("load_half", h)]
-            return [("sort", what, n, h) if (what, n) in SORTED else ("load", what, n)]
+            return [("sort", what, n, h) if (what, n) in SORTER else ("load", what, n)]
 
-        def plan_turn_b(i):
-            for h in range(2):
-                tensor_step("b", ("turn_b", i, h), ready("b", i, h), [("scale_b", i, h)], turn_b, i, h)
+        def plan_turn(what, n):
+            if what == "b":
+                for h in range(2):
+                    tensor_step("b", ("turn_b", n, h), ready("b", n, h), [("scale_b", n, h)], turn_b, n, h)
+            else:
+                tensor_step("rest", ("turn_d", n), ready("d", n, 1), [("d_t", n, 0), ("d_t", n, 1)], turn_d, n)
 
         def plan_scale_b(i, which=(0, 1)):
             for h in which:
-                tag = "b_t" if i % 4 == 0 else None
+                tag = "wide" if i % 4 == 0 else None
                 buffered("vector", ("scale_b", i, h), [("turn_b", i, h), "ginv"], tag, [("quant_b", i // 4, h)], scale_b, i, h)
 
         def plan_quant_b(g, h):
             step("vector", ("quant_b", g, h), [("scale_b", 4 * g + c, h) for c in range(4)], quant_b, g, h)
-
-        def plan_turn_d(r):
-            tensor_step("rest", ("turn_d", r), ready("d", r, 0) + ready("d", r, 1), [("d_t", r, 0), ("d_t", r, 1)], turn_d, r)
 
         def plan_fill_d(r):
             for h in range(2):
@@ -433,12 +465,9 @@ def tile_rpa_density_step_s12_kernel(tc, d, b, gap, h_words, h_scales, x_words, 
                 buffered("scalar", ("d_t", r, h), [("turn_d", r)], tag, [("quant_d", r // 2)], evict_d, r, h)
 
         def plan_weave_blocks(r, eng):
-            needs = [("turn_blocks", r)] + ([("d_t", r - 1, 0)] if r % 2 else [])
-            tag = ("d_t" if eng == "S" else "b_t") if r % 2 == 0 else None
+            needs = [("turn_blocks", r)] + POT_FIRST[eng] + ([("d_t", r - 1, 0)] if r % 2 else [])
+            tag = ("d_t" if eng == "S" else "wide") if r % 2 == 0 else None
             buffered(engine[eng], [("d_t", r, 0), ("d_t", r, 1)], needs, tag, [("quant_d", r // 2)], weave_blocks, r, eng)
-
-        def plan_sort_blocks(r):
-            buffered("scalar", ("sort", "d", r, 1), [("load", "d", r)], "sortedS", [("turn_blocks", r)], sort_blocks, r)
 
         def plan_turn_blocks(r):
             buffered("vector", ("turn_blocks", r), [("sort", "d", r, 1)], "d_flip", [("d_t", r, 0), ("d_t", r, 1)], turn_blocks, r)
@@ -452,33 +481,37 @@ def tile_rpa_density_step_s12_kernel(tc, d, b, gap, h_words, h_scales, x_words, 
         def plan_scale_t(g, t):
             step("scalar", ("scale_t", g, t), [("mul_t", g, t), "coul_col"], scale_t, g, t)
 
-        def plan_weave_p(g):
-            buffered("vector", ("weave_p", g), [("scale_t", g, t) for t in range(4)], "pot", [("quant_p", g)], weave_p, g)
+        def plan_weave_p(g, eng):
+            needs = [("scale_t", g, t) for t in range(4)]
+            if eng == "G":
+                name, freed_by = POT_PLACE[g]
+                step("gpsimd", ("weave_p", g), needs + [freed_by], weave_p, name, g, eng)
+            else:
+                buffered(engine[eng], ("weave_p", g), needs, "pot", [("quant_p", g)], weave_p, g, eng)
 
         def plan_quant_p(g):
             step("vector", ("quant_p", g), [("weave_p", g)], quant_p, g)
 
         def plan_response(q, s, first=0, count=2):
-            needs = [("quant_b", s // 2, 0), ("quant_b", s // 2, 1), ("quant_d", q)]
             keys = [("mul_c", q, s, e) for e in range(first, first + count)]
-            tensor_step("rest", keys, needs, [("evict_c", q, s, first + count - 1)], mul_c, q, s, first, count)
+            tensor_step("rest", keys, [("quant_b", s // 2, 0), ("quant_b", s // 2, 1), ("quant_d", q)], [("evict_c", q, s, first + count - 1)], mul_c, q, s, first, count)
 
         def plan_evict_c(q, s, first=0, count=2):
             keys = [("evict_c", q, s, e) for e in range(first, first + count)]
-            tag = "chi" if s == 0 and first == 0 else None
-            buffered("scalar", keys, [("mul_c", q, s, first)], tag, [("quant_c", q, n) for n in range(4)], evict_c, q, s, first, count)
+            if q >= FIRST_DIRECT:
+                tag = "chi" if s == 0 and first == 0 else None
+                buffered("scalar", keys, [("mul_c", q, s, first)], tag, [("quant_c", q, n) for n in range(4)], evict_c, q, s, first, count)
+            else:
+                buffered("scalar", keys, [("mul_c", q, s, 0)], "chi" if s == 0 else None, [("weave_c", q)], evict_pairs, q, s)
 
-        def plan_evict_pairs(q, s):
-            keys = [("evict_c", q, s, e) for e in range(2)]
-            buffered("scalar", keys, [("mul_c", q, s, 0)], "chi" if s == 0 else None, [("weave_c", q)], evict_pairs, q, s)
-
-        def plan_weave_c(q):
-            buffered("vector", ("weave_c", q), [("evict_c", q, s, 1) for s in range(NS)], "b_t", [("quant_c", q, 0)], weave_c, q)
+        def plan_weave_c(q, eng):
+            buffered(engine[eng], ("weave_c", q), [("evict_c", q, s, 1) for s in range(NS)], "woven", [("quant_c", q, 0)], weave_c, q, eng)
 
         def plan_quant_c(q, first=0, count=4):
             pieces = range(first, first + count)
-            needs = ([("weave_c", q)] if q < NQ - 1 else []) + [("evict_c", q, 2 * (n // 2) + tp, n % 2) for n in pieces for tp in range(2)]
-            step("vector", [("quant_c", q, n) for n in pieces], needs, quant_c, q, first, count)
+            needs = ([("weave_c", q)] if q < FIRST_DIRECT else []) + [("evict_c", q, 2 * (n // 2) + tp, n % 2) for n in pieces for tp in range(2)]
+            tag = "ccodes" if first == 0 else None
+            buffered("vector", [("quant_c", q, n) for n in pieces], needs, tag, [("mul_o", 2 * q + 1)], quant_c, q, first, count)
 
         def plan_induced(r):
             needs = [("quant_c", r // 2, r % 2), ("quant_c", r // 2, 2 + r % 2), ("quant_p", 0), ("quant_p", 1)]
@@ -494,171 +527,249 @@ def tile_rpa_density_step_s12_kernel(tc, d, b, gap, h_words, h_scales, x_words, 
 
         last = NQ - 1
         in_halves = ((0, 1), (1, 1))
+        def join_banks():
+            own = ring["rest"]
+            ring["rest"] = ring["b"][:2] + [own[(turn["rest"] + k) % 4] for k in range(4)] + ring["b"][2:]
+            turn["rest"] = 0
+
+        def after_head():
+            ring["b"], ring["rest"] = [4, 5, 6, 7], [1, 2, 3, 0]
+            turn["b"], turn["rest"] = 0, 0
 
         step("sync", "gap", [], load_gap)
-        step("gpsimd", "coul", [], load_coul)
-        for h in range(2):
-            buffered("sync", ("load_half", h), [], "first", [("turn_b", 0, h)], load_half, h)
+        buffered("sync", ("load_half", 0), [], "first", [("turn_b", 0, 0)], load_half, 0)
+        buffered("sync", ("load_half", 1), [], "first", [("turn_b", 0, 1)], load_half, 1)
         plan_load("b", 1)
-        step("sync", "load_hs", [], load_scales, hs_in, h_scales)
+        plan_load_hs()
         plan_load_h(0)
         step("sync", "load_x", [], load_x)
         plan_load("b", 2)
-        step("sync", "load_xs", [], load_scales, x_s[:].bitcast(I32), x_scales)
+        step("sync", "load_xs", [], load_scales, x_s[:].bitcast(I32), x_scales.bitcast(I32))
         plan_load("b", 3)
         plan_load_h(1)
-        for what, n in [("b", 4), ("d", 0), ("b", 5), ("d", 1), ("b", 6), ("d", 2), ("d", 3), ("b", 7)]:
-            plan_load(what, n)
-        for r in range(4, ND):
-            plan_load("d", r)
-        for c in range(ND // 4):
-            buffered("sync", ("load_n0", c), [], "rows", [("evict_o", 4 * c + 3, 1)], load_n0, c)
-        for r in range(ND - 1):
-            plan_store(r)
-        for first, count in in_halves:
-            plan_store(ND - 1, first, count)
+        plan_load("b", 4)
+        plan_load("d", 0)
+        plan_load("b", 5)
+        plan_load("d", 1)
+        plan_load("b", 6)
+        plan_load("d", 2)
+        plan_load("d", 3)
+        plan_load("b", 7)
+        plan_load("d", 4)
+        plan_load("d", 5)
+        plan_load("d", 6)
+        plan_load("d", 7)
+        plan_load("d", 8)
+        plan_load("d", 9)
+        plan_load("d", 10)
+        plan_load("d", 11)
+        buffered("sync", ("load_n0", 0), [], "rows", [("evict_o", 3, 1)], load_n0, 0)
+        buffered("sync", ("load_n0", 1), [], "rows", [("evict_o", 7, 1)], load_n0, 1)
+        buffered("sync", ("load_n0", 2), [], "rows", [("evict_o", 11, 1)], load_n0, 2)
+        plan_store(0)
+        plan_store(1)
+        plan_store(2)
+        plan_store(3)
+        plan_store(4)
+        plan_store(5)
+        plan_store(6)
+        plan_store(7)
+        plan_store(8)
+        plan_store(9)
+        plan_store(10)
+        plan_store(11, 0, 1)
+        plan_store(11, 1, 1)
 
-        plan_turn_b(0)
-        plan_turn_b(1)
-        tensor_step("rest", "turn_coul", ["coul_rows"], ["coul_col"], turn_coul)
+        plan_turn("b", 0)
+        plan_turn("b", 1)
         tensor_step("rest", "warm_up", [("sort_h", 0), ("sort_hs", 0)], ["warm_up"], warm_up)
-        plan_turn_b(2)
-        runs = [[("b", 3)], [("b", 4)], [("d", 0), ("b", 5), ("d", 1)], [("b", 6), ("d", 2), ("d", 3), ("b", 7)], [("d", 4), ("d", 5)]]
-        for n, run in enumerate(runs):
-            for e in range(2):
-                if n < 2 * NG:
-                    plan_trial(n // 2, 2 * (n % 2) + e)
-                else:
-                    plan_response(0, e)
-            for what, tile in run:
-                (plan_turn_b if what == "b" else plan_turn_d)(tile)
+        plan_turn("b", 2)
+        tensor_step("rest", "turn_coul", ["coul_rows"], ["coul_col"], turn_coul)
+        plan_trial(0, 0)
+        plan_trial(0, 1)
+        plan_turn("b", 3)
+        plan_trial(0, 2)
+        plan_trial(0, 3)
+        plan_turn("b", 4)
+        plan_trial(1, 0)
+        plan_trial(1, 1)
+        plan_turn("d", 0)
+        plan_turn("b", 5)
+        plan_turn("d", 1)
+        plan_trial(1, 2)
+        plan_trial(1, 3)
+        plan_turn("b", 6)
+        plan_turn("d", 2)
+        plan_turn("d", 3)
+        plan_turn("b", 7)
+        plan_response(0, 0)
+        plan_response(0, 1)
+        plan_turn("d", 4)
+        plan_turn("d", 5)
         plan_response(1, 0)
-        ring["rest"] = [0, 1] + [4 + (turn["rest"] + k) % 4 for k in range(4)] + [2, 3]
-        turn["rest"] = 0
+        join_banks()
         plan_response(1, 1)
-        early = [(q, s) for q in range(2) for s in (2, 3)]
-        whole = [(q, s) for q in range(2, last) for s in range(NS)]
-        for q, s in early + whole:
-            plan_response(q, s)
-        for s in range(NS - 1):
-            plan_induced(2 * s)
-            plan_induced(2 * s + 1)
-            plan_response(last, s)
-        for r in range(2 * NS - 2, ND - 3):
-            plan_induced(r)
-        for first, count in in_halves:
-            plan_response(last, NS - 1, first, count)
-        for r in range(ND - 3, ND):
-            plan_induced(r)
+        plan_response(0, 2)
+        plan_response(0, 3)
+        plan_response(1, 2)
+        plan_response(1, 3)
+        plan_response(2, 0)
+        plan_response(2, 1)
+        plan_response(2, 2)
+        plan_response(2, 3)
+        plan_response(3, 0)
+        plan_response(3, 1)
+        plan_response(3, 2)
+        plan_response(3, 3)
+        plan_response(4, 0)
+        plan_response(4, 1)
+        plan_response(4, 2)
+        plan_response(4, 3)
+        plan_induced(0)
+        plan_induced(1)
+        plan_response(5, 0)
+        plan_induced(2)
+        plan_induced(3)
+        plan_response(5, 1)
+        plan_induced(4)
+        plan_induced(5)
+        plan_response(5, 2)
+        plan_induced(6)
+        plan_induced(7)
+        plan_response(5, 3, 0, 1)
+        plan_response(5, 3, 1, 1)
+        plan_induced(8)
+        plan_induced(9)
+        plan_induced(10)
+        plan_induced(11)
 
         step("vector", "ginv", ["gap"], invert_gap)
         plan_scale_b(0)
-        for g in range(NG):
-            step("vector", ("sort_hs", g), ["load_hs"], sort_hs, g)
-        plan_sort_h(0)
+        plan_sort_hs(0, "V")
+        plan_sort_hs(1, "V")
+        plan_sort_h(0, "V")
         plan_scale_b(1)
         plan_scale_b(2)
-        plan_sort_h(1)
+        plan_sort_h(1, "V")
         plan_scale_b(3)
         plan_quant_b(0, 0)
-        plan_sort("b", 5, "V")
+        plan_sort("b", 5)
         plan_quant_b(0, 1)
-        plan_scale_b(4, (0,))
-        plan_sort("b", 6, "V")
-        plan_scale_b(4, (1,))
+        plan_scale_b(4)
         plan_scale_b(5)
         plan_quant_d(0)
         plan_scale_b(6)
-        plan_scale_b(7, (0,))
+        plan_scale_b(7)
         plan_quant_d(1)
-        plan_scale_b(7, (1,))
         plan_quant_b(1, 0)
         plan_quant_b(1, 1)
         plan_quant_d(2)
         plan_turn_blocks(6)
-        plan_weave_p(0)
+        plan_quant_p(0)
         plan_turn_blocks(7)
         plan_weave_blocks(6, "V")
-        plan_quant_p(0)
+        plan_quant_p(1)
         plan_weave_blocks(7, "V")
         plan_turn_blocks(8)
         plan_quant_d(3)
         plan_turn_blocks(9)
-        plan_weave_p(1)
+        plan_weave_blocks(8, "V")
         plan_turn_blocks(10)
+        plan_weave_blocks(9, "V")
+        plan_weave_c(0, "V")
         plan_quant_d(4)
         plan_turn_blocks(11)
-        plan_quant_p(1)
-        plan_weave_c(0)
-        plan_weave_c(1)
+        plan_weave_c(1, "V")
         plan_quant_c(0)
-        plan_quant_d(last)
         plan_quant_c(1)
-        plan_weave_c(2)
+        plan_quant_d(5)
+        plan_weave_c(2, "V")
         plan_evict_o(0)
         plan_quant_c(2)
-        for q in range(3, last):
-            plan_evict_o(2 * q - 5)
-            plan_weave_c(q)
-            plan_evict_o(2 * q - 4)
-            plan_quant_c(q)
+        plan_evict_o(1)
+        plan_weave_c(3, "V")
+        plan_evict_o(2)
+        plan_quant_c(3)
+        plan_evict_o(3)
+        plan_evict_o(4)
+        plan_quant_c(4)
         plan_evict_o(5)
-        plan_quant_c(last, 0, 2)
-        for r in range(6, ND - 3):
-            plan_evict_o(r)
-        for e in range(2):
-            plan_quant_c(last, 2 + e, 1)
-            plan_evict_o(ND - 3 + e)
-        for first, count in in_halves:
-            plan_evict_o(ND - 1, first, count)
+        plan_quant_c(5, 0, 2)
+        plan_evict_o(6)
+        plan_evict_o(7)
+        plan_quant_c(5, 2, 1)
+        plan_evict_o(8)
+        plan_quant_c(5, 3, 1)
+        plan_evict_o(9)
+        plan_evict_o(10)
+        plan_evict_o(11, 0, 1)
+        plan_evict_o(11, 1, 1)
 
-        plan_sort("b", 1, "S", in_halves)
+        plan_sort("b", 1, in_halves)
         step("scalar", "coul_rows", ["coul"], widen_coul)
         step("scalar", "coul_col", ["turn_coul"], evict_coul)
-        plan_sort("b", 3, "S", in_halves)
+        plan_sort("b", 3, in_halves)
         plan_scale_t(0, 0)
         plan_scale_t(0, 1)
-        plan_sort("b", 4, "S")
+        plan_sort("b", 4)
         plan_scale_t(0, 2)
-        plan_sort("d", 0, "S")
+        plan_sort("d", 0)
         plan_scale_t(0, 3)
         plan_scale_t(1, 0)
-        plan_sort("d", 1, "S")
+        plan_sort("d", 1)
         plan_scale_t(1, 1)
         plan_fill_d(0)
-        plan_sort("d", 2, "S")
         plan_fill_d(1)
+        plan_sort("d", 2)
         plan_scale_t(1, 2)
         plan_scale_t(1, 3)
         plan_fill_d(2)
         plan_fill_d(3)
-        plan_sort("d", 4, "S")
-        plan_evict_pairs(0, 0)
-        plan_evict_pairs(0, 1)
+        plan_sort("d", 4)
+        plan_evict_c(0, 0)
+        plan_evict_c(0, 1)
         plan_fill_d(4)
         plan_fill_d(5)
-        ahead = {
-            (1, 0): [(plan_sort_blocks, 6)],
-            (1, 1): [(plan_sort_blocks, 7)],
-            (0, 3): [(plan_sort_blocks, 8)],
-            (1, 2): [(plan_sort_blocks, 9)],
-            (2, 0): [(plan_sort_blocks, 10), (plan_weave_blocks, 8, "S")],
-            (2, 1): [(plan_weave_blocks, 9, "S"), (plan_sort_blocks, 11)],
-            (2, 3): [(plan_weave_blocks, 10, "S")],
-            (3, 0): [(plan_weave_blocks, 11, "S")],
-        }
-        for q, s in [(1, 0), (1, 1)] + early + whole:
-            for job in ahead.get((q, s), []):
-                job[0](*job[1:])
-            plan_evict_pairs(q, s)
-        for s in range(NS - 1):
-            plan_evict_c(last, s)
-        for first, count in in_halves:
-            plan_evict_c(last, NS - 1, first, count)
+        plan_sort("d", 6)
+        plan_evict_c(1, 0)
+        plan_sort("d", 7)
+        plan_evict_c(1, 1)
+        plan_evict_c(0, 2)
+        plan_sort("d", 8)
+        plan_evict_c(0, 3)
+        plan_sort("d", 9)
+        plan_evict_c(1, 2)
+        plan_evict_c(1, 3)
+        plan_sort("d", 10)
+        plan_evict_c(2, 0)
+        plan_evict_c(2, 1)
+        plan_sort("d", 11)
+        plan_evict_c(2, 2)
+        plan_weave_blocks(10, "S")
+        plan_evict_c(2, 3)
+        plan_evict_c(3, 0)
+        plan_weave_blocks(11, "S")
+        plan_evict_c(3, 1)
+        plan_evict_c(3, 2)
+        plan_evict_c(3, 3)
+        plan_evict_c(4, 0)
+        plan_evict_c(4, 1)
+        plan_evict_c(4, 2)
+        plan_evict_c(4, 3)
+        plan_evict_c(5, 0)
+        plan_weave_c(4, "S")
+        plan_evict_c(5, 1)
+        plan_evict_c(5, 2)
+        plan_evict_c(5, 3, 0, 1)
+        plan_evict_c(5, 3, 1, 1)
+
+        plan_weave_p(0, "G")
+        plan_weave_p(1, "G")
 
         with tc.manual_schedule():
             nc.vector.memset(hs_in[:], 0)
             nc.vector.memset(x_s[:].rearrange("p j n -> p (j n)").bitcast(I32), 0)
             nc.vector.memset(coul_rows[:], 0.0)
             make_identity(nc, ident[:])
-            emit(set())
+            load_coul()
+            emit({"coul"})

@@ -23,10 +23,10 @@ NB = A // 128
 NS = NB // 2
 ND = R // 128
 NQ = ND // 2
-FIRST_BLOCK = 6
+FIRST_BLOCK = 5
 FIRST_DIRECT = 5
 WARM_UPS = 3
-SORTER = {**{("b", i): "S" for i in (1, 3, 4)}, ("b", 5): "V", **{("d", r): "S" for r in range(ND) if r not in (3, 5)}}
+SORTER = {**{("b", i): "S" for i in (1, 3, 4)}, ("b", 5): "V", **{("d", r): "S" for r in range(ND) if r != 3}}
 DEPTH = {"rows": 9, "sortedS": 4, "sortedV": 2, "wide": 3, "d_t": 3, "chi": 5, "first": 2}
 OWN = {tag: [f"{tag}{k}" for k in range(n)] for tag, n in DEPTH.items()}
 RINGS = {
@@ -34,11 +34,13 @@ RINGS = {
     "res": OWN["first"] + OWN["sortedV"] + ["x_w", "pot_s0", "pot_s1"],
     "d_flip": ["h_in0", "h_in1", "flip2"],
     "chi": OWN["chi"] + ["h_w0"],
+    "d_t": ["d_t0", "d_t1", "d_t2", "d_t1", "d_t2", "d_t0"],
     "woven": OWN["wide"],
     "ccodes": ["dcodes0", "dcodes1", "dcodes2"],
 }
 POT_PLACE = [("wide1", ("quant_b", 0, 1)), ("d_t0", ("quant_d", 0))]
-POT_FIRST = {"V": [("quant_p", 0)], "S": [("quant_p", 1)]}
+POT_FIRST = {10: [("quant_p", 1)]}
+LEFT_BY = {}
 
 
 def tile_rpa_density_step_s12_kernel(tc, d, b, gap, h_words, h_scales, x_words, x_scales, coul, n0, out):
@@ -359,6 +361,7 @@ def tile_rpa_density_step_s12_kernel(tc, d, b, gap, h_words, h_scales, x_words, 
             holder[f"h_in{g}"] = [("sort_h", g)]
             holder[f"h_w{g}"] = [("mul_t", g, 3)]
             holder[f"pot_s{g}"] = [("weave_p", g)]
+        holder.update(LEFT_BY)
         holder["x_w"] = [("mul_t", NG - 1, 3)]
         for q in range(NQ):
             holder[f"dcodes{q}"] = [("mul_c", q, NS - 1, 1)]
@@ -465,8 +468,8 @@ def tile_rpa_density_step_s12_kernel(tc, d, b, gap, h_words, h_scales, x_words, 
                 buffered("scalar", ("d_t", r, h), [("turn_d", r)], tag, [("quant_d", r // 2)], evict_d, r, h)
 
         def plan_weave_blocks(r, eng):
-            needs = [("turn_blocks", r)] + POT_FIRST[eng] + ([("d_t", r - 1, 0)] if r % 2 else [])
-            tag = ("d_t" if eng == "S" else "wide") if r % 2 == 0 else None
+            needs = [("turn_blocks", r)] + POT_FIRST.get(r, []) + ([("d_t", r - 1, 0)] if r % 2 else [])
+            tag = ("d_t" if eng == "S" else "d_by_V") if r % 2 == 0 else None
             buffered(engine[eng], [("d_t", r, 0), ("d_t", r, 1)], needs, tag, [("quant_d", r // 2)], weave_blocks, r, eng)
 
         def plan_turn_blocks(r):
@@ -605,7 +608,6 @@ def tile_rpa_density_step_s12_kernel(tc, d, b, gap, h_words, h_scales, x_words, 
         plan_response(0, 0)
         plan_response(0, 1)
         plan_turn("d", 4)
-        plan_turn("d", 5)
         plan_response(1, 0)
         join_banks()
         plan_response(1, 1)
@@ -659,31 +661,33 @@ def tile_rpa_density_step_s12_kernel(tc, d, b, gap, h_words, h_scales, x_words, 
         plan_scale_b(5)
         plan_quant_d(0)
         plan_scale_b(6)
-        plan_scale_b(7)
+        plan_scale_b(7, (0,))
         plan_quant_d(1)
+        plan_scale_b(7, (1,))
         plan_quant_b(1, 0)
         plan_quant_b(1, 1)
-        plan_quant_d(2)
+        plan_turn_blocks(5)
         plan_turn_blocks(6)
+        plan_weave_blocks(5, "V")
         plan_quant_p(0)
+        plan_quant_d(2)
         plan_turn_blocks(7)
-        plan_weave_blocks(6, "V")
-        plan_quant_p(1)
-        plan_weave_blocks(7, "V")
         plan_turn_blocks(8)
+        plan_weave_blocks(7, "V")
         plan_quant_d(3)
         plan_turn_blocks(9)
-        plan_weave_blocks(8, "V")
-        plan_turn_blocks(10)
+        plan_quant_p(1)
         plan_weave_blocks(9, "V")
         plan_weave_c(0, "V")
         plan_quant_d(4)
-        plan_turn_blocks(11)
+        plan_turn_blocks(10)
         plan_weave_c(1, "V")
         plan_quant_c(0)
+        plan_turn_blocks(11)
         plan_quant_c(1)
-        plan_quant_d(5)
+        plan_weave_blocks(11, "V")
         plan_weave_c(2, "V")
+        plan_quant_d(5)
         plan_evict_o(0)
         plan_quant_c(2)
         plan_evict_o(1)
@@ -727,17 +731,19 @@ def tile_rpa_density_step_s12_kernel(tc, d, b, gap, h_words, h_scales, x_words, 
         plan_fill_d(3)
         plan_sort("d", 4)
         plan_evict_c(0, 0)
+        plan_sort("d", 5)
         plan_evict_c(0, 1)
         plan_fill_d(4)
-        plan_fill_d(5)
         plan_sort("d", 6)
         plan_evict_c(1, 0)
         plan_sort("d", 7)
         plan_evict_c(1, 1)
-        plan_evict_c(0, 2)
+        plan_weave_blocks(6, "S")
         plan_sort("d", 8)
+        plan_evict_c(0, 2)
         plan_evict_c(0, 3)
         plan_sort("d", 9)
+        plan_weave_blocks(8, "S")
         plan_evict_c(1, 2)
         plan_evict_c(1, 3)
         plan_sort("d", 10)
@@ -748,7 +754,6 @@ def tile_rpa_density_step_s12_kernel(tc, d, b, gap, h_words, h_scales, x_words, 
         plan_weave_blocks(10, "S")
         plan_evict_c(2, 3)
         plan_evict_c(3, 0)
-        plan_weave_blocks(11, "S")
         plan_evict_c(3, 1)
         plan_evict_c(3, 2)
         plan_evict_c(3, 3)

@@ -26,7 +26,7 @@ NQ = ND // 2
 FIRST_BLOCK = 5
 FIRST_DIRECT = 5
 WARM_UPS = 3
-SORTER = {**{("b", i): "S" for i in (1, 3, 4)}, ("b", 5): "V", **{("d", r): "S" for r in range(ND) if r != 3}}
+SORTER = {**{("b", i): "S" for i in (1, 3, 4)}, ("b", 5): "V", ("b", 6): "G", **{("d", r): "S" for r in range(ND) if r != 3}}
 DEPTH = {"rows": 9, "sortedS": 4, "sortedV": 2, "wide": 3, "d_t": 3, "chi": 5, "first": 2}
 OWN = {tag: [f"{tag}{k}" for k in range(n)] for tag, n in DEPTH.items()}
 RINGS = {
@@ -34,12 +34,12 @@ RINGS = {
     "res": OWN["first"] + OWN["sortedV"] + ["x_w", "pot_s0", "pot_s1"],
     "d_flip": ["h_in0", "h_in1", "flip2"],
     "chi": OWN["chi"] + ["h_w0"],
-    "d_t": ["d_t0", "d_t1", "d_t2", "d_t1", "d_t2", "d_t0"],
+    "d_t": ["d_t0", "d_t1", "d_t2", "d_t1", "d_t3", "d_t0"],
     "woven": OWN["wide"],
     "ccodes": ["dcodes0", "dcodes1", "dcodes2"],
 }
-POT_PLACE = [("wide1", ("quant_b", 0, 1)), ("d_t0", ("quant_d", 0))]
-POT_FIRST = {10: [("quant_p", 1)]}
+POT_PLACE = {(0, 0): ("d_t0", ("quant_d", 0)), (1, 0): ("wide0", ("quant_b", 1, 1)), (1, 1): ("d_t2", ("quant_d", 2))}
+POT_FIRST = {10: [("quant_p", 0, 1)]}
 LEFT_BY = {}
 
 
@@ -110,6 +110,16 @@ def tile_rpa_density_step_s12_kernel(tc, d, b, gap, h_words, h_scales, x_words, 
         def sort_rows(name, what, n, eng, first, count):
             if name is not None:
                 perm[what, n] = buf(name, [128, 2, 2, T // 8], F32)
+            if eng == "G":
+                nc.gpsimd.tensor_scalar(
+                    out=perm[what, n][:].bitcast(BF16).rearrange("p h u (n e) -> p u h n e", e=2),
+                    in0=rows[what, n][:].rearrange("p (h n u e) -> p u h n e", h=2, u=2, e=2),
+                    scalar1=1.0,
+                    scalar2=0.0,
+                    op0=ALU.mult,
+                    op1=ALU.add,
+                )
+                return
             pairs = rows[what, n][:].bitcast(F32)[:, 512 * first : 512 * (first + count)]
             copy(
                 eng,
@@ -192,15 +202,14 @@ def tile_rpa_density_step_s12_kernel(tc, d, b, gap, h_words, h_scales, x_words, 
         def scale_t(g, t):
             nc.scalar.activation(out=pot_s[g][:, t, :], in_=ps_t[g, t][:], func=ACT.Copy, scale=coul_col[:, g, t : t + 1])
 
-        def weave_p(name, g, eng):
-            pot[g] = buf(name, [128, P, 4], BF16)
-            if eng == "G":
-                nc.gpsimd.tensor_scalar(out=pot[g][:], in0=pot_s[g][:].rearrange("p t n -> p n t"), scalar1=1.0, scalar2=0.0, op0=ALU.mult, op1=ALU.add)
-            else:
-                copy(eng, pot[g][:].rearrange("p (c i) t -> p c t i", i=4), pot_s[g][:].rearrange("p t (c i) -> p c t i", i=4))
+        def weave_p(name, g, first, count):
+            pot[g, first] = buf(name, [128, 256 * count, 4], BF16)
+            places = pot_s[g][:, :, 256 * first : 256 * (first + count)].rearrange("p t n -> p n t")
+            nc.gpsimd.tensor_scalar(out=pot[g, first][:], in0=places, scalar1=1.0, scalar2=0.0, op0=ALU.mult, op1=ALU.add)
 
-        def quant_p(g):
-            nc.vector.quantize_mx(out=pcodes[g][:].bitcast(FP8X4), scales=pscale[g][:], in_=pot[g][:].rearrange("p n t -> p (n t)"))
+        def quant_p(g, first, count):
+            cols = slice(256 * first, 256 * (first + count))
+            nc.vector.quantize_mx(out=pcodes[g][:, cols].bitcast(FP8X4), scales=pscale[g][:, cols], in_=pot[g, first][:].rearrange("p n t -> p (n t)"))
 
         def turn_d(banks, r):
             for h in range(2):
@@ -360,7 +369,7 @@ def tile_rpa_density_step_s12_kernel(tc, d, b, gap, h_words, h_scales, x_words, 
         for g in range(NG):
             holder[f"h_in{g}"] = [("sort_h", g)]
             holder[f"h_w{g}"] = [("mul_t", g, 3)]
-            holder[f"pot_s{g}"] = [("weave_p", g)]
+            holder[f"pot_s{g}"] = [("weave_p", g, 1)]
         holder.update(LEFT_BY)
         holder["x_w"] = [("mul_t", NG - 1, 3)]
         for q in range(NQ):
@@ -437,6 +446,10 @@ def tile_rpa_density_step_s12_kernel(tc, d, b, gap, h_words, h_scales, x_words, 
             if by_vector(what, n):
                 buffered(engine[eng], ("sort", what, n, 1), [("load", what, n)], "sorted" + eng, turned(what, n), sort_blocks, n, eng)
                 return
+            if eng == "G":
+                keys = [("sort", what, n, h) for h in range(2)]
+                step("gpsimd", keys, [("load", what, n), ("quant_b", 0, 1)], sort_rows, "wide1", what, n, eng, 0, 2)
+                return
             for first, count in pieces:
                 keys = [("sort", what, n, h) for h in range(first, first + count)]
                 tag = "sorted" + eng if first == 0 else None
@@ -484,16 +497,13 @@ def tile_rpa_density_step_s12_kernel(tc, d, b, gap, h_words, h_scales, x_words, 
         def plan_scale_t(g, t):
             step("scalar", ("scale_t", g, t), [("mul_t", g, t), "coul_col"], scale_t, g, t)
 
-        def plan_weave_p(g, eng):
-            needs = [("scale_t", g, t) for t in range(4)]
-            if eng == "G":
-                name, freed_by = POT_PLACE[g]
-                step("gpsimd", ("weave_p", g), needs + [freed_by], weave_p, name, g, eng)
-            else:
-                buffered(engine[eng], ("weave_p", g), needs, "pot", [("quant_p", g)], weave_p, g, eng)
+        def plan_weave_p(g, first, count):
+            name, freed_by = POT_PLACE[g, first]
+            keys = [("weave_p", g, n) for n in range(first, first + count)]
+            step("gpsimd", keys, [("scale_t", g, t) for t in range(4)] + [freed_by], weave_p, name, g, first, count)
 
-        def plan_quant_p(g):
-            step("vector", ("quant_p", g), [("weave_p", g)], quant_p, g)
+        def plan_quant_p(g, first, count):
+            step("vector", [("quant_p", g, n) for n in range(first, first + count)], [("weave_p", g, first)], quant_p, g, first, count)
 
         def plan_response(q, s, first=0, count=2):
             keys = [("mul_c", q, s, e) for e in range(first, first + count)]
@@ -517,7 +527,7 @@ def tile_rpa_density_step_s12_kernel(tc, d, b, gap, h_words, h_scales, x_words, 
             buffered("vector", [("quant_c", q, n) for n in pieces], needs, tag, [("mul_o", 2 * q + 1)], quant_c, q, first, count)
 
         def plan_induced(r):
-            needs = [("quant_c", r // 2, r % 2), ("quant_c", r // 2, 2 + r % 2), ("quant_p", 0), ("quant_p", 1)]
+            needs = [("quant_c", r // 2, r % 2), ("quant_c", r // 2, 2 + r % 2), ("quant_p", 0, 1), ("quant_p", 1, 1)]
             tensor_step("rest", ("mul_o", r), needs, [("evict_o", r, 1)], mul_o, r)
 
         def plan_evict_o(r, first=0, count=2):
@@ -585,9 +595,9 @@ def tile_rpa_density_step_s12_kernel(tc, d, b, gap, h_words, h_scales, x_words, 
 
         plan_turn("b", 0)
         plan_turn("b", 1)
+        tensor_step("rest", "turn_coul", ["coul_rows"], ["coul_col"], turn_coul)
         tensor_step("rest", "warm_up", [("sort_h", 0), ("sort_hs", 0)], ["warm_up"], warm_up)
         plan_turn("b", 2)
-        tensor_step("rest", "turn_coul", ["coul_rows"], ["coul_col"], turn_coul)
         plan_trial(0, 0)
         plan_trial(0, 1)
         plan_turn("b", 3)
@@ -669,14 +679,15 @@ def tile_rpa_density_step_s12_kernel(tc, d, b, gap, h_words, h_scales, x_words, 
         plan_turn_blocks(5)
         plan_turn_blocks(6)
         plan_weave_blocks(5, "V")
-        plan_quant_p(0)
+        plan_quant_p(0, 0, 2)
         plan_quant_d(2)
         plan_turn_blocks(7)
         plan_turn_blocks(8)
         plan_weave_blocks(7, "V")
         plan_quant_d(3)
         plan_turn_blocks(9)
-        plan_quant_p(1)
+        plan_quant_p(1, 0, 1)
+        plan_quant_p(1, 1, 1)
         plan_weave_blocks(9, "V")
         plan_weave_c(0, "V")
         plan_quant_d(4)
@@ -768,8 +779,10 @@ def tile_rpa_density_step_s12_kernel(tc, d, b, gap, h_words, h_scales, x_words, 
         plan_evict_c(5, 3, 0, 1)
         plan_evict_c(5, 3, 1, 1)
 
-        plan_weave_p(0, "G")
-        plan_weave_p(1, "G")
+        plan_sort("b", 6)
+        plan_weave_p(0, 0, 2)
+        plan_weave_p(1, 0, 1)
+        plan_weave_p(1, 1, 1)
 
         with tc.manual_schedule():
             nc.vector.memset(hs_in[:], 0)

@@ -26,7 +26,7 @@ NQ = ND // 2
 FIRST_BLOCK = 5
 FIRST_DIRECT = 5
 WARM_UPS = 3
-SORTER = {**{("b", i): "S" for i in (1, 3, 4)}, ("b", 5): "V", ("b", 6): "G", **{("d", r): "S" for r in range(ND) if r != 3}}
+SORTER = {**{("b", i): "S" for i in (1, 3, 4)}, ("b", 6): "G", **{("d", r): "S" for r in range(ND) if r != 3}}
 DEPTH = {"rows": 9, "sortedS": 4, "sortedV": 2, "wide": 3, "d_t": 3, "chi": 5, "first": 2}
 OWN = {tag: [f"{tag}{k}" for k in range(n)] for tag, n in DEPTH.items()}
 RINGS = {
@@ -665,7 +665,6 @@ def tile_rpa_density_step_s12_kernel(tc, d, b, gap, h_words, h_scales, x_words, 
         plan_sort_h(1, "V")
         plan_scale_b(3)
         plan_quant_b(0, 0)
-        plan_sort("b", 5)
         plan_quant_b(0, 1)
         plan_scale_b(4)
         plan_scale_b(5)
@@ -684,9 +683,9 @@ def tile_rpa_density_step_s12_kernel(tc, d, b, gap, h_words, h_scales, x_words, 
         plan_turn_blocks(7)
         plan_turn_blocks(8)
         plan_weave_blocks(7, "V")
+        plan_quant_p(1, 0, 1)
         plan_quant_d(3)
         plan_turn_blocks(9)
-        plan_quant_p(1, 0, 1)
         plan_quant_p(1, 1, 1)
         plan_weave_blocks(9, "V")
         plan_weave_c(0, "V")
@@ -702,7 +701,6 @@ def tile_rpa_density_step_s12_kernel(tc, d, b, gap, h_words, h_scales, x_words, 
         plan_evict_o(0)
         plan_quant_c(2)
         plan_evict_o(1)
-        plan_weave_c(3, "V")
         plan_evict_o(2)
         plan_quant_c(3)
         plan_evict_o(3)
@@ -772,6 +770,7 @@ def tile_rpa_density_step_s12_kernel(tc, d, b, gap, h_words, h_scales, x_words, 
         plan_evict_c(4, 1)
         plan_evict_c(4, 2)
         plan_evict_c(4, 3)
+        plan_weave_c(3, "S")
         plan_evict_c(5, 0)
         plan_weave_c(4, "S")
         plan_evict_c(5, 1)

from contextlib import ExitStack

import concourse.mybir as mybir
from concourse.masks import make_identity

R, T, A, F, P = 1536, 2048, 1024, 1536, 512
FLOPS = 2 * (R * T * A + F * A * P + R * A * P)

F32 = mybir.dt.float32
BF16 = mybir.dt.bfloat16
U32 = mybir.dt.uint32
I32 = mybir.dt.int32
U8 = mybir.dt.uint8
FP8X4 = mybir.dt.float8_e4m3fn_x4
FP4X4 = mybir.dt.float4_e2m1fn_x4
ALU = mybir.AluOpType
ACT = mybir.ActivationFunctionType

NJ = T // 512
NF = F // 512
NG = A // 512
NB = A // 128
NS = NB // 2
ND = R // 128
NQ = ND // 2
FIRST_BLOCK = 5
FIRST_DIRECT = 5
WARM_UPS = 3
SORTER = {**{("b", i): "S" for i in (1, 3, 4)}, ("b", 6): "G", **{("d", r): "S" for r in range(ND) if r != 3}}
DEPTH = {"rows": 9, "sortedS": 4, "sortedV": 2, "wide": 3, "d_t": 3, "chi": 5, "first": 2}
OWN = {tag: [f"{tag}{k}" for k in range(n)] for tag, n in DEPTH.items()}
RINGS = {
    **OWN,
    "res": OWN["first"] + OWN["sortedV"] + ["x_w", "pot_s0", "pot_s1"],
    "d_flip": ["h_in0", "h_in1", "flip2"],
    "chi": OWN["chi"] + ["h_w0"],
    "d_t": ["d_t0", "d_t1", "d_t2", "d_t1", "d_t3", "d_t0"],
    "woven": OWN["wide"],
    "ccodes": ["dcodes0", "dcodes1", "dcodes2"],
}
POT_PLACE = {(0, 0): ("d_t0", ("quant_d", 0)), (1, 0): ("wide0", ("quant_b", 1, 1)), (1, 1): ("d_t2", ("quant_d", 2))}
POT_FIRST = {10: [("quant_p", 0, 1)]}
LEFT_BY = {}


def tile_rpa_density_step_s12_kernel(tc, d, b, gap, h_words, h_scales, x_words, x_scales, coul, n0, out):
    nc = tc.nc
    with ExitStack() as ctx:
        keep = ctx.enter_context(tc.tile_pool(name="keep", bufs=1))
        psum = ctx.enter_context(tc.psum_pool(name="psum", bufs=1))

        def buf(name, shape, dtype):
            return keep.tile(shape, dtype, name=name, align_bytes=64)

        def bank(n, shape):
            return psum.tile(shape, F32, name=f"bank{n}")

        ident = buf("ident", [128, 128], F32)
        gap_in = buf("gap_in", [128, NJ, 4], BF16)
        coul_in = buf("coul_in", [128, NG, 128], BF16)
        coul_rows = buf("coul_rows", [128, NG, 128], F32)
        ginv = buf("ginv", [128, NJ, 4], F32)
        coul_col = buf("coul_col", [128, NG, 4], F32)
        x_w = buf("x_w", [128, NF, 2 * P], U8)
        x_s = buf("x_s", [128, NF, P], U8)
        h_in = [buf(f"h_in{g}", [128, NF, 256], I32) for g in range(NG)]
        hs_in = buf("hs_in", [128, NF, 256], I32)
        h_w = [buf(f"h_w{g}", [128, NF, 4, 256], U8) for g in range(NG)]
        h_s = [buf(f"h_s{g}", [128, NF, 4, 128], U8) for g in range(NG)]
        bcodes = [[buf(f"bcodes{g}_{h}", [128, 2, 4, 128], U32) for h in range(2)] for g in range(NG)]
        bscale = [[buf(f"bscale{g}_{h}", [128, 2, 4, 128], U8) for h in range(2)] for g in range(NG)]
        dcodes = [buf(f"dcodes{q}", [128, NJ, 256], U32) for q in range(NQ)]
        dscale = [buf(f"dscale{q}", [128, NJ, 256], U8) for q in range(NQ)]
        pot_s = [buf(f"pot_s{g}", [128, 4, P], BF16) for g in range(NG)]
        pcodes = [buf(f"pcodes{g}", [128, P], U32) for g in range(NG)]
        pscale = [buf(f"pscale{g}", [128, P], U8) for g in range(NG)]
        cscale = [buf(f"cscale{q}", [128, NG, 256], U8) for q in range(NQ)]

        halves, rows, n0_sb, perm, b_t, d_t, d_flip, pot, chi_pairs, chi, ccodes, res = {}, {}, {}, {}, {}, {}, {}, {}, {}, {}, {}, {}
        tr_coul, tr_b, tr_d, ps_t, ps_c, ps_o = {}, {}, {}, {}, {}, {}

        def copy(eng, dst, src):
            if eng == "S":
                nc.scalar.copy(out=dst, in_=src)
            else:
                nc.vector.tensor_copy(out=dst, in_=src)

        def load_rows(name, what, n):
            rows[what, n] = buf(name, [128, T], BF16)
            nc.sync.dma_start(out=rows[what, n][:], in_=(b if what == "b" else d)[n * 128 : (n + 1) * 128, :])

        def load_half(name, h):
            halves[h] = buf(name, [128, T // 2], BF16)
            nc.sync.dma_start(out=halves[h][:], in_=b[0:128, 1024 * h : 1024 * (h + 1)])

        def load_n0(name, c):
            n0_sb[c] = buf(name, [128, 4, P], BF16)
            nc.sync.dma_start(out=n0_sb[c][:], in_=n0[c * 512 : (c + 1) * 512, :].rearrange("(c p) n -> p c n", p=128))

        def load_h(g):
            nc.sync.dma_start(out=h_in[g][:], in_=h_words.bitcast(I32)[:, :, 256 * g : 256 * (g + 1)].rearrange("j p n -> p j n"))

        def load_x():
            nc.sync.dma_start(out=x_w[:].bitcast(I32), in_=x_words.bitcast(I32).rearrange("j p n -> p j n"))

        def load_scales(plane, scales):
            for r in range(4):
                nc.sync.dma_start(out=plane[r:128:32], in_=scales[:, r:16:4, :].rearrange("j Q n -> Q j n"))

        def sort_rows(name, what, n, eng, first, count):
            if name is not None:
                perm[what, n] = buf(name, [128, 2, 2, T // 8], F32)
            if eng == "G":
                nc.gpsimd.tensor_scalar(
                    out=perm[what, n][:].bitcast(BF16).rearrange("p h u (n e) -> p u h n e", e=2),
                    in0=rows[what, n][:].rearrange("p (h n u e) -> p u h n e", h=2, u=2, e=2),
                    scalar1=1.0,
                    scalar2=0.0,
                    op0=ALU.mult,
                    op1=ALU.add,
                )
                return
            pairs = rows[what, n][:].bitcast(F32)[:, 512 * first : 512 * (first + count)]
            copy(
                eng,
                perm[what, n][:, first : first + count].rearrange("p h u (c i) -> p h c u i", i=4),
                pairs.rearrange("p (h c i u) -> p h c u i", h=count, u=2, i=4),
            )

        def pairs_of(what, n, h, jj, u):
            if (what, n) == ("b", 0):
                return halves[h][:].bitcast(F32)[:, 256 * jj + u : 256 * (jj + 1) : 2]
            if (what, n) in SORTER:
                return perm[what, n][:, h, u, 128 * jj : 128 * (jj + 1)]
            return rows[what, n][:].bitcast(F32)[:, 512 * h + 256 * jj + u : 512 * h + 256 * (jj + 1) : 2]

        def turn_b(banks, i, h):
            tr_b[i, h] = bank(banks[0], [128, 2, 2, 128])
            for jj in range(2):
                for u in range(2):
                    cols = tr_b[i, h][:, u, jj, :].rearrange("p (t q r) -> p q t r", t=4, r=8)
                    nc.tensor.transpose(cols, pairs_of("b", i, h, jj, u), ident[:])

        def scale_b(name, i, h):
            g, c = i // 4, i % 4
            if name is not None:
                b_t[g, h] = buf(name, [128, 2, 4, 128, 4], BF16)
            nc.vector.tensor_tensor(
                out=b_t[g, h][:, :, :, 32 * c : 32 * (c + 1), :].rearrange("p j t m e -> p (j t) (m e)"),
                in0=tr_b[i, h][:].bitcast(BF16).rearrange("p u j (a e) -> p (j a) u e", e=2),
                in1=ginv[:, 2 * h : 2 * h + 2].unsqueeze(2).to_broadcast([128, 2, 128, 4]),
                op=ALU.mult,
            )

        def quant_b(g, h):
            nc.vector.quantize_mx(
                out=bcodes[g][h][:].rearrange("p j t m -> p (j t m)").bitcast(FP8X4),
                scales=bscale[g][h][:].rearrange("p j t m -> p (j t m)"),
                in_=b_t[g, h][:].rearrange("p j t m e -> p (j t m e)"),
            )

        def sort_h(g, eng):
            copy(
                eng,
                h_w[g][:].bitcast(U32 if eng == "S" else I32).rearrange("p j t (q w) -> p q j t w", w=4),
                h_in[g][:].bitcast(U32 if eng == "S" else I32).rearrange("p j (q t w) -> p q j t w", t=4, w=4),
            )

        def sort_hs(g, eng):
            copy(
                eng,
                h_s[g][:].bitcast(U32 if eng == "S" else I32).rearrange("p j t (q w) -> p j q t w", w=2),
                hs_in[:, :, 128 * g : 128 * (g + 1)].bitcast(U32 if eng == "S" else I32).rearrange("p j (q t w) -> p j q t w", t=4, w=2),
            )

        def mul_t(banks, g, t):
            ps_t[g, t] = bank(banks[0], [128, 512])
            for j in range(NF):
                nc.tensor.matmul_mx(
                    out=ps_t[g, t][:],
                    lhsT=h_w[g][:, j, t, :].bitcast(FP4X4),
                    lhsT_scale=h_s[g][:, j, t, :],
                    rhs=x_w[:, j, :].bitcast(FP4X4),
                    rhs_scale=x_s[:, j, :],
                    start=(j == 0),
                    stop=(j == NF - 1),
                )

        def warm_up(banks):
            spare = bank(banks[0], [128, 512])
            for n in range(WARM_UPS):
                nc.tensor.matmul_mx(
                    out=spare[:],
                    lhsT=h_w[0][:, 0, 0, :].bitcast(FP4X4),
                    lhsT_scale=h_s[0][:, 0, 0, :],
                    rhs=h_w[0][:, 0].rearrange("p t n -> p (t n)").bitcast(FP4X4),
                    rhs_scale=h_s[0][:, 0].rearrange("p t n -> p (t n)"),
                    start=True,
                    stop=True,
                )

        def scale_t(g, t):
            nc.scalar.activation(out=pot_s[g][:, t, :], in_=ps_t[g, t][:], func=ACT.Copy, scale=coul_col[:, g, t : t + 1])

        def weave_p(name, g, first, count):
            pot[g, first] = buf(name, [128, 256 * count, 4], BF16)
            places = pot_s[g][:, :, 256 * first : 256 * (first + count)].rearrange("p t n -> p n t")
            nc.gpsimd.tensor_scalar(out=pot[g, first][:], in0=places, scalar1=1.0, scalar2=0.0, op0=ALU.mult, op1=ALU.add)

        def quant_p(g, first, count):
            cols = slice(256 * first, 256 * (first + count))
            nc.vector.quantize_mx(out=pcodes[g][:, cols].bitcast(FP8X4), scales=pscale[g][:, cols], in_=pot[g, first][:].rearrange("p n t -> p (n t)"))

        def turn_d(banks, r):
            for h in range(2):
                tr_d[r, h] = bank(banks[h], [128, 2, 2, 128])
                for jj in range(2):
                    for u in range(2):
                        nc.tensor.transpose(tr_d[r, h][:, jj, u, :], pairs_of("d", r, h, jj, u), ident[:])

        def evict_d(name, r, h):
            q = r // 2
            if name is not None:
                d_t[q] = buf(name, [128, NJ, 256, 2], F32)
            words = d_t[q][:, 2 * h : 2 * h + 2, 128 * (r % 2) : 128 * (r % 2) + 128, :]
            if 2 * q + 1 >= FIRST_BLOCK:
                nc.scalar.copy(out=words.rearrange("p j (c i) u -> p j c i u", c=4), in_=tr_d[r, h][:].rearrange("p j u (i c) -> p j c i u", c=4))
            else:
                nc.scalar.copy(out=words, in_=tr_d[r, h][:].rearrange("p j u a -> p j a u"))

        def load_blocks(name, r):
            rows["d", r] = buf(name, [128, 4, NJ, 128], BF16)
            src = d[128 * r : 128 * (r + 1), :].rearrange("(i c) (j s k) -> s i c j k", c=4, s=4, k=128)
            for s in (0, 2, 1, 3):
                nc.sync.dma_start(out=rows["d", r][32 * s : 32 * (s + 1)], in_=src[s])

        def sort_blocks(name, r, eng):
            perm["d", r] = buf(name, [128, 16, 2, 32], F32)
            copy(
                eng,
                perm["d", r][:].rearrange("p n u (a i) -> p n a u i", i=4),
                rows["d", r][:].rearrange("p c j k -> p (c j k)").bitcast(F32).rearrange("p (n a i u) -> p n a u i", n=16, i=4, u=2),
            )

        def turn_blocks(name, r):
            d_flip[r] = buf(name, [128, 4, NJ, 2, 32], F32)
            nc.vector.transpose(out=d_flip[r][:].rearrange("p c j u i -> p (c j u i)"), in_=perm["d", r][:].rearrange("p n u w -> p (n u w)"))

        def weave_blocks(name, r, eng):
            q = r // 2
            if name is not None:
                d_t[q] = buf(name, [128, NJ, 256, 2], F32)
            copy(
                eng,
                d_t[q][:, :, 128 * (r % 2) : 128 * (r % 2) + 128, :].rearrange("p j (c i) u -> p j c i u", i=32),
                d_flip[r][:].rearrange("p c j u i -> p j c i u"),
            )

        def quant_d(q):
            nc.vector.quantize_mx(
                out=dcodes[q][:].rearrange("p j a -> p (j a)").bitcast(FP8X4),
                scales=dscale[q][:].rearrange("p j a -> p (j a)"),
                in_=d_t[q][:].rearrange("p j a u -> p (j a u)").bitcast(BF16),
            )

        def mul_c(banks, q, s, first, count):
            cols = slice(128 * first, 128 * (first + count))
            acc = bank(banks[0], [128, 2, 128 * count])
            ps_c[q, s, first] = acc
            for e in range(2):
                g, t = s // 2, 2 * (s % 2) + e
                for j in range(NJ):
                    nc.tensor.matmul_mx(
                        out=acc[:, e, :],
                        lhsT=bcodes[g][j // 2][:, j % 2, t, :].bitcast(FP8X4),
                        lhsT_scale=bscale[g][j // 2][:, j % 2, t, :],
                        rhs=dcodes[q][:, j, cols].bitcast(FP8X4),
                        rhs_scale=dscale[q][:, j, cols],
                        start=(j == 0),
                        stop=(j == NJ - 1),
                    )

        def in_row_order(q, sums):
            if 2 * q + 1 >= FIRST_BLOCK:
                return sums.rearrange("p e (n c i) -> p n i c e", c=4, i=32)
            return sums.rearrange("p e (n i c) -> p n i c e", c=4, i=32)

        def evict_c(name, q, s, first, count):
            g, tp = s // 2, s % 2
            if name is not None:
                chi[q] = buf(name, [128, NG, 256, 4], BF16)
            words = chi[q][:, g, 128 * first : 128 * (first + count), 2 * tp : 2 * tp + 2]
            nc.scalar.copy(out=words.rearrange("p (n i c) e -> p n i c e", c=4, i=32), in_=in_row_order(q, ps_c[q, s, first][:]))

        def evict_pairs(name, q, s):
            g, tp = s // 2, s % 2
            if name is not None:
                chi_pairs[q] = buf(name, [128, 2, NG, 256, 2], BF16)
            nc.scalar.copy(out=chi_pairs[q][:, tp, g].rearrange("p (n i c) e -> p n i c e", c=4, i=32), in_=in_row_order(q, ps_c[q, s, 0][:]))

        def weave_c(name, q, eng):
            chi[q] = buf(name, [128, NG, 256, 4], BF16)
            copy(
                eng,
                chi[q][:].rearrange("p g a t -> p (g a t)").bitcast(F32).rearrange("p (c i u) -> p c u i", i=4, u=2),
                chi_pairs[q][:].rearrange("p u g a e -> p u (g a e)").bitcast(F32).rearrange("p u (c i) -> p c u i", i=4),
            )

        def quant_c(name, q, first, count):
            if name is not None:
                ccodes[q] = buf(name, [128, NG, 256], U32)
            cols = slice(128 * first, 128 * (first + count))
            nc.vector.quantize_mx(
                out=ccodes[q][:].rearrange("p g a -> p (g a)")[:, cols].bitcast(FP8X4),
                scales=cscale[q][:].rearrange("p g a -> p (g a)")[:, cols],
                in_=chi[q][:].rearrange("p g a t -> p (g a) t")[:, cols].rearrange("p a t -> p (a t)"),
            )

        def mul_o(banks, r):
            q = r // 2
            ps_o[r] = bank(banks[0], [128, 512])
            cols = slice(128 * (r % 2), 128 * (r % 2) + 128)
            for g in range(NG):
                nc.tensor.matmul_mx(
                    out=ps_o[r][:],
                    lhsT=ccodes[q][:, g, cols].bitcast(FP8X4),
                    lhsT_scale=cscale[q][:, g, cols],
                    rhs=pcodes[g][:].bitcast(FP8X4),
                    rhs_scale=pscale[g][:],
                    start=(g == 0),
                    stop=(g == NG - 1),
                )

        def evict_o(name, r, first, count):
            if name is not None:
                res[r] = buf(name, [128, P], F32)
            cols = slice(256 * first, 256 * (first + count))
            nc.vector.tensor_tensor(out=res[r][:, cols], in0=n0_sb[r // 4][:, r % 4, cols], in1=ps_o[r][:, cols], op=ALU.subtract)

        def store(r, first, count):
            cols = slice(256 * first, 256 * (first + count))
            nc.sync.dma_start(out=out[r * 128 : (r + 1) * 128, cols], in_=res[r][:, cols])

        def load_gap():
            nc.scalar.dma_start(out=gap_in[:], in_=gap.rearrange("(j p t) -> p j t", p=128, t=4))

        def load_coul():
            nc.gpsimd.dma_start(out=coul_in[0:4].rearrange("p g (q r) -> p (g q) r", r=8), in_=coul.rearrange("(q t r) -> t q r", t=4, r=8))

        def invert_gap():
            nc.vector.reciprocal(out=ginv[:], in_=gap_in[:])

        def widen_coul():
            nc.scalar.copy(out=coul_rows[0:4], in_=coul_in[0:4])

        def turn_coul(banks):
            tr_coul[0] = bank(banks[0], [128, NG, 128])
            for g in range(NG):
                nc.tensor.transpose(tr_coul[0][:, g, :], coul_rows[:, g, :], ident[:])

        def evict_coul():
            nc.scalar.copy(out=coul_col[:], in_=tr_coul[0][:, :, 0:4])

        queue = {"sync": [], "tensor": [], "scalar": [], "vector": [], "gpsimd": []}
        engine = {"S": "scalar", "V": "vector"}
        ring = {"b": [0, 1, 2, 3], "rest": [4, 5, 6, 7]}
        turn = {}
        holder = {}
        for g in range(NG):
            holder[f"h_in{g}"] = [("sort_h", g)]
            holder[f"h_w{g}"] = [("mul_t", g, 3)]
            holder[f"pot_s{g}"] = [("weave_p", g, 1)]
        holder.update(LEFT_BY)
        holder["x_w"] = [("mul_t", NG - 1, 3)]
        for q in range(NQ):
            holder[f"dcodes{q}"] = [("mul_c", q, NS - 1, 1)]

        def step(where, key, needs, fn, *args):
            queue[where].append((key, needs, fn, args))

        def take(kind, place, last_readers):
            n = turn.get(kind, 0)
            turn[kind] = n + 1
            name = place(n)
            needs = holder.get(name, [])
            holder[name] = last_readers
            return name, needs

        def tensor_step(kind, key, needs, readers, fn, *args):
            banks = []
            for reader in readers:
                n, freed = take(kind, lambda k: ring[kind][k % len(ring[kind])], [reader])
                needs = needs + freed
                banks.append(n)
            step("tensor", key, needs, fn, banks, *args)

        def buffered(where, key, needs, tag, last_readers, fn, *args):
            name = None
            if tag is not None:
                name, freed = take(tag, lambda k: RINGS[tag][k % len(RINGS[tag])], last_readers)
                needs = needs + freed
            step(where, key, needs, fn, name, *args)

        def emit(done):
            at = {where: 0 for where in queue}
            while any(at[where] < len(queue[where]) for where in queue):
                before = len(done)
                for where in queue:
                    while at[where] < len(queue[where]) and all(n in done for n in queue[where][at[where]][1]):
                        key, needs, fn, args = queue[where][at[where]]
                        fn(*args)
                        for name in key if isinstance(key, list) else [key]:
                            done.add(name)
                        at[where] = at[where] + 1
                assert len(done) > before, [queue[w][at[w]][:2] for w in queue if at[w] < len(queue[w])]

        def by_vector(what, n):
            return what == "d" and n >= FIRST_BLOCK

        def turned(what, n):
            if by_vector(what, n):
                return [("turn_blocks", n)]
            return [("turn_b", n, 1)] if what == "b" else [("turn_d", n)]

        def plan_load(what, n):
            readers = [("sort", what, n, 1)] if (what, n) in SORTER else turned(what, n)
            if by_vector(what, n):
                buffered("sync", ("load", what, n), [], "rows", readers, load_blocks, n)
            else:
                buffered("sync", ("load", what, n), [], "rows", readers, load_rows, what, n)

        def plan_load_h(g):
            step("sync", ("load_h", g), [], load_h, g)

        def plan_load_hs():
            step("sync", "load_hs", [], load_scales, hs_in, h_scales.bitcast(I32))

        def plan_sort_h(g, eng):
            step(engine[eng], ("sort_h", g), [("load_h", g)], sort_h, g, eng)

        def plan_sort_hs(g, eng):
            step(engine[eng], ("sort_hs", g), ["load_hs"], sort_hs, g, eng)

        def plan_sort(what, n, pieces=((0, 2),)):
            eng = SORTER[what, n]
            if by_vector(what, n):
                buffered(engine[eng], ("sort", what, n, 1), [("load", what, n)], "sorted" + eng, turned(what, n), sort_blocks, n, eng)
                return
            if eng == "G":
                keys = [("sort", what, n, h) for h in range(2)]
                step("gpsimd", keys, [("load", what, n), ("quant_b", 0, 1)], sort_rows, "wide1", what, n, eng, 0, 2)
                return
            for first, count in pieces:
                keys = [("sort", what, n, h) for h in range(first, first + count)]
                tag = "sorted" + eng if first == 0 else None
                buffered(engine[eng], keys, [("load", what, n)], tag, turned(what, n), sort_rows, what, n, eng, first, count)

        def ready(what, n, h):
            if (what, n) == ("b", 0):
                return [("load_half", h)]
            return [("sort", what, n, h) if (what, n) in SORTER else ("load", what, n)]

        def plan_turn(what, n):
            if what == "b":
                for h in range(2):
                    tensor_step("b", ("turn_b", n, h), ready("b", n, h), [("scale_b", n, h)], turn_b, n, h)
            else:
                tensor_step("rest", ("turn_d", n), ready("d", n, 1), [("d_t", n, 0), ("d_t", n, 1)], turn_d, n)

        def plan_scale_b(i, which=(0, 1)):
            for h in which:
                tag = "wide" if i % 4 == 0 else None
                buffered("vector", ("scale_b", i, h), [("turn_b", i, h), "ginv"], tag, [("quant_b", i // 4, h)], scale_b, i, h)

        def plan_quant_b(g, h):
            step("vector", ("quant_b", g, h), [("scale_b", 4 * g + c, h) for c in range(4)], quant_b, g, h)

        def plan_fill_d(r):
            for h in range(2):
                tag = "d_t" if r % 2 == 0 and h == 0 else None
                buffered("scalar", ("d_t", r, h), [("turn_d", r)], tag, [("quant_d", r // 2)], evict_d, r, h)

        def plan_weave_blocks(r, eng):
            needs = [("turn_blocks", r)] + POT_FIRST.get(r, []) + ([("d_t", r - 1, 0)] if r % 2 else [])
            tag = ("d_t" if eng == "S" else "d_by_V") if r % 2 == 0 else None
            buffered(engine[eng], [("d_t", r, 0), ("d_t", r, 1)], needs, tag, [("quant_d", r // 2)], weave_blocks, r, eng)

        def plan_turn_blocks(r):
            buffered("vector", ("turn_blocks", r), [("sort", "d", r, 1)], "d_flip", [("d_t", r, 0), ("d_t", r, 1)], turn_blocks, r)

        def plan_quant_d(q):
            step("vector", ("quant_d", q), [("d_t", 2 * q + e, h) for e in range(2) for h in range(2)], quant_d, q)

        def plan_trial(g, t):
            tensor_step("rest", ("mul_t", g, t), [("sort_h", g), ("sort_hs", g), "load_x", "load_xs"], [("scale_t", g, t)], mul_t, g, t)

        def plan_scale_t(g, t):
            step("scalar", ("scale_t", g, t), [("mul_t", g, t), "coul_col"], scale_t, g, t)

        def plan_weave_p(g, first, count):
            name, freed_by = POT_PLACE[g, first]
            keys = [("weave_p", g, n) for n in range(first, first + count)]
            step("gpsimd", keys, [("scale_t", g, t) for t in range(4)] + [freed_by], weave_p, name, g, first, count)

        def plan_quant_p(g, first, count):
            step("vector", [("quant_p", g, n) for n in range(first, first + count)], [("weave_p", g, first)], quant_p, g, first, count)

        def plan_response(q, s, first=0, count=2):
            keys = [("mul_c", q, s, e) for e in range(first, first + count)]
            tensor_step("rest", keys, [("quant_b", s // 2, 0), ("quant_b", s // 2, 1), ("quant_d", q)], [("evict_c", q, s, first + count - 1)], mul_c, q, s, first, count)

        def plan_evict_c(q, s, first=0, count=2):
            keys = [("evict_c", q, s, e) for e in range(first, first + count)]
            if q >= FIRST_DIRECT:
                tag = "chi" if s == 0 and first == 0 else None
                buffered("scalar", keys, [("mul_c", q, s, first)], tag, [("quant_c", q, n) for n in range(4)], evict_c, q, s, first, count)
            else:
                buffered("scalar", keys, [("mul_c", q, s, 0)], "chi" if s == 0 else None, [("weave_c", q)], evict_pairs, q, s)

        def plan_weave_c(q, eng):
            buffered(engine[eng], ("weave_c", q), [("evict_c", q, s, 1) for s in range(NS)], "woven", [("quant_c", q, 0)], weave_c, q, eng)

        def plan_quant_c(q, first=0, count=4):
            pieces = range(first, first + count)
            needs = ([("weave_c", q)] if q < FIRST_DIRECT else []) + [("evict_c", q, 2 * (n // 2) + tp, n % 2) for n in pieces for tp in range(2)]
            tag = "ccodes" if first == 0 else None
            buffered("vector", [("quant_c", q, n) for n in pieces], needs, tag, [("mul_o", 2 * q + 1)], quant_c, q, first, count)

        def plan_induced(r):
            needs = [("quant_c", r // 2, r % 2), ("quant_c", r // 2, 2 + r % 2), ("quant_p", 0, 1), ("quant_p", 1, 1)]
            tensor_step("rest", ("mul_o", r), needs, [("evict_o", r, 1)], mul_o, r)

        def plan_evict_o(r, first=0, count=2):
            keys = [("evict_o", r, n) for n in range(first, first + count)]
            buffered("vector", keys, [("mul_o", r), ("load_n0", r // 4)], "res" if first == 0 else None, [("store", r, 1)], evict_o, r, first, count)

        def plan_store(r, first=0, count=2):
            halves_of_row = range(first, first + count)
            step("sync", [("store", r, n) for n in halves_of_row], [("evict_o", r, n) for n in halves_of_row], store, r, first, count)

        last = NQ - 1
        in_halves = ((0, 1), (1, 1))
        def join_banks():
            own = ring["rest"]
            ring["rest"] = ring["b"][:2] + [own[(turn["rest"] + k) % 4] for k in range(4)] + ring["b"][2:]
            turn["rest"] = 0

        def after_head():
            ring["b"], ring["rest"] = [4, 5, 6, 7], [1, 2, 3, 0]
            turn["b"], turn["rest"] = 0, 0

        step("sync", "gap", [], load_gap)
        buffered("sync", ("load_half", 0), [], "first", [("turn_b", 0, 0)], load_half, 0)
        buffered("sync", ("load_half", 1), [], "first", [("turn_b", 0, 1)], load_half, 1)
        plan_load("b", 1)
        plan_load_hs()
        plan_load_h(0)
        step("sync", "load_x", [], load_x)
        plan_load("b", 2)
        step("sync", "load_xs", [], load_scales, x_s[:].bitcast(I32), x_scales.bitcast(I32))
        plan_load("b", 3)
        plan_load_h(1)
        plan_load("b", 4)
        plan_load("d", 0)
        plan_load("b", 5)
        plan_load("d", 1)
        plan_load("b", 6)
        plan_load("d", 2)
        plan_load("d", 3)
        plan_load("b", 7)
        plan_load("d", 4)
        plan_load("d", 5)
        plan_load("d", 6)
        plan_load("d", 7)
        plan_load("d", 8)
        plan_load("d", 9)
        plan_load("d", 10)
        plan_load("d", 11)
        buffered("sync", ("load_n0", 0), [], "rows", [("evict_o", 3, 1)], load_n0, 0)
        buffered("sync", ("load_n0", 1), [], "rows", [("evict_o", 7, 1)], load_n0, 1)
        buffered("sync", ("load_n0", 2), [], "rows", [("evict_o", 11, 1)], load_n0, 2)
        plan_store(0)
        plan_store(1)
        plan_store(2)
        plan_store(3)
        plan_store(4)
        plan_store(5)
        plan_store(6)
        plan_store(7)
        plan_store(8)
        plan_store(9)
        plan_store(10)
        plan_store(11, 0, 1)
        plan_store(11, 1, 1)

        plan_turn("b", 0)
        plan_turn("b", 1)
        tensor_step("rest", "turn_coul", ["coul_rows"], ["coul_col"], turn_coul)
        tensor_step("rest", "warm_up", [("sort_h", 0), ("sort_hs", 0)], ["warm_up"], warm_up)
        plan_turn("b", 2)
        plan_trial(0, 0)
        plan_trial(0, 1)
        plan_turn("b", 3)
        plan_trial(0, 2)
        plan_trial(0, 3)
        plan_turn("b", 4)
        plan_trial(1, 0)
        plan_trial(1, 1)
        plan_turn("d", 0)
        plan_turn("b", 5)
        plan_turn("d", 1)
        plan_trial(1, 2)
        plan_trial(1, 3)
        plan_turn("b", 6)
        plan_turn("d", 2)
        plan_turn("d", 3)
        plan_turn("b", 7)
        plan_response(0, 0)
        plan_response(0, 1)
        plan_turn("d", 4)
        plan_response(1, 0)
        join_banks()
        plan_response(1, 1)
        plan_response(0, 2)
        plan_response(0, 3)
        plan_response(1, 2)
        plan_response(1, 3)
        plan_response(2, 0)
        plan_response(2, 1)
        plan_response(2, 2)
        plan_response(2, 3)
        plan_response(3, 0)
        plan_response(3, 1)
        plan_response(3, 2)
        plan_response(3, 3)
        plan_response(4, 0)
        plan_response(4, 1)
        plan_response(4, 2)
        plan_response(4, 3)
        plan_induced(0)
        plan_induced(1)
        plan_response(5, 0)
        plan_induced(2)
        plan_induced(3)
        plan_response(5, 1)
        plan_induced(4)
        plan_induced(5)
        plan_response(5, 2)
        plan_induced(6)
        plan_induced(7)
        plan_response(5, 3, 0, 1)
        plan_response(5, 3, 1, 1)
        plan_induced(8)
        plan_induced(9)
        plan_induced(10)
        plan_induced(11)

        step("vector", "ginv", ["gap"], invert_gap)
        plan_scale_b(0)
        plan_sort_hs(0, "V")
        plan_sort_hs(1, "V")
        plan_sort_h(0, "V")
        plan_scale_b(1)
        plan_scale_b(2)
        plan_sort_h(1, "V")
        plan_scale_b(3)
        plan_quant_b(0, 0)
        plan_quant_b(0, 1)
        plan_scale_b(4)
        plan_scale_b(5)
        plan_quant_d(0)
        plan_scale_b(6)
        plan_scale_b(7, (0,))
        plan_quant_d(1)
        plan_scale_b(7, (1,))
        plan_quant_b(1, 0)
        plan_quant_b(1, 1)
        plan_turn_blocks(5)
        plan_turn_blocks(6)
        plan_weave_blocks(5, "V")
        plan_quant_p(0, 0, 2)
        plan_quant_d(2)
        plan_turn_blocks(7)
        plan_turn_blocks(8)
        plan_weave_blocks(7, "V")
        plan_quant_p(1, 0, 1)
        plan_quant_d(3)
        plan_turn_blocks(9)
        plan_quant_p(1, 1, 1)
        plan_weave_blocks(9, "V")
        plan_weave_c(0, "V")
        plan_quant_d(4)
        plan_turn_blocks(10)
        plan_weave_c(1, "V")
        plan_quant_c(0)
        plan_turn_blocks(11)
        plan_quant_c(1)
        plan_weave_blocks(11, "V")
        plan_weave_c(2, "V")
        plan_quant_d(5)
        plan_evict_o(0)
        plan_quant_c(2)
        plan_evict_o(1)
        plan_evict_o(2)
        plan_quant_c(3)
        plan_evict_o(3)
        plan_evict_o(4)
        plan_quant_c(4)
        plan_evict_o(5)
        plan_quant_c(5, 0, 2)
        plan_evict_o(6)
        plan_evict_o(7)
        plan_quant_c(5, 2, 1)
        plan_evict_o(8)
        plan_quant_c(5, 3, 1)
        plan_evict_o(9)
        plan_evict_o(10)
        plan_evict_o(11, 0, 1)
        plan_evict_o(11, 1, 1)

        plan_sort("b", 1, in_halves)
        step("scalar", "coul_rows", ["coul"], widen_coul)
        step("scalar", "coul_col", ["turn_coul"], evict_coul)
        plan_sort("b", 3, in_halves)
        plan_scale_t(0, 0)
        plan_scale_t(0, 1)
        plan_sort("b", 4)
        plan_scale_t(0, 2)
        plan_sort("d", 0)
        plan_scale_t(0, 3)
        plan_scale_t(1, 0)
        plan_sort("d", 1)
        plan_scale_t(1, 1)
        plan_fill_d(0)
        plan_fill_d(1)
        plan_sort("d", 2)
        plan_scale_t(1, 2)
        plan_scale_t(1, 3)
        plan_fill_d(2)
        plan_fill_d(3)
        plan_sort("d", 4)
        plan_evict_c(0, 0)
        plan_sort("d", 5)
        plan_evict_c(0, 1)
        plan_fill_d(4)
        plan_sort("d", 6)
        plan_evict_c(1, 0)
        plan_sort("d", 7)
        plan_evict_c(1, 1)
        plan_weave_blocks(6, "S")
        plan_sort("d", 8)
        plan_evict_c(0, 2)
        plan_evict_c(0, 3)
        plan_sort("d", 9)
        plan_weave_blocks(8, "S")
        plan_evict_c(1, 2)
        plan_evict_c(1, 3)
        plan_sort("d", 10)
        plan_evict_c(2, 0)
        plan_evict_c(2, 1)
        plan_sort("d", 11)
        plan_evict_c(2, 2)
        plan_weave_blocks(10, "S")
        plan_evict_c(2, 3)
        plan_evict_c(3, 0)
        plan_evict_c(3, 1)
        plan_evict_c(3, 2)
        plan_evict_c(3, 3)
        plan_evict_c(4, 0)
        plan_evict_c(4, 1)
        plan_evict_c(4, 2)
        plan_evict_c(4, 3)
        plan_weave_c(3, "S")
        plan_evict_c(5, 0)
        plan_weave_c(4, "S")
        plan_evict_c(5, 1)
        plan_evict_c(5, 2)
        plan_evict_c(5, 3, 0, 1)
        plan_evict_c(5, 3, 1, 1)

        plan_sort("b", 6)
        plan_weave_p(0, 0, 2)
        plan_weave_p(1, 0, 1)
        plan_weave_p(1, 1, 1)

        with tc.manual_schedule():
            nc.vector.memset(hs_in[:], 0)
            nc.vector.memset(x_s[:].rearrange("p j n -> p (j n)").bitcast(I32), 0)
            nc.vector.memset(coul_rows[:], 0.0)
            make_identity(nc, ident[:])
            load_coul()
            emit({"coul"})
